import numpy as np
import ml_dtypes


def mxq(x, axis, fmt="e4m3"):
    dtype, down = {"e4m3": (ml_dtypes.float8_e4m3fn, 7), "e5m2": (ml_dtypes.float8_e5m2, 14)}[fmt]
    v = np.moveaxis(np.asarray(x, np.float32).astype(ml_dtypes.bfloat16).astype(np.float64), axis, -1)
    blocks = v.reshape(v.shape[:-1] + (-1, 32))
    amax = np.abs(blocks).max(-1, keepdims=True)
    byte = np.maximum(np.where(amax > 0, np.frexp(amax)[1] - 1 + 127, 0) - down, 1)
    scale = np.exp2(byte - 127.0)
    codes = (blocks / scale).astype(np.float32).astype(dtype).astype(np.float64)
    return np.moveaxis((codes * scale).reshape(v.shape), -1, axis)


WIDE = False


def mx_kscale(k):
    if not WIDE:
        return np.ones(k)
    levels = np.array([10, -10, 5, -5, 0])
    if k % 512:
        return np.exp2(np.random.permutation(np.resize(levels, k // 32))).repeat(32)
    a = np.empty((k // 512, 16))
    for p in range(k // 512):
        a[p, :8] = np.random.permutation(np.resize(levels, 8))
        for g in range(8):
            far = levels[np.abs(levels - a[p, g]) >= 10]
            a[p, g + 8] = far[np.random.randint(len(far))]
    return np.exp2(a.ravel()).repeat(32)


def f64(x):
    return np.asarray(x).astype(np.float64)


def striped(idx):
    return np.tile(idx.reshape(-1, 16).T, (8, 1)).astype(np.uint16)


def unstriped(offs):
    return offs[:16].T.reshape(-1).astype(np.int64)


E2M1 = np.array([0.0, 0.5, 1.0, 1.5, 2.0, 3.0, 4.0, 6.0, -0.0, -0.5, -1.0, -1.5, -2.0, -3.0, -4.0, -6.0])


def pack_weight(w, fmt):
    k, n = w.shape
    w = f64(np.asarray(w, np.float32).astype(ml_dtypes.bfloat16)).reshape(k // 32, 32, n)
    amax = np.abs(w).max(1)
    if fmt == "e4m3":
        byte = np.frexp(amax)[1] - 1 + 127 - 7
    else:
        mant, ex = np.frexp(amax / 6.0)
        byte = np.where(mant > 0.5, ex, ex - 1) + 127
    byte = np.clip(np.where(amax > 0, byte, 1), 1, 254)
    scaled = (w * np.exp2(127.0 - byte)[:, None, :]).reshape(k, n).astype(np.float32)
    by_word = np.ascontiguousarray(scaled.reshape(k // 512, 128, 4, n).transpose(0, 1, 3, 2))
    if fmt == "e4m3":
        words = by_word.astype(ml_dtypes.float8_e4m3fn).view(np.uint8)
    else:
        c = by_word.astype(ml_dtypes.float4_e2m1fn).view(np.uint8) & 0xF
        words = (c[..., 0::2] | (c[..., 1::2] << 4)).reshape(k // 512, 128, 2 * n)
    return np.ascontiguousarray(words), np.ascontiguousarray(byte.astype(np.uint8).reshape(k // 512, 16, n))


def unpack_weight(words, scales, fmt):
    g, _, n = scales.shape
    words = np.ascontiguousarray(words).reshape(g, 128, n, -1)
    if fmt == "e4m3":
        vals = words.view(ml_dtypes.float8_e4m3fn).astype(np.float64)
    else:
        nib = np.empty((g, 128, n, 4), np.uint8)
        nib[..., 0::2] = words & 0xF
        nib[..., 1::2] = words >> 4
        vals = E2M1[nib]
    vals = vals * np.repeat(np.exp2(scales.astype(np.float64) - 127.0), 8, axis=1)[..., None]
    return vals.transpose(0, 1, 3, 2).reshape(g * 512, n)


def gelu(v):
    return 0.5 * v * (1.0 + np.tanh(np.sqrt(2.0 / np.pi) * (v + 0.044715 * v**3)))


K, T, S, P, H = 1536, 2048, 1024, 512, 1024

def setup_inputs():
    n = np.random.standard_normal
    s = mx_kscale(K)[:, None]
    u = mx_kscale(H)[:, None]
    tab_words, tab_scales = pack_weight(n((K, T)) * s, "e4m3")
    wa_words, wa_scales = pack_weight(2.0 * n((H, H)) / np.sqrt(H) / u, "e2m1")
    return {
        "tab_words": tab_words, "tab_scales": tab_scales,
        "offs": striped(np.random.permutation(T)[:S]),
        "pos1": striped(np.random.permutation(S)[:P]),
        "pos2": striped(np.random.permutation(S)[:P]),
        "w1": (1.5 * n((K, H)) / np.sqrt(K) / s).astype(np.float32),
        "gain": (np.exp(0.3 * n(H)) * u[:, 0]).astype(np.float32),
        "wa_words": wa_words, "wa_scales": wa_scales,
        "wb": (2.0 * n((H, H)) / np.sqrt(H) / u).astype(np.float32),
        "bg": n(H).astype(np.float32),
    }

def reference(tab_words, tab_scales, offs, pos1, pos2, w1, gain, wa_words, wa_scales, wb, bg):
    v = unpack_weight(tab_words, tab_scales, "e4m3")[:, unstriped(offs)]
    h = mxq(f64(w1), 0, "e4m3").T @ v
    d = h[:, unstriped(pos1)]
    x = d / (1.0 + np.exp(-d)) * f64(gain)[:, None]
    xq = mxq(x, 0, "e4m3")
    wa = unpack_weight(wa_words, wa_scales, "e2m1")
    val = wa.T @ xq
    gate = mxq(f64(wb), 0, "e4m3").T @ xq
    y = val / (1.0 + np.exp(-(gate + f64(bg)[:, None])))
    return y + h[:, unstriped(pos2)]

@@ -1,0 +1,276 @@
+from contextlib import ExitStack
+
+import concourse.mybir as mybir
+
+K, T, S, M, H = 1536, 2048, 1024, 512, 1024
+FLOPS = 2 * K * H * S + 2 * 2 * H * H * M
+
+F32 = mybir.dt.float32
+BF16 = mybir.dt.bfloat16
+I32 = mybir.dt.int32
+U32 = mybir.dt.uint32
+U16 = mybir.dt.uint16
+U8 = mybir.dt.uint8
+FP8X4 = mybir.dt.float8_e4m3fn_x4
+FP4X4 = mybir.dt.float4_e2m1fn_x4
+ACT = mybir.ActivationFunctionType
+ALU = mybir.AluOpType
+
+P = 128
+PACK = 4
+KP = P * PACK
+BANK = 512
+K_PASSES = K // KP
+H_PASSES = H // KP
+
+
+def tile_list_reef_mosaic_skip_kernel(
+    tc, tab_words, tab_scales, offs, pos1, pos2, w1, gain, wa_words, wa_scales, wb, bg, out
+):
+    nc = tc.nc
+    with ExitStack() as ctx:
+        keep = ctx.enter_context(tc.tile_pool(name="keep", bufs=1))
+        ring = ctx.enter_context(tc.tile_pool(name="ring", bufs=1))
+        psum = ctx.enter_context(tc.psum_pool(name="psum", bufs=8))
+
+        offs_sb = keep.tile([P, S // 16], U16, name="offs_sb")
+        pos1_sb = keep.tile([P, M // 16], U16, name="pos1_sb")
+        pos2_sb = keep.tile([P, M // 16], U16, name="pos2_sb")
+        tab_scale_sb = keep.tile([P, T], U8, name="tab_scale_sb", align_bytes=64)
+        wa_scale_raw = keep.tile([P, H_PASSES * H], U8, name="wa_scale_raw", align_bytes=64)
+        vec_raw = keep.tile([P, 2, H_PASSES, 2 * PACK], F32, name="vec_raw")
+        vec_half = keep.tile([P, 2, H_PASSES, PACK], F32, name="vec_half")
+
+        nc.gpsimd.memset(tab_scale_sb[:].bitcast(I32), 0)
+        nc.gpsimd.memset(wa_scale_raw[:].bitcast(I32), 0)
+        for q in range(4):
+            nc.scalar.dma_start(
+                out=tab_scale_sb[32 * q : 32 * q + 4 * K_PASSES, :].bitcast(I32),
+                in_=tab_scales[:, 4 * q : 4 * q + 4, :].bitcast(I32),
+            )
+        for i, vec in enumerate((gain, bg)):
+            nc.scalar.dma_start(out=vec_raw[:, i, :, 0:PACK], in_=vec.rearrange("(b p t) -> p b t", b=H_PASSES, t=PACK))
+        for q in range(4):
+            nc.gpsimd.dma_start(
+                out=wa_scale_raw[32 * q : 32 * q + 4, :].bitcast(I32).rearrange("r (a c) -> r a c", a=H_PASSES),
+                in_=wa_scales[:, 4 * q : 4 * q + 4, :].bitcast(I32).rearrange("a r c -> r a c"),
+            )
+        nc.scalar.activation(out=vec_half[:], in_=vec_raw[:, :, :, 0:PACK], func=ACT.Copy, scale=0.5)
+        half_gain = vec_half[:, 0]
+        half_bg = vec_half[:, 1]
+
+        def slot(tag, shape, dtype):
+            return ring.tile(shape, dtype, name=tag, tag=tag, align_bytes=64)
+
+        def load_table(a):
+            words = keep.tile([P, T], I32, name="tab_%d" % a, align_bytes=64)
+            nc.sync.dma_start(out=words[:], in_=tab_words[a].rearrange("p t i -> p (t i)").bitcast(I32))
+            return words
+
+        def load_weight(w, a, b, tag):
+            raw = slot(tag, [P, PACK, KP], F32)
+            nc.sync.dma_start(
+                out=raw[:],
+                in_=w[KP * a : KP * (a + 1), KP * b : KP * (b + 1)].rearrange("(p j) c -> p j c", j=PACK),
+            )
+            return raw
+
+        def round_weight(raw, how):
+            rounded = ring.tile([P, KP * PACK], BF16, name="w_bf16", bufs=3, align_bytes=64)
+            dst = rounded[:].rearrange("p (u v m j) -> p u m j v", u=2, v=2, j=PACK)
+            src = raw[:].rearrange("p j (m u v) -> p u m j v", u=2, v=2)
+            if how == "S":
+                nc.scalar.copy(out=dst, in_=src)
+            elif how == "V":
+                nc.vector.tensor_copy(out=dst, in_=src)
+            elif how == "G":
+                for u in range(2):
+                    nc.gpsimd.tensor_copy(out=dst[:, u], in_=src[:, u])
+            else:
+                nc.vector.tensor_copy(out=dst[:, 1], in_=src[:, 1])
+                nc.scalar.copy(out=dst[:, 0], in_=src[:, 0])
+            return rounded
+
+        def quantise(rounded, name):
+            codes = keep.tile([P, KP], U32, name=name + "_codes", align_bytes=64)
+            scales = keep.tile([P, KP], U8, name=name + "_scales", align_bytes=64)
+            nc.vector.quantize_mx(out=codes[:].bitcast(FP8X4), scales=scales[:], in_=rounded[:])
+            return codes, scales
+
+        def gather_words(words, a):
+            halves = []
+            for half in range(2):
+                picked = keep.tile([P, BANK], U32, name="v_%d_%d" % (a, half), align_bytes=64)
+                nc.vector.tensor_copy(
+                    out=picked[:], in_=words[:].bitcast(U32).indirect(offs_sb[:, 32 * half : 32 * (half + 1)])
+                )
+                halves.append(picked)
+            return halves
+
+        how_w1 = {(0, 0): "S", (1, 0): "X", (2, 0): "X", (0, 1): "S", (1, 1): "S", (2, 1): "S"}
+        how_wb = {(0, 0): "S", (1, 0): "S", (0, 1): "S", (1, 1): "S"}
+
+        nc.sync.dma_start(offs_sb[:], offs)
+        tab = {}
+        w1_raw = {}
+        tab[0] = load_table(0)
+        tab[1] = load_table(1)
+        w1_raw[0, 0] = load_weight(w1, 0, 0, "raw0")
+        w1_raw[1, 0] = load_weight(w1, 1, 0, "raw1")
+        tab[2] = load_table(2)
+        w1_raw[2, 0] = load_weight(w1, 2, 0, "raw2")
+        nc.sync.dma_start(pos1_sb[:], pos1)
+        nc.sync.dma_start(pos2_sb[:], pos2)
+        for a in range(K_PASSES):
+            w1_raw[a, 1] = load_weight(w1, a, 1, "raw%d" % (3 + a))
+        wa_raw = keep.tile([P, H_PASSES, H // 2], I32, name="wa_raw", align_bytes=64)
+        nc.sync.dma_start(out=wa_raw[:], in_=wa_words.bitcast(I32).rearrange("a p c -> p a c"))
+
+        v = {}
+        w1_q = {}
+        v[0] = gather_words(tab[0], 0)
+        v_scale = keep.tile([P, S], U8, name="v_scale", align_bytes=64)
+        nc.vector.tensor_copy(out=v_scale[:], in_=tab_scale_sb[:].indirect(offs_sb[:]))
+        v[1] = gather_words(tab[1], 1)
+        w1_q[0, 0] = quantise(round_weight(w1_raw[0, 0], how_w1[0, 0]), "w1_0_0")
+        w1_q[1, 0] = quantise(round_weight(w1_raw[1, 0], how_w1[1, 0]), "w1_1_0")
+        v[2] = gather_words(tab[2], 2)
+        w1_q[2, 0] = quantise(round_weight(w1_raw[2, 0], how_w1[2, 0]), "w1_2_0")
+
+        wb_raw = {}
+        wb_raw[0, 0] = load_weight(wb, 0, 0, "raw0")
+        wb_raw[1, 0] = load_weight(wb, 1, 0, "raw1")
+        wb_raw[0, 1] = load_weight(wb, 0, 1, "raw6")
+
+        def first_product(b):
+            acc = {}
+            for t in range(PACK):
+                for half in range(2):
+                    acc[t, half] = psum.tile([P, BANK], F32, name="acc")
+            for a in range(K_PASSES):
+                codes, scales = w1_q[a, b]
+                for t in range(PACK):
+                    cols = slice(P * t, P * (t + 1))
+                    for half in range(2):
+                        nc.tensor.matmul_mx(
+                            out=acc[t, half][:],
+                            lhsT=codes[:, cols].bitcast(FP8X4),
+                            lhsT_scale=scales[:, cols],
+                            rhs=v[a][half][:].bitcast(FP8X4),
+                            rhs_scale=v_scale[4 * a : P, BANK * half : BANK * (half + 1)],
+                            start=(a == 0),
+                            stop=(a == K_PASSES - 1),
+                        )
+            return acc
+
+        h = {}
+        skip = {}
+        x_q = {}
+        wb_q = {}
+
+        def leave_psum(b, acc):
+            for t in range(PACK):
+                h[b, t] = keep.tile([P, S], F32, name="h_%d_%d" % (b, t), align_bytes=64)
+                for half in range(2):
+                    nc.scalar.copy(out=h[b, t][:, BANK * half : BANK * (half + 1)], in_=acc[t, half][:])
+
+        def activation_operand(b, engine):
+            silu = slot("silu%d" % b, [P, PACK, M], F32)
+            for t in range(PACK):
+                deep = ring.tile([P, M], F32, name="deep", bufs=4)
+                nc.vector.tensor_copy(out=deep[:], in_=h[b, t][:].indirect(pos1_sb[:]))
+                nc.scalar.activation(out=silu[:, t, :], in_=deep[:], func=ACT.Silu)
+            x = ring.tile([P, M * PACK], BF16, name="x_bf16", bufs=2, align_bytes=64)
+            engine.tensor_tensor(
+                out=x[:].rearrange("p (c i t) -> p c t i", i=2, t=PACK),
+                in0=silu[:].rearrange("p t (c i) -> p c t i", i=2),
+                in1=half_gain[:, b, :].unsqueeze(1).unsqueeze(3).to_broadcast([P, M // 2, PACK, 2]),
+                op=ALU.mult,
+            )
+            x_q[b] = quantise(x, "x_%d" % b)
+
+        def quantise_wb(a, b):
+            wb_q[a, b] = quantise(round_weight(wb_raw[a, b], how_wb[a, b]), "wb_%d_%d" % (a, b))
+
+        def gather_skip(b, t):
+            nc.vector.tensor_copy(out=skip[b][:, t, :], in_=h[b, t][:].indirect(pos2_sb[:]))
+
+        acc0 = first_product(0)
+        leave_psum(0, acc0)
+        for a in range(K_PASSES):
+            w1_q[a, 1] = quantise(round_weight(w1_raw[a, 1], how_w1[a, 1]), "w1_%d_1" % a)
+        wb_raw[1, 1] = load_weight(wb, 1, 1, "raw4")
+        acc1 = first_product(1)
+        activation_operand(0, nc.vector)
+        quantise_wb(0, 0)
+        leave_psum(1, acc1)
+        activation_operand(1, nc.vector)
+
+        wa = keep.tile([P, H_PASSES * H], U16, name="wa", align_bytes=64)
+        nc.vector.tensor_copy(
+            out=wa[:].rearrange("p (g t m) -> p g t m", t=PACK, m=P),
+            in_=wa_raw[:].rearrange("p a c -> p (a c)").bitcast(U16).rearrange("p (g m t) -> p g t m", t=PACK, m=P),
+        )
+        wa_scale = slot("raw2", [P, H_PASSES * H], U8)
+        nc.vector.tensor_copy(
+            out=wa_scale[:].rearrange("p (g t m) -> p g t m", t=PACK, m=P),
+            in_=wa_scale_raw[:].rearrange("p (g m t) -> p g t m", t=PACK, m=P),
+        )
+        quantise_wb(1, 0)
+        skip[0] = slot("raw3", [P, PACK, M], F32)
+        skip[1] = slot("silu1", [P, PACK, M], F32)
+        unfused = [(b, t) for b in range(2) for t in range(4)]
+        for t in range(PACK):
+            if (0, t) in unfused:
+                gather_skip(0, t)
+
+        out_rows = out.rearrange("(b p t) m -> b t p m", b=H_PASSES, t=PACK)
+        for b in range(H_PASSES):
+            if b == 1:
+                quantise_wb(0, 1)
+                quantise_wb(1, 1)
+            gate = {}
+            val = {}
+            for t in range(PACK):
+                gate[t] = psum.tile([P, BANK], F32, name="acc")
+                val[t] = psum.tile([P, BANK], F32, name="acc")
+            for a in range(H_PASSES):
+                x_codes, x_scales = x_q[a]
+                wb_codes, wb_scales = wb_q[a, b]
+                for t in range(PACK):
+                    cols = slice(P * t, P * (t + 1))
+                    nc.tensor.matmul_mx(
+                        out=gate[t][:],
+                        lhsT=wb_codes[:, cols].bitcast(FP8X4),
+                        lhsT_scale=wb_scales[:, cols],
+                        rhs=x_codes[:].bitcast(FP8X4),
+                        rhs_scale=x_scales[:],
+                        start=(a == 0),
+                        stop=(a == H_PASSES - 1),
+                    )
+                    wa_cols = slice(H * a + KP * b + P * t, H * a + KP * b + P * (t + 1))
+                    nc.tensor.matmul_mx(
+                        out=val[t][:],
+                        lhsT=wa[:, wa_cols].bitcast(FP4X4),
+                        lhsT_scale=wa_scale[:, wa_cols],
+                        rhs=x_codes[:].bitcast(FP8X4),
+                        rhs_scale=x_scales[:],
+                        start=(a == 0),
+                        stop=(a == H_PASSES - 1),
+                    )
+            for t in range(PACK):
+                tanh = ring.tile([P, M], F32, name="tanh", bufs=3)
+                nc.scalar.activation(out=tanh[:], in_=gate[t][:], func=ACT.Tanh, bias=half_bg[:, b, t : t + 1])
+                gated = ring.tile([P, M], F32, name="gated", bufs=3)
+                nc.vector.scalar_tensor_tensor(
+                    out=gated[:], in0=tanh[:], scalar=1.0, in1=val[t][:], op0=ALU.add, op1=ALU.mult
+                )
+                if (b, t) in unfused:
+                    if b == 1:
+                        gather_skip(b, t)
+                    nc.vector.tensor_tensor(out=skip[b][:, t, :], in0=skip[b][:, t, :], in1=gated[:], op=ALU.add)
+                else:
+                    nc.vector.tensor_tensor(
+                        out=skip[b][:, t, :], in0=h[b, t][:].indirect(pos2_sb[:]), in1=gated[:], op=ALU.add
+                    )
+                nc.sync.dma_start(out=out_rows[b, t], in_=skip[b][:, t, :])

@@ -51,7 +51,7 @@ def tile_list_reef_mosaic_skip_kernel(
         for i, vec in enumerate((gain, bg)):
             nc.scalar.dma_start(out=vec_raw[:, i, :, 0:PACK], in_=vec.rearrange("(b p t) -> p b t", b=H_PASSES, t=PACK))
         for q in range(4):
-            nc.gpsimd.dma_start(
+            nc.scalar.dma_start(
                 out=wa_scale_raw[32 * q : 32 * q + 4, :].bitcast(I32).rearrange("r (a c) -> r a c", a=H_PASSES),
                 in_=wa_scales[:, 4 * q : 4 * q + 4, :].bitcast(I32).rearrange("a r c -> r a c"),
             )
@@ -107,7 +107,7 @@ def tile_list_reef_mosaic_skip_kernel(
                 halves.append(picked)
             return halves
 
-        how_w1 = {(0, 0): "S", (1, 0): "X", (2, 0): "X", (0, 1): "S", (1, 1): "S", (2, 1): "S"}
+        how_w1 = {(0, 0): "S", (1, 0): "X", (2, 0): "X", (0, 1): "V", (1, 1): "X", (2, 1): "X"}
         how_wb = {(0, 0): "S", (1, 0): "S", (0, 1): "S", (1, 1): "S"}
 
         nc.sync.dma_start(offs_sb[:], offs)
@@ -119,12 +119,12 @@ def tile_list_reef_mosaic_skip_kernel(
         w1_raw[1, 0] = load_weight(w1, 1, 0, "raw1")
         tab[2] = load_table(2)
         w1_raw[2, 0] = load_weight(w1, 2, 0, "raw2")
+        wa_raw = keep.tile([P, H_PASSES, H // 2], I32, name="wa_raw", align_bytes=64)
+        nc.sync.dma_start(out=wa_raw[:], in_=wa_words.bitcast(I32).rearrange("a p c -> p a c"))
         nc.sync.dma_start(pos1_sb[:], pos1)
         nc.sync.dma_start(pos2_sb[:], pos2)
         for a in range(K_PASSES):
             w1_raw[a, 1] = load_weight(w1, a, 1, "raw%d" % (3 + a))
-        wa_raw = keep.tile([P, H_PASSES, H // 2], I32, name="wa_raw", align_bytes=64)
-        nc.sync.dma_start(out=wa_raw[:], in_=wa_words.bitcast(I32).rearrange("a p c -> p a c"))
 
         v = {}
         w1_q = {}
@@ -136,6 +136,17 @@ def tile_list_reef_mosaic_skip_kernel(
         w1_q[1, 0] = quantise(round_weight(w1_raw[1, 0], how_w1[1, 0]), "w1_1_0")
         v[2] = gather_words(tab[2], 2)
         w1_q[2, 0] = quantise(round_weight(w1_raw[2, 0], how_w1[2, 0]), "w1_2_0")
+
+        wa = slot("raw2", [P, H_PASSES * H], U16)
+        nc.vector.tensor_copy(
+            out=wa[:].rearrange("p (g t m) -> p g t m", t=PACK, m=P),
+            in_=wa_raw[:].rearrange("p a c -> p (a c)").bitcast(U16).rearrange("p (g m t) -> p g t m", t=PACK, m=P),
+        )
+        wa_scale = keep.tile([P, H_PASSES * H], U8, name="wa_scale", align_bytes=64)
+        nc.vector.tensor_copy(
+            out=wa_scale[:].rearrange("p (g t m) -> p g t m", t=PACK, m=P),
+            in_=wa_scale_raw[:].rearrange("p (g m t) -> p g t m", t=PACK, m=P),
+        )
 
         wb_raw = {}
         wb_raw[0, 0] = load_weight(wb, 0, 0, "raw0")
@@ -177,7 +188,7 @@ def tile_list_reef_mosaic_skip_kernel(
         def activation_operand(b, engine):
             silu = slot("silu%d" % b, [P, PACK, M], F32)
             for t in range(PACK):
-                deep = ring.tile([P, M], F32, name="deep", bufs=4)
+                deep = slot("deep%d" % t, [P, M], F32)
                 nc.vector.tensor_copy(out=deep[:], in_=h[b, t][:].indirect(pos1_sb[:]))
                 nc.scalar.activation(out=silu[:, t, :], in_=deep[:], func=ACT.Silu)
             x = ring.tile([P, M * PACK], BF16, name="x_bf16", bufs=2, align_bytes=64)
@@ -189,36 +200,52 @@ def tile_list_reef_mosaic_skip_kernel(
             )
             x_q[b] = quantise(x, "x_%d" % b)
 
+        def activation_operand_pool(b):
+            deep = slot("deep4", [P, PACK, M], F32)
+            for t in range(PACK):
+                nc.vector.tensor_copy(out=deep[:, t, :], in_=h[b, t][:].indirect(pos1_sb[:]))
+            silu = slot("silu%d" % b, [P, M * PACK], F32)
+            nc.scalar.activation(
+                out=silu[:].rearrange("p (c i t) -> p c t i", i=2, t=PACK),
+                in_=deep[:].rearrange("p t (c i) -> p c t i", i=2),
+                func=ACT.Silu,
+            )
+            x = ring.tile([P, M * PACK], BF16, name="x_bf16", bufs=2, align_bytes=64)
+            for piece in range(4):
+                cols = slice(M * piece, M * (piece + 1))
+                nc.gpsimd.tensor_tensor(
+                    out=x[:, cols].rearrange("p (m t) -> p m t", t=PACK),
+                    in0=silu[:, cols].rearrange("p (m t) -> p m t", t=PACK),
+                    in1=half_gain[:, b, :].unsqueeze(1).to_broadcast([P, M // PACK, PACK]),
+                    op=ALU.mult,
+                )
+            x_q[b] = quantise(x, "x_%d" % b)
+
         def quantise_wb(a, b):
             wb_q[a, b] = quantise(round_weight(wb_raw[a, b], how_wb[a, b]), "wb_%d_%d" % (a, b))
 
         def gather_skip(b, t):
-            nc.vector.tensor_copy(out=skip[b][:, t, :], in_=h[b, t][:].indirect(pos2_sb[:]))
+            nc.vector.tensor_copy(out=skip[b, t], in_=h[b, t][:].indirect(pos2_sb[:]))
 
         acc0 = first_product(0)
         leave_psum(0, acc0)
         for a in range(K_PASSES):
             w1_q[a, 1] = quantise(round_weight(w1_raw[a, 1], how_w1[a, 1]), "w1_%d_1" % a)
-        wb_raw[1, 1] = load_weight(wb, 1, 1, "raw4")
+        wb_raw[1, 1] = load_weight(wb, 1, 1, "raw3")
         acc1 = first_product(1)
-        activation_operand(0, nc.vector)
+        activation_operand_pool(0)
         quantise_wb(0, 0)
+        quantise_wb(1, 0)
         leave_psum(1, acc1)
         activation_operand(1, nc.vector)
 
-        wa = keep.tile([P, H_PASSES * H], U16, name="wa", align_bytes=64)
-        nc.vector.tensor_copy(
-            out=wa[:].rearrange("p (g t m) -> p g t m", t=PACK, m=P),
-            in_=wa_raw[:].rearrange("p a c -> p (a c)").bitcast(U16).rearrange("p (g m t) -> p g t m", t=PACK, m=P),
-        )
-        wa_scale = slot("raw2", [P, H_PASSES * H], U8)
-        nc.vector.tensor_copy(
-            out=wa_scale[:].rearrange("p (g t m) -> p g t m", t=PACK, m=P),
-            in_=wa_scale_raw[:].rearrange("p (g m t) -> p g t m", t=PACK, m=P),
-        )
-        quantise_wb(1, 0)
-        skip[0] = slot("raw3", [P, PACK, M], F32)
-        skip[1] = slot("silu1", [P, PACK, M], F32)
+        skip_first = slot("raw4", [P, PACK, M], F32)
+        skip_late = slot("silu1", [P, 3, M], F32)
+        for t in range(PACK):
+            skip[0, t] = skip_first[:, t, :]
+        skip[1, 0] = slot("deep2", [P, M], F32)[:]
+        skip[1, 1] = skip_late[:, 0, :]
+        skip[1, 2] = skip_late[:, 1, :]
         unfused = [(b, t) for b in range(2) for t in range(4)]
         for t in range(PACK):
             if (0, t) in unfused:
@@ -259,18 +286,24 @@ def tile_list_reef_mosaic_skip_kernel(
                         stop=(a == H_PASSES - 1),
                     )
             for t in range(PACK):
-                tanh = ring.tile([P, M], F32, name="tanh", bufs=3)
+                if (b, t) == (0, 0):
+                    tanh = slot("tanh_first", [P, M], F32)
+                else:
+                    tanh = ring.tile([P, M], F32, name="tanh", bufs=3)
                 nc.scalar.activation(out=tanh[:], in_=gate[t][:], func=ACT.Tanh, bias=half_bg[:, b, t : t + 1])
-                gated = ring.tile([P, M], F32, name="gated", bufs=3)
+                gated = ring.tile([P, M], F32, name="gated", bufs=4)
                 nc.vector.scalar_tensor_tensor(
                     out=gated[:], in0=tanh[:], scalar=1.0, in1=val[t][:], op0=ALU.add, op1=ALU.mult
                 )
                 if (b, t) in unfused:
+                    if (b, t) == (1, 3):
+                        skip[b, t] = slot("tanh_first", [P, M], F32)[:]
                     if b == 1:
                         gather_skip(b, t)
-                    nc.vector.tensor_tensor(out=skip[b][:, t, :], in0=skip[b][:, t, :], in1=gated[:], op=ALU.add)
+                    adder = nc.gpsimd if PACK * b + t < 5 else nc.vector
+                    adder.tensor_tensor(out=skip[b, t], in0=skip[b, t], in1=gated[:], op=ALU.add)
                 else:
                     nc.vector.tensor_tensor(
-                        out=skip[b][:, t, :], in0=h[b, t][:].indirect(pos2_sb[:]), in1=gated[:], op=ALU.add
+                        out=skip[b, t], in0=h[b, t][:].indirect(pos2_sb[:]), in1=gated[:], op=ALU.add
                     )
-                nc.sync.dma_start(out=out_rows[b, t], in_=skip[b][:, t, :])
+                nc.sync.dma_start(out=out_rows[b, t], in_=skip[b, t])

@@ -20,8 +20,16 @@ P = 128
 PACK = 4
 KP = P * PACK
 BANK = 512
+LIST_ROWS = 16
+QUADRANT = 32
 K_PASSES = K // KP
-H_PASSES = H // KP
+GROUPS = H // KP
+HALVES = S // BANK
+ROUNDED_BUFS = 3
+TANH_BUFS = 2
+GATED_BUFS = 4
+GAIN_PIECES = 4
+GPSIMD_SUMS = 5
 
 
 def tile_list_reef_mosaic_skip_kernel(
@@ -33,29 +41,33 @@ def tile_list_reef_mosaic_skip_kernel(
         ring = ctx.enter_context(tc.tile_pool(name="ring", bufs=1))
         psum = ctx.enter_context(tc.psum_pool(name="psum", bufs=8))
 
-        offs_sb = keep.tile([P, S // 16], U16, name="offs_sb")
-        pos1_sb = keep.tile([P, M // 16], U16, name="pos1_sb")
-        pos2_sb = keep.tile([P, M // 16], U16, name="pos2_sb")
-        tab_scale_sb = keep.tile([P, T], U8, name="tab_scale_sb", align_bytes=64)
-        wa_scale_raw = keep.tile([P, H_PASSES * H], U8, name="wa_scale_raw", align_bytes=64)
-        vec_raw = keep.tile([P, 2, H_PASSES, 2 * PACK], F32, name="vec_raw")
-        vec_half = keep.tile([P, 2, H_PASSES, PACK], F32, name="vec_half")
+        offs_sb = keep.tile([P, S // LIST_ROWS], U16, name="offs_sb")
+        pos1_sb = keep.tile([P, M // LIST_ROWS], U16, name="pos1_sb")
+        pos2_sb = keep.tile([P, M // LIST_ROWS], U16, name="pos2_sb")
+        tab_planes = keep.tile([P, T], U8, name="tab_planes", align_bytes=64)
+        wa_planes_raw = keep.tile([P, GROUPS * H], U8, name="wa_planes_raw", align_bytes=64)
+        vec_raw = keep.tile([P, 2, GROUPS, 2 * PACK], F32, name="vec_raw")
+        vec_half = keep.tile([P, 2, GROUPS, PACK], F32, name="vec_half")
+        warm = keep.tile([P, 1], F32, name="warm")
 
-        nc.gpsimd.memset(tab_scale_sb[:].bitcast(I32), 0)
-        nc.gpsimd.memset(wa_scale_raw[:].bitcast(I32), 0)
-        for q in range(4):
+        nc.gpsimd.memset(tab_planes[:].bitcast(I32), 0)
+        nc.gpsimd.memset(wa_planes_raw[:].bitcast(I32), 0)
+        for q in range(P // QUADRANT):
             nc.scalar.dma_start(
-                out=tab_scale_sb[32 * q : 32 * q + 4 * K_PASSES, :].bitcast(I32),
+                out=tab_planes[QUADRANT * q : QUADRANT * q + 4 * K_PASSES, :].bitcast(I32),
                 in_=tab_scales[:, 4 * q : 4 * q + 4, :].bitcast(I32),
             )
         for i, vec in enumerate((gain, bg)):
-            nc.scalar.dma_start(out=vec_raw[:, i, :, 0:PACK], in_=vec.rearrange("(b p t) -> p b t", b=H_PASSES, t=PACK))
-        for q in range(4):
+            nc.scalar.dma_start(out=vec_raw[:, i, :, 0:PACK], in_=vec.rearrange("(b p t) -> p b t", b=GROUPS, t=PACK))
+        for q in range(P // QUADRANT):
             nc.scalar.dma_start(
-                out=wa_scale_raw[32 * q : 32 * q + 4, :].bitcast(I32).rearrange("r (a c) -> r a c", a=H_PASSES),
+                out=wa_planes_raw[QUADRANT * q : QUADRANT * q + 4, :].bitcast(I32).rearrange("r (a c) -> r a c", a=GROUPS),
                 in_=wa_scales[:, 4 * q : 4 * q + 4, :].bitcast(I32).rearrange("a r c -> r a c"),
             )
-        nc.scalar.activation(out=vec_half[:], in_=vec_raw[:, :, :, 0:PACK], func=ACT.Copy, scale=0.5)
+        nc.gpsimd.tensor_scalar(
+            out=vec_half[:], in0=vec_raw[:, :, :, 0:PACK], scalar1=0.5, scalar2=0.0, op0=ALU.mult, op1=ALU.add
+        )
+        nc.scalar.activation(out=warm[:], in_=vec_half[:, 0, 0, 0:1], func=ACT.Silu)
         half_gain = vec_half[:, 0]
         half_bg = vec_half[:, 1]
 
@@ -75,40 +87,51 @@ def tile_list_reef_mosaic_skip_kernel(
             )
             return raw
 
-        def round_weight(raw, how):
-            rounded = ring.tile([P, KP * PACK], BF16, name="w_bf16", bufs=3, align_bytes=64)
+        def rounding_views(raw, rounded):
             dst = rounded[:].rearrange("p (u v m j) -> p u m j v", u=2, v=2, j=PACK)
             src = raw[:].rearrange("p j (m u v) -> p u m j v", u=2, v=2)
-            if how == "S":
-                nc.scalar.copy(out=dst, in_=src)
-            elif how == "V":
-                nc.vector.tensor_copy(out=dst, in_=src)
-            elif how == "G":
-                for u in range(2):
-                    nc.gpsimd.tensor_copy(out=dst[:, u], in_=src[:, u])
-            else:
-                nc.vector.tensor_copy(out=dst[:, 1], in_=src[:, 1])
-                nc.scalar.copy(out=dst[:, 0], in_=src[:, 0])
+            return dst, src
+
+        def rounded_tile():
+            return ring.tile([P, KP * PACK], BF16, name="w_bf16", bufs=ROUNDED_BUFS, align_bytes=64)
+
+        def round_on_scalar(raw, rounded):
+            dst, src = rounding_views(raw, rounded)
+            nc.scalar.copy(out=dst, in_=src)
             return rounded
 
-        def quantise(rounded, name):
-            codes = keep.tile([P, KP], U32, name=name + "_codes", align_bytes=64)
+        def round_on_vector(raw, rounded):
+            dst, src = rounding_views(raw, rounded)
+            nc.vector.tensor_copy(out=dst, in_=src)
+            return rounded
+
+        def round_on_both(raw, rounded):
+            dst, src = rounding_views(raw, rounded)
+            nc.vector.tensor_copy(out=dst[:, 1], in_=src[:, 1])
+            nc.scalar.copy(out=dst[:, 0], in_=src[:, 0])
+            return rounded
+
+        def quantise(rounded, name, codes=None):
+            if codes is None:
+                codes = keep.tile([P, KP], U32, name=name + "_codes", align_bytes=64)
             scales = keep.tile([P, KP], U8, name=name + "_scales", align_bytes=64)
             nc.vector.quantize_mx(out=codes[:].bitcast(FP8X4), scales=scales[:], in_=rounded[:])
             return codes, scales
 
         def gather_words(words, a):
             halves = []
-            for half in range(2):
+            for half in range(HALVES):
                 picked = keep.tile([P, BANK], U32, name="v_%d_%d" % (a, half), align_bytes=64)
-                nc.vector.tensor_copy(
-                    out=picked[:], in_=words[:].bitcast(U32).indirect(offs_sb[:, 32 * half : 32 * (half + 1)])
-                )
+                entries = offs_sb[:, BANK // LIST_ROWS * half : BANK // LIST_ROWS * (half + 1)]
+                nc.vector.tensor_copy(out=picked[:], in_=words[:].bitcast(U32).indirect(entries))
                 halves.append(picked)
             return halves
 
-        how_w1 = {(0, 0): "S", (1, 0): "X", (2, 0): "X", (0, 1): "V", (1, 1): "X", (2, 1): "X"}
-        how_wb = {(0, 0): "S", (1, 0): "S", (0, 1): "S", (1, 1): "S"}
+        def into_slice_order(dst, src):
+            nc.vector.tensor_copy(
+                out=dst.rearrange("p (g t m) -> p g t m", t=PACK, m=P),
+                in_=src.rearrange("p (g m t) -> p g t m", t=PACK, m=P),
+            )
 
         nc.sync.dma_start(offs_sb[:], offs)
         tab = {}
@@ -119,149 +142,130 @@ def tile_list_reef_mosaic_skip_kernel(
         w1_raw[1, 0] = load_weight(w1, 1, 0, "raw1")
         tab[2] = load_table(2)
         w1_raw[2, 0] = load_weight(w1, 2, 0, "raw2")
-        wa_raw = keep.tile([P, H_PASSES, H // 2], I32, name="wa_raw", align_bytes=64)
-        nc.sync.dma_start(out=wa_raw[:], in_=wa_words.bitcast(I32).rearrange("a p c -> p a c"))
+        w1_raw[0, 1] = load_weight(w1, 0, 1, "raw3")
         nc.sync.dma_start(pos1_sb[:], pos1)
+        w1_raw[1, 1] = load_weight(w1, 1, 1, "raw4")
+        w1_raw[2, 1] = load_weight(w1, 2, 1, "raw5")
         nc.sync.dma_start(pos2_sb[:], pos2)
-        for a in range(K_PASSES):
-            w1_raw[a, 1] = load_weight(w1, a, 1, "raw%d" % (3 + a))
 
         v = {}
         w1_q = {}
         v[0] = gather_words(tab[0], 0)
-        v_scale = keep.tile([P, S], U8, name="v_scale", align_bytes=64)
-        nc.vector.tensor_copy(out=v_scale[:], in_=tab_scale_sb[:].indirect(offs_sb[:]))
+        v_planes = keep.tile([P, S], U8, name="v_planes", align_bytes=64)
+        nc.vector.tensor_copy(out=v_planes[:], in_=tab_planes[:].indirect(offs_sb[:]))
         v[1] = gather_words(tab[1], 1)
-        w1_q[0, 0] = quantise(round_weight(w1_raw[0, 0], how_w1[0, 0]), "w1_0_0")
-        w1_q[1, 0] = quantise(round_weight(w1_raw[1, 0], how_w1[1, 0]), "w1_1_0")
+        w1_q[0, 0] = quantise(round_on_scalar(w1_raw[0, 0], rounded_tile()), "w1_0_0")
+        w1_q[1, 0] = quantise(round_on_both(w1_raw[1, 0], rounded_tile()), "w1_1_0")
         v[2] = gather_words(tab[2], 2)
-        w1_q[2, 0] = quantise(round_weight(w1_raw[2, 0], how_w1[2, 0]), "w1_2_0")
+        w1_q[2, 0] = quantise(round_on_both(w1_raw[2, 0], rounded_tile()), "w1_2_0")
 
-        wa = slot("raw2", [P, H_PASSES * H], U16)
-        nc.vector.tensor_copy(
-            out=wa[:].rearrange("p (g t m) -> p g t m", t=PACK, m=P),
-            in_=wa_raw[:].rearrange("p a c -> p (a c)").bitcast(U16).rearrange("p (g m t) -> p g t m", t=PACK, m=P),
-        )
-        wa_scale = keep.tile([P, H_PASSES * H], U8, name="wa_scale", align_bytes=64)
-        nc.vector.tensor_copy(
-            out=wa_scale[:].rearrange("p (g t m) -> p g t m", t=PACK, m=P),
-            in_=wa_scale_raw[:].rearrange("p (g m t) -> p g t m", t=PACK, m=P),
-        )
-
+        wa_planes = keep.tile([P, GROUPS * H], U8, name="wa_planes", align_bytes=64)
+        into_slice_order(wa_planes[:], wa_planes_raw[:])
         wb_raw = {}
         wb_raw[0, 0] = load_weight(wb, 0, 0, "raw0")
+        wa_raw = keep.tile([P, GROUPS, H // 2], I32, name="wa_raw", align_bytes=64)
+        nc.sync.dma_start(out=wa_raw[:], in_=wa_words.bitcast(I32).rearrange("a p c -> p a c"))
+        wa = slot("raw2", [P, GROUPS * H], U16)
+        into_slice_order(wa[:], wa_raw[:].rearrange("p a c -> p (a c)").bitcast(U16))
         wb_raw[1, 0] = load_weight(wb, 1, 0, "raw1")
         wb_raw[0, 1] = load_weight(wb, 0, 1, "raw6")
 
         def first_product(b):
             acc = {}
             for t in range(PACK):
-                for half in range(2):
+                for half in range(HALVES):
                     acc[t, half] = psum.tile([P, BANK], F32, name="acc")
             for a in range(K_PASSES):
                 codes, scales = w1_q[a, b]
                 for t in range(PACK):
                     cols = slice(P * t, P * (t + 1))
-                    for half in range(2):
+                    for half in range(HALVES):
                         nc.tensor.matmul_mx(
                             out=acc[t, half][:],
                             lhsT=codes[:, cols].bitcast(FP8X4),
                             lhsT_scale=scales[:, cols],
                             rhs=v[a][half][:].bitcast(FP8X4),
-                            rhs_scale=v_scale[4 * a : P, BANK * half : BANK * (half + 1)],
+                            rhs_scale=v_planes[4 * a : P, BANK * half : BANK * (half + 1)],
                             start=(a == 0),
                             stop=(a == K_PASSES - 1),
                         )
             return acc
 
         h = {}
-        skip = {}
-        x_q = {}
-        wb_q = {}
 
         def leave_psum(b, acc):
             for t in range(PACK):
                 h[b, t] = keep.tile([P, S], F32, name="h_%d_%d" % (b, t), align_bytes=64)
-                for half in range(2):
+                for half in range(HALVES):
                     nc.scalar.copy(out=h[b, t][:, BANK * half : BANK * (half + 1)], in_=acc[t, half][:])
 
-        def activation_operand(b, engine):
-            silu = slot("silu%d" % b, [P, PACK, M], F32)
-            for t in range(PACK):
-                deep = slot("deep%d" % t, [P, M], F32)
-                nc.vector.tensor_copy(out=deep[:], in_=h[b, t][:].indirect(pos1_sb[:]))
-                nc.scalar.activation(out=silu[:, t, :], in_=deep[:], func=ACT.Silu)
-            x = ring.tile([P, M * PACK], BF16, name="x_bf16", bufs=2, align_bytes=64)
-            engine.tensor_tensor(
-                out=x[:].rearrange("p (c i t) -> p c t i", i=2, t=PACK),
-                in0=silu[:].rearrange("p t (c i) -> p c t i", i=2),
-                in1=half_gain[:, b, :].unsqueeze(1).unsqueeze(3).to_broadcast([P, M // 2, PACK, 2]),
+        leave_psum(0, first_product(0))
+        w1_q[0, 1] = quantise(round_on_vector(w1_raw[0, 1], rounded_tile()), "w1_0_1")
+        w1_q[1, 1] = quantise(round_on_scalar(w1_raw[1, 1], rounded_tile()), "w1_1_1")
+        w1_q[2, 1] = quantise(round_on_both(w1_raw[2, 1], rounded_tile()), "w1_2_1")
+        wb_raw[1, 1] = load_weight(wb, 1, 1, "raw3")
+        acc_group1 = first_product(1)
+
+        wb_q = {}
+        deep_group0 = slot("deep_group0", [P, PACK, M], F32)
+        for t in range(PACK):
+            nc.vector.tensor_copy(out=deep_group0[:, t, :], in_=h[0, t][:].indirect(pos1_sb[:]))
+        silu0 = slot("silu0", [P, M * PACK], F32)
+        nc.scalar.activation(
+            out=silu0[:].rearrange("p (c i t) -> p c t i", i=2, t=PACK),
+            in_=deep_group0[:].rearrange("p t (c i) -> p c t i", i=2),
+            func=ACT.Silu,
+        )
+        wb_q[0, 0] = quantise(round_on_scalar(wb_raw[0, 0], slot("x0", [P, KP * PACK], BF16)), "wb_0_0")
+        x0 = slot("x0", [P, M * PACK], BF16)
+        piece_width = M * PACK // GAIN_PIECES
+        for piece in range(GAIN_PIECES):
+            cols = slice(piece_width * piece, piece_width * (piece + 1))
+            nc.gpsimd.tensor_tensor(
+                out=x0[:, cols].rearrange("p (m t) -> p m t", t=PACK),
+                in0=silu0[:, cols].rearrange("p (m t) -> p m t", t=PACK),
+                in1=half_gain[:, 0, :].unsqueeze(1).to_broadcast([P, piece_width // PACK, PACK]),
                 op=ALU.mult,
             )
-            x_q[b] = quantise(x, "x_%d" % b)
 
-        def activation_operand_pool(b):
-            deep = slot("deep4", [P, PACK, M], F32)
-            for t in range(PACK):
-                nc.vector.tensor_copy(out=deep[:, t, :], in_=h[b, t][:].indirect(pos1_sb[:]))
-            silu = slot("silu%d" % b, [P, M * PACK], F32)
-            nc.scalar.activation(
-                out=silu[:].rearrange("p (c i t) -> p c t i", i=2, t=PACK),
-                in_=deep[:].rearrange("p t (c i) -> p c t i", i=2),
-                func=ACT.Silu,
-            )
-            x = ring.tile([P, M * PACK], BF16, name="x_bf16", bufs=2, align_bytes=64)
-            for piece in range(4):
-                cols = slice(M * piece, M * (piece + 1))
-                nc.gpsimd.tensor_tensor(
-                    out=x[:, cols].rearrange("p (m t) -> p m t", t=PACK),
-                    in0=silu[:, cols].rearrange("p (m t) -> p m t", t=PACK),
-                    in1=half_gain[:, b, :].unsqueeze(1).to_broadcast([P, M // PACK, PACK]),
-                    op=ALU.mult,
-                )
-            x_q[b] = quantise(x, "x_%d" % b)
+        leave_psum(1, acc_group1)
+        silu1 = slot("silu1", [P, PACK, M], F32)
+        for t in range(PACK):
+            deep = slot("deep%d" % t, [P, M], F32)
+            nc.vector.tensor_copy(out=deep[:], in_=h[1, t][:].indirect(pos1_sb[:]))
+            nc.scalar.activation(out=silu1[:, t, :], in_=deep[:], func=ACT.Silu)
+        x_q = {0: quantise(x0, "x_0", slot("deep1", [P, KP], U32))}
+        x1 = ring.tile([P, M * PACK], BF16, name="x1", align_bytes=64)
+        nc.vector.tensor_tensor(
+            out=x1[:].rearrange("p (c i t) -> p c t i", i=2, t=PACK),
+            in0=silu1[:].rearrange("p t (c i) -> p c t i", i=2),
+            in1=half_gain[:, 1, :].unsqueeze(1).unsqueeze(3).to_broadcast([P, M // 2, PACK, 2]),
+            op=ALU.mult,
+        )
+        x_q[1] = quantise(x1, "x_1")
+        wb_q[1, 0] = quantise(round_on_scalar(wb_raw[1, 0], rounded_tile()), "wb_1_0")
 
-        def quantise_wb(a, b):
-            wb_q[a, b] = quantise(round_weight(wb_raw[a, b], how_wb[a, b]), "wb_%d_%d" % (a, b))
+        skip = {}
+        skip_group0 = slot("raw5", [P, PACK, M], F32)
+        skip[1, 1] = slot("silu1", [P, M], F32)[:]
+        skip[1, 0] = slot("deep2", [P, M], F32)[:]
 
         def gather_skip(b, t):
             nc.vector.tensor_copy(out=skip[b, t], in_=h[b, t][:].indirect(pos2_sb[:]))
 
-        acc0 = first_product(0)
-        leave_psum(0, acc0)
-        for a in range(K_PASSES):
-            w1_q[a, 1] = quantise(round_weight(w1_raw[a, 1], how_w1[a, 1]), "w1_%d_1" % a)
-        wb_raw[1, 1] = load_weight(wb, 1, 1, "raw3")
-        acc1 = first_product(1)
-        activation_operand_pool(0)
-        quantise_wb(0, 0)
-        quantise_wb(1, 0)
-        leave_psum(1, acc1)
-        activation_operand(1, nc.vector)
-
-        skip_first = slot("raw4", [P, PACK, M], F32)
-        skip_late = slot("silu1", [P, 3, M], F32)
         for t in range(PACK):
-            skip[0, t] = skip_first[:, t, :]
-        skip[1, 0] = slot("deep2", [P, M], F32)[:]
-        skip[1, 1] = skip_late[:, 0, :]
-        skip[1, 2] = skip_late[:, 1, :]
-        unfused = [(b, t) for b in range(2) for t in range(4)]
-        for t in range(PACK):
-            if (0, t) in unfused:
-                gather_skip(0, t)
+            skip[0, t] = skip_group0[:, t, :]
+            gather_skip(0, t)
 
-        out_rows = out.rearrange("(b p t) m -> b t p m", b=H_PASSES, t=PACK)
-        for b in range(H_PASSES):
-            if b == 1:
-                quantise_wb(0, 1)
-                quantise_wb(1, 1)
+        out_rows = out.rearrange("(b p t) m -> b t p m", b=GROUPS, t=PACK)
+
+        def second_products(b):
             gate = {}
             val = {}
             for t in range(PACK):
                 gate[t] = psum.tile([P, BANK], F32, name="acc")
                 val[t] = psum.tile([P, BANK], F32, name="acc")
-            for a in range(H_PASSES):
+            for a in range(GROUPS):
                 x_codes, x_scales = x_q[a]
                 wb_codes, wb_scales = wb_q[a, b]
                 for t in range(PACK):
@@ -273,37 +277,50 @@ def tile_list_reef_mosaic_skip_kernel(
                         rhs=x_codes[:].bitcast(FP8X4),
                         rhs_scale=x_scales[:],
                         start=(a == 0),
-                        stop=(a == H_PASSES - 1),
+                        stop=(a == GROUPS - 1),
                     )
                     wa_cols = slice(H * a + KP * b + P * t, H * a + KP * b + P * (t + 1))
                     nc.tensor.matmul_mx(
                         out=val[t][:],
                         lhsT=wa[:, wa_cols].bitcast(FP4X4),
-                        lhsT_scale=wa_scale[:, wa_cols],
+                        lhsT_scale=wa_planes[:, wa_cols],
                         rhs=x_codes[:].bitcast(FP8X4),
                         rhs_scale=x_scales[:],
                         start=(a == 0),
-                        stop=(a == H_PASSES - 1),
+                        stop=(a == GROUPS - 1),
                     )
-            for t in range(PACK):
-                if (b, t) == (0, 0):
-                    tanh = slot("tanh_first", [P, M], F32)
-                else:
-                    tanh = ring.tile([P, M], F32, name="tanh", bufs=3)
-                nc.scalar.activation(out=tanh[:], in_=gate[t][:], func=ACT.Tanh, bias=half_bg[:, b, t : t + 1])
-                gated = ring.tile([P, M], F32, name="gated", bufs=4)
-                nc.vector.scalar_tensor_tensor(
-                    out=gated[:], in0=tanh[:], scalar=1.0, in1=val[t][:], op0=ALU.add, op1=ALU.mult
-                )
-                if (b, t) in unfused:
-                    if (b, t) == (1, 3):
-                        skip[b, t] = slot("tanh_first", [P, M], F32)[:]
-                    if b == 1:
-                        gather_skip(b, t)
-                    adder = nc.gpsimd if PACK * b + t < 5 else nc.vector
-                    adder.tensor_tensor(out=skip[b, t], in0=skip[b, t], in1=gated[:], op=ALU.add)
-                else:
-                    nc.vector.tensor_tensor(
-                        out=skip[b, t], in0=h[b, t][:].indirect(pos2_sb[:]), in1=gated[:], op=ALU.add
-                    )
-                nc.sync.dma_start(out=out_rows[b, t], in_=skip[b, t])
+            return gate, val
+
+        def gated_value(b, t, gate, val, tanh):
+            nc.scalar.activation(out=tanh[:], in_=gate[:], func=ACT.Tanh, bias=half_bg[:, b, t : t + 1])
+            gated = ring.tile([P, M], F32, name="gated", bufs=GATED_BUFS)
+            nc.vector.scalar_tensor_tensor(out=gated[:], in0=tanh[:], scalar=1.0, in1=val[:], op0=ALU.add, op1=ALU.mult)
+            return gated
+
+        def tanh_tile():
+            return ring.tile([P, M], F32, name="tanh", bufs=TANH_BUFS)
+
+        def add_and_store(engine, b, t, gated):
+            engine.tensor_tensor(out=skip[b, t], in0=skip[b, t], in1=gated[:], op=ALU.add)
+            nc.sync.dma_start(out=out_rows[b, t], in_=skip[b, t])
+
+        gate, val = second_products(0)
+        for t in range(PACK):
+            tanh = slot("tanh_%d" % t, [P, M], F32) if t < PACK // 2 else tanh_tile()
+            add_and_store(nc.gpsimd, 0, t, gated_value(0, t, gate[t], val[t], tanh))
+
+        wb_q[0, 1] = quantise(round_on_both(wb_raw[0, 1], slot("deep3", [P, KP * PACK], BF16)), "wb_0_1")
+        wb_q[1, 1] = quantise(round_on_scalar(wb_raw[1, 1], rounded_tile()), "wb_1_1")
+        gate, val = second_products(1)
+        left_to_vector = []
+        for t in range(PACK):
+            gated = gated_value(1, t, gate[t], val[t], tanh_tile())
+            if t >= PACK // 2:
+                skip[1, t] = slot("tanh_%d" % (t - PACK // 2), [P, M], F32)[:]
+            gather_skip(1, t)
+            if PACK + t < GPSIMD_SUMS:
+                add_and_store(nc.gpsimd, 1, t, gated)
+            else:
+                left_to_vector.append((t, gated))
+        for t, gated in left_to_vector:
+            add_and_store(nc.vector, 1, t, gated)

@@ -127,18 +127,18 @@ def tile_list_reef_mosaic_skip_kernel(
                 halves.append(picked)
             return halves
 
-        def into_slice_order(dst, src):
-            nc.vector.tensor_copy(
-                out=dst.rearrange("p (g t m) -> p g t m", t=PACK, m=P),
-                in_=src.rearrange("p (g m t) -> p g t m", t=PACK, m=P),
-            )
+        def into_slice_order(dst, src, width):
+            dst_runs = dst.rearrange("p (g t m e) -> p g t m e", t=PACK, m=P, e=width)
+            src_runs = src.rearrange("p (g m t e) -> p g t m e", t=PACK, m=P, e=width)
+            for g in range(GROUPS * GROUPS):
+                nc.gpsimd.tensor_copy(out=dst_runs[:, g], in_=src_runs[:, g])
 
         nc.sync.dma_start(offs_sb[:], offs)
         tab = {}
         w1_raw = {}
         tab[0] = load_table(0)
-        tab[1] = load_table(1)
         w1_raw[0, 0] = load_weight(w1, 0, 0, "raw0")
+        tab[1] = load_table(1)
         w1_raw[1, 0] = load_weight(w1, 1, 0, "raw1")
         tab[2] = load_table(2)
         w1_raw[2, 0] = load_weight(w1, 2, 0, "raw2")
@@ -155,18 +155,18 @@ def tile_list_reef_mosaic_skip_kernel(
         nc.vector.tensor_copy(out=v_planes[:], in_=tab_planes[:].indirect(offs_sb[:]))
         v[1] = gather_words(tab[1], 1)
         w1_q[0, 0] = quantise(round_on_scalar(w1_raw[0, 0], rounded_tile()), "w1_0_0")
-        w1_q[1, 0] = quantise(round_on_both(w1_raw[1, 0], rounded_tile()), "w1_1_0")
+        w1_q[1, 0] = quantise(round_on_scalar(w1_raw[1, 0], rounded_tile()), "w1_1_0")
         v[2] = gather_words(tab[2], 2)
         w1_q[2, 0] = quantise(round_on_both(w1_raw[2, 0], rounded_tile()), "w1_2_0")
 
         wa_planes = keep.tile([P, GROUPS * H], U8, name="wa_planes", align_bytes=64)
-        into_slice_order(wa_planes[:], wa_planes_raw[:])
+        into_slice_order(wa_planes[:], wa_planes_raw[:], 1)
         wb_raw = {}
         wb_raw[0, 0] = load_weight(wb, 0, 0, "raw0")
         wa_raw = keep.tile([P, GROUPS, H // 2], I32, name="wa_raw", align_bytes=64)
         nc.sync.dma_start(out=wa_raw[:], in_=wa_words.bitcast(I32).rearrange("a p c -> p a c"))
         wa = slot("raw2", [P, GROUPS * H], U16)
-        into_slice_order(wa[:], wa_raw[:].rearrange("p a c -> p (a c)").bitcast(U16))
+        into_slice_order(wa[:].bitcast(U8), wa_raw[:].rearrange("p a c -> p (a c)").bitcast(U8), 2)
         wb_raw[1, 0] = load_weight(wb, 1, 0, "raw1")
         wb_raw[0, 1] = load_weight(wb, 0, 1, "raw6")
 
@@ -322,5 +322,10 @@ def tile_list_reef_mosaic_skip_kernel(
                 add_and_store(nc.gpsimd, 1, t, gated)
             else:
                 left_to_vector.append((t, gated))
-        for t, gated in left_to_vector:
+        for t, gated in left_to_vector[:-1]:
             add_and_store(nc.vector, 1, t, gated)
+        t, gated = left_to_vector[-1]
+        for half in range(2):
+            cols = slice(M // 2 * half, M // 2 * (half + 1))
+            nc.vector.tensor_tensor(out=skip[1, t][:, cols], in0=skip[1, t][:, cols], in1=gated[:, cols], op=ALU.add)
+            nc.sync.dma_start(out=out_rows[1, t][:, cols], in_=skip[1, t][:, cols])

@@ -27,7 +27,7 @@ GROUPS = H // KP
 HALVES = S // BANK
 ROUNDED_BUFS = 3
 TANH_BUFS = 2
-GATED_BUFS = 4
+GATED_BUFS = 6
 GAIN_PIECES = 4
 GPSIMD_SUMS = 5
 
@@ -50,8 +50,8 @@ def tile_list_reef_mosaic_skip_kernel(
         vec_half = keep.tile([P, 2, GROUPS, PACK], F32, name="vec_half")
         warm = keep.tile([P, 1], F32, name="warm")
 
-        nc.gpsimd.memset(tab_planes[:].bitcast(I32), 0)
-        nc.gpsimd.memset(wa_planes_raw[:].bitcast(I32), 0)
+        nc.vector.memset(tab_planes[:].bitcast(I32), 0)
+        nc.vector.memset(wa_planes_raw[:].bitcast(I32), 0)
         for q in range(P // QUADRANT):
             nc.scalar.dma_start(
                 out=tab_planes[QUADRANT * q : QUADRANT * q + 4 * K_PASSES, :].bitcast(I32),
@@ -64,7 +64,7 @@ def tile_list_reef_mosaic_skip_kernel(
                 out=wa_planes_raw[QUADRANT * q : QUADRANT * q + 4, :].bitcast(I32).rearrange("r (a c) -> r a c", a=GROUPS),
                 in_=wa_scales[:, 4 * q : 4 * q + 4, :].bitcast(I32).rearrange("a r c -> r a c"),
             )
-        nc.gpsimd.tensor_scalar(
+        nc.vector.tensor_scalar(
             out=vec_half[:], in0=vec_raw[:, :, :, 0:PACK], scalar1=0.5, scalar2=0.0, op0=ALU.mult, op1=ALU.add
         )
         nc.scalar.activation(out=warm[:], in_=vec_half[:, 0, 0, 0:1], func=ACT.Silu)
@@ -75,7 +75,7 @@ def tile_list_reef_mosaic_skip_kernel(
             return ring.tile(shape, dtype, name=tag, tag=tag, align_bytes=64)
 
         def load_table(a):
-            words = keep.tile([P, T], I32, name="tab_%d" % a, align_bytes=64)
+            words = slot("tab_%d" % a, [P, T], I32)
             nc.sync.dma_start(out=words[:], in_=tab_words[a].rearrange("p t i -> p (t i)").bitcast(I32))
             return words
 
@@ -92,8 +92,8 @@ def tile_list_reef_mosaic_skip_kernel(
             src = raw[:].rearrange("p j (m u v) -> p u m j v", u=2, v=2)
             return dst, src
 
-        def rounded_tile():
-            return ring.tile([P, KP * PACK], BF16, name="w_bf16", bufs=ROUNDED_BUFS, align_bytes=64)
+        def rounded_tile(tag):
+            return slot(tag, [P, KP * PACK], BF16)
 
         def round_on_scalar(raw, rounded):
             dst, src = rounding_views(raw, rounded)
@@ -107,15 +107,31 @@ def tile_list_reef_mosaic_skip_kernel(
 
         def round_on_both(raw, rounded):
             dst, src = rounding_views(raw, rounded)
-            nc.vector.tensor_copy(out=dst[:, 1], in_=src[:, 1])
-            nc.scalar.copy(out=dst[:, 0], in_=src[:, 0])
+            nc.vector.tensor_copy(out=dst[:, 0], in_=src[:, 0])
+            nc.scalar.copy(out=dst[:, 1], in_=src[:, 1])
             return rounded
 
-        def quantise(rounded, name, codes=None):
+        def round_on_gpsimd(raw, rounded):
+            dst = rounded[:].rearrange("p (u v m j) -> p u m v j", u=2, v=2, j=PACK)
+            src = raw[:].rearrange("p j (m u v) -> p u m v j", u=2, v=2)
+            for u in range(2):
+                for c in range(2):
+                    cols = slice(P // 2 * c, P // 2 * (c + 1))
+                    nc.gpsimd.tensor_copy(out=dst[:, u, cols], in_=src[:, u, cols])
+            return rounded
+
+        def quantise(rounded, name, codes=None, parts=1):
             if codes is None:
                 codes = keep.tile([P, KP], U32, name=name + "_codes", align_bytes=64)
             scales = keep.tile([P, KP], U8, name=name + "_scales", align_bytes=64)
-            nc.vector.quantize_mx(out=codes[:].bitcast(FP8X4), scales=scales[:], in_=rounded[:])
+            width = KP // parts
+            for part in range(parts):
+                cols = slice(width * part, width * (part + 1))
+                nc.vector.quantize_mx(
+                    out=codes[:, cols].bitcast(FP8X4),
+                    scales=scales[:, cols],
+                    in_=rounded[:, PACK * width * part : PACK * width * (part + 1)],
+                )
             return codes, scales
 
         def gather_words(words, a):
@@ -127,96 +143,176 @@ def tile_list_reef_mosaic_skip_kernel(
                 halves.append(picked)
             return halves
 
-        def into_slice_order(dst, src, width):
-            dst_runs = dst.rearrange("p (g t m e) -> p g t m e", t=PACK, m=P, e=width)
-            src_runs = src.rearrange("p (g m t e) -> p g t m e", t=PACK, m=P, e=width)
-            for g in range(GROUPS * GROUPS):
-                nc.gpsimd.tensor_copy(out=dst_runs[:, g], in_=src_runs[:, g])
 
-        nc.sync.dma_start(offs_sb[:], offs)
-        tab = {}
-        w1_raw = {}
-        tab[0] = load_table(0)
-        w1_raw[0, 0] = load_weight(w1, 0, 0, "raw0")
-        tab[1] = load_table(1)
-        w1_raw[1, 0] = load_weight(w1, 1, 0, "raw1")
-        tab[2] = load_table(2)
-        w1_raw[2, 0] = load_weight(w1, 2, 0, "raw2")
-        w1_raw[0, 1] = load_weight(w1, 0, 1, "raw3")
-        nc.sync.dma_start(pos1_sb[:], pos1)
-        w1_raw[1, 1] = load_weight(w1, 1, 1, "raw4")
-        w1_raw[2, 1] = load_weight(w1, 2, 1, "raw5")
-        nc.sync.dma_start(pos2_sb[:], pos2)
-
+        h = {}
+        skip = {}
         v = {}
         w1_q = {}
-        v[0] = gather_words(tab[0], 0)
-        v_planes = keep.tile([P, S], U8, name="v_planes", align_bytes=64)
-        nc.vector.tensor_copy(out=v_planes[:], in_=tab_planes[:].indirect(offs_sb[:]))
-        v[1] = gather_words(tab[1], 1)
-        w1_q[0, 0] = quantise(round_on_scalar(w1_raw[0, 0], rounded_tile()), "w1_0_0")
-        w1_q[1, 0] = quantise(round_on_scalar(w1_raw[1, 0], rounded_tile()), "w1_1_0")
-        v[2] = gather_words(tab[2], 2)
-        w1_q[2, 0] = quantise(round_on_both(w1_raw[2, 0], rounded_tile()), "w1_2_0")
+        wb_q = {}
+        x_q = {}
+        out_rows = out.rearrange("(b p t) m -> b t p m", b=GROUPS, t=PACK)
 
-        wa_planes = keep.tile([P, GROUPS * H], U8, name="wa_planes", align_bytes=64)
-        into_slice_order(wa_planes[:], wa_planes_raw[:], 1)
-        wb_raw = {}
-        wb_raw[0, 0] = load_weight(wb, 0, 0, "raw0")
-        wa_raw = keep.tile([P, GROUPS, H // 2], I32, name="wa_raw", align_bytes=64)
-        nc.sync.dma_start(out=wa_raw[:], in_=wa_words.bitcast(I32).rearrange("a p c -> p a c"))
-        wa = slot("raw2", [P, GROUPS * H], U16)
-        into_slice_order(wa[:].bitcast(U8), wa_raw[:].rearrange("p a c -> p (a c)").bitcast(U8), 2)
-        wb_raw[1, 0] = load_weight(wb, 1, 0, "raw1")
-        wb_raw[0, 1] = load_weight(wb, 0, 1, "raw6")
-
-        def first_product(b):
+        def banks():
             acc = {}
             for t in range(PACK):
                 for half in range(HALVES):
                     acc[t, half] = psum.tile([P, BANK], F32, name="acc")
-            for a in range(K_PASSES):
-                codes, scales = w1_q[a, b]
-                for t in range(PACK):
-                    cols = slice(P * t, P * (t + 1))
-                    for half in range(HALVES):
-                        nc.tensor.matmul_mx(
-                            out=acc[t, half][:],
-                            lhsT=codes[:, cols].bitcast(FP8X4),
-                            lhsT_scale=scales[:, cols],
-                            rhs=v[a][half][:].bitcast(FP8X4),
-                            rhs_scale=v_planes[4 * a : P, BANK * half : BANK * (half + 1)],
-                            start=(a == 0),
-                            stop=(a == K_PASSES - 1),
-                        )
             return acc
 
-        h = {}
-
-        def leave_psum(b, acc):
-            for t in range(PACK):
-                h[b, t] = keep.tile([P, S], F32, name="h_%d_%d" % (b, t), align_bytes=64)
+        def first_pass(acc, a, b, slices=range(PACK)):
+            codes, scales = w1_q[a, b]
+            for t in slices:
+                cols = slice(P * t, P * (t + 1))
                 for half in range(HALVES):
+                    nc.tensor.matmul_mx(
+                        out=acc[t, half][:],
+                        lhsT=codes[:, cols].bitcast(FP8X4),
+                        lhsT_scale=scales[:, cols],
+                        rhs=v[a][half][:].bitcast(FP8X4),
+                        rhs_scale=v_planes[4 * a : P, BANK * half : BANK * (half + 1)],
+                        start=(a == 0),
+                        stop=(a == K_PASSES - 1),
+                    )
+
+        def leave_psum(b, acc, t, engines=(None, None)):
+            h[b, t] = slot("h_%d_%d" % (b, t), [P, S], F32)
+            for half in range(HALVES):
+                if engines[half] is None:
                     nc.scalar.copy(out=h[b, t][:, BANK * half : BANK * (half + 1)], in_=acc[t, half][:])
+                else:
+                    nc.vector.tensor_copy(out=h[b, t][:, BANK * half : BANK * (half + 1)], in_=acc[t, half][:])
 
-        leave_psum(0, first_product(0))
-        w1_q[0, 1] = quantise(round_on_vector(w1_raw[0, 1], rounded_tile()), "w1_0_1")
-        w1_q[1, 1] = quantise(round_on_scalar(w1_raw[1, 1], rounded_tile()), "w1_1_1")
-        w1_q[2, 1] = quantise(round_on_both(w1_raw[2, 1], rounded_tile()), "w1_2_1")
-        wb_raw[1, 1] = load_weight(wb, 1, 1, "raw3")
-        acc_group1 = first_product(1)
+        def gather_skip(b, t):
+            nc.vector.tensor_copy(out=skip[b, t], in_=h[b, t][:].indirect(pos2_sb[:]))
 
-        wb_q = {}
+        def gate_pass(acc, a, b, t):
+            x_codes, x_scales = x_q[a]
+            wb_codes, wb_scales = wb_q[a, b]
+            cols = slice(P * t, P * (t + 1))
+            nc.tensor.matmul_mx(
+                out=acc[t, 0][:],
+                lhsT=wb_codes[:, cols].bitcast(FP8X4),
+                lhsT_scale=wb_scales[:, cols],
+                rhs=x_codes[:, 0:KP].bitcast(FP8X4),
+                rhs_scale=x_scales[:],
+                start=(a == 0),
+                stop=(a == GROUPS - 1),
+            )
+
+        def value_pass(acc, a, b, t):
+            x_codes, x_scales = x_q[a]
+            wa_cols = slice(H * a + KP * b + P * t, H * a + KP * b + P * (t + 1))
+            nc.tensor.matmul_mx(
+                out=acc[t, 1][:],
+                lhsT=wa[:, wa_cols].bitcast(FP4X4),
+                lhsT_scale=wa_planes[:, wa_cols],
+                rhs=x_codes[:, 0:KP].bitcast(FP8X4),
+                rhs_scale=x_scales[:],
+                start=(a == 0),
+                stop=(a == GROUPS - 1),
+            )
+
+        def second_pass(acc, a, b):
+            for t in range(PACK):
+                gate_pass(acc, a, b, t)
+                value_pass(acc, a, b, t)
+
+        def tanh_of(b, t, acc, tanh):
+            nc.scalar.activation(out=tanh[:], in_=acc[t, 0][:], func=ACT.Tanh, bias=half_bg[:, b, t : t + 1])
+            return tanh
+
+        def gated_value(t, acc, tanh):
+            gated = ring.tile([P, M], F32, name="gated", bufs=GATED_BUFS)
+            nc.vector.scalar_tensor_tensor(out=gated[:], in0=tanh[:], scalar=1.0, in1=acc[t, 1][:], op0=ALU.add, op1=ALU.mult)
+            return gated
+
+        def add_and_store(engine, b, t, gated):
+            engine.tensor_tensor(out=skip[b, t], in0=skip[b, t], in1=gated[:], op=ALU.add)
+            nc.sync.dma_start(out=out_rows[b, t], in_=skip[b, t])
+
+        def fused_and_store(b, t, gated, parts=1):
+            res = slot(("raw1", "raw4", "raw5", "raw2")[t], [P, M], F32)
+            w = M // parts
+            for part in range(parts):
+                cols = slice(w * part, w * (part + 1))
+                entries = pos2_sb[:, w // LIST_ROWS * part : w // LIST_ROWS * (part + 1)]
+                nc.vector.tensor_tensor(out=res[:, cols], in0=h[b, t][:].indirect(entries), in1=gated[:, cols], op=ALU.add)
+                nc.scalar.dma_start(out=out_rows[b, t][:, cols], in_=res[:, cols])
+
+        def gather_deep(b, t, deep):
+            nc.vector.tensor_copy(out=deep, in_=h[b, t][:].indirect(pos1_sb[:]))
+
+        nc.sync.dma_start(offs_sb[:], offs)
+        tab = {}
+        w1_raw = {}
+        wb_raw = {}
+        for a in range(K_PASSES):
+            tab[a] = load_table(a)
+            w1_raw[a, 0] = load_weight(w1, a, 0, "raw%d" % a)
+        w1_raw[0, 1] = load_weight(w1, 0, 1, "raw3")
+        nc.sync.dma_start(pos1_sb[:], pos1)
+        nc.sync.dma_start(pos2_sb[:], pos2)
+        w1_raw[1, 1] = load_weight(w1, 1, 1, "raw4")
+        w1_raw[2, 1] = load_weight(w1, 2, 1, "raw5")
+
+        v[0] = gather_words(tab[0], 0)
+        v_planes = keep.tile([P, S], U8, name="v_planes", align_bytes=64)
+        nc.vector.tensor_copy(out=v_planes[:], in_=tab_planes[:].indirect(offs_sb[:]))
+        v[1] = gather_words(tab[1], 1)
+        acc = banks()
+        w1_q[0, 0] = quantise(round_on_scalar(w1_raw[0, 0], rounded_tile("r0")), "w1_0_0")
+        first_pass(acc, 0, 0)
+        w1_q[1, 0] = quantise(round_on_both(w1_raw[1, 0], rounded_tile("r1")), "w1_1_0")
+        first_pass(acc, 1, 0)
+        v[2] = gather_words(tab[2], 2)
+        w1_q[2, 0] = quantise(round_on_both(w1_raw[2, 0], rounded_tile("r2")), "w1_2_0", parts=2)
+        first_pass(acc, 2, 0)
+
+        wa_planes = keep.tile([P, GROUPS * H], U8, name="wa_planes", align_bytes=64)
+        dst_runs = wa_planes[:].rearrange("p (g t m) -> p g t m", t=PACK, m=P)
+        src_runs = wa_planes_raw[:].rearrange("p (g m t) -> p g t m", t=PACK, m=P)
+        for g in range(GROUPS * GROUPS):
+            nc.gpsimd.tensor_copy(out=dst_runs[:, g], in_=src_runs[:, g])
+        wb_raw[0, 0] = load_weight(wb, 0, 0, "raw0")
+        wa_raw = slot("tab_0", [P, GROUPS, H // 2], I32)
+        nc.sync.dma_start(out=wa_raw[:], in_=wa_words.bitcast(I32).rearrange("a p c -> p a c"))
+        wb_raw[1, 0] = load_weight(wb, 1, 0, "raw1")
+        wb_raw[0, 1] = load_weight(wb, 0, 1, "raw2")
+        wb_raw[1, 1] = load_weight(wb, 1, 1, "tab_1")
+
+        leave_psum(0, acc, 0)
+        r01 = round_on_vector(w1_raw[0, 1], rounded_tile("r0"))
+        for t in range(1, PACK):
+            leave_psum(0, acc, t)
         deep_group0 = slot("deep_group0", [P, PACK, M], F32)
+        gather_deep(0, 0, deep_group0[:, 0, :])
+        w1_q[0, 1] = quantise(r01, "w1_0_1")
+        acc = banks()
+        first_pass(acc, 0, 1)
+        r11 = round_on_scalar(w1_raw[1, 1], rounded_tile("r1"))
+        gather_deep(0, 1, deep_group0[:, 1, :])
+        gather_deep(0, 2, deep_group0[:, 2, :])
+        r21 = round_on_vector(w1_raw[2, 1], rounded_tile("r2"))
+        gather_deep(0, 3, deep_group0[:, 3, :])
+        w1_q[1, 1] = quantise(r11, "w1_1_1")
+        w1_q[2, 1] = quantise(r21, "w1_2_1")
         for t in range(PACK):
-            nc.vector.tensor_copy(out=deep_group0[:, t, :], in_=h[0, t][:].indirect(pos1_sb[:]))
+            first_pass(acc, 1, 1, [t])
+            first_pass(acc, 2, 1, [t])
+        wa = slot("wa", [P, GROUPS * H], U16)
+        nc.vector.tensor_copy(
+            out=wa[:].rearrange("p (g t m) -> p g t m", t=PACK, m=P),
+            in_=wa_raw[:].rearrange("p a c -> p (a c)").bitcast(U16).rearrange("p (g m t) -> p g t m", t=PACK, m=P),
+        )
+
         silu0 = slot("silu0", [P, M * PACK], F32)
         nc.scalar.activation(
             out=silu0[:].rearrange("p (c i t) -> p c t i", i=2, t=PACK),
             in_=deep_group0[:].rearrange("p t (c i) -> p c t i", i=2),
             func=ACT.Silu,
         )
-        wb_q[0, 0] = quantise(round_on_scalar(wb_raw[0, 0], slot("x0", [P, KP * PACK], BF16)), "wb_0_0")
+
+        rounded_wb00 = round_on_scalar(wb_raw[0, 0], rounded_tile("deep_group0"))
         x0 = slot("x0", [P, M * PACK], BF16)
         piece_width = M * PACK // GAIN_PIECES
         for piece in range(GAIN_PIECES):
@@ -228,13 +324,20 @@ def tile_list_reef_mosaic_skip_kernel(
                 op=ALU.mult,
             )
 
-        leave_psum(1, acc_group1)
+        both = slot("r2", [P, 2, M], F32)
+        for t in range(2):
+            skip[0, t] = both[:, t, :]
+            gather_skip(0, t)
+
         silu1 = slot("silu1", [P, PACK, M], F32)
         for t in range(PACK):
+            leave_psum(1, acc, t)
+        for t in range(PACK):
             deep = slot("deep%d" % t, [P, M], F32)
-            nc.vector.tensor_copy(out=deep[:], in_=h[1, t][:].indirect(pos1_sb[:]))
+            gather_deep(1, t, deep[:])
             nc.scalar.activation(out=silu1[:, t, :], in_=deep[:], func=ACT.Silu)
-        x_q = {0: quantise(x0, "x_0", slot("deep1", [P, KP], U32))}
+        x_q[0] = quantise(x0, "x_0", slot("deep1", [P, KP], U32))
+        wb_q[0, 0] = quantise(rounded_wb00, "wb_0_0", slot("deep2", [P, KP], U32))
         x1 = ring.tile([P, M * PACK], BF16, name="x1", align_bytes=64)
         nc.vector.tensor_tensor(
             out=x1[:].rearrange("p (c i t) -> p c t i", i=2, t=PACK),
@@ -242,90 +345,40 @@ def tile_list_reef_mosaic_skip_kernel(
             in1=half_gain[:, 1, :].unsqueeze(1).unsqueeze(3).to_broadcast([P, M // 2, PACK, 2]),
             op=ALU.mult,
         )
+
         x_q[1] = quantise(x1, "x_1")
-        wb_q[1, 0] = quantise(round_on_scalar(wb_raw[1, 0], rounded_tile()), "wb_1_0")
-
-        skip = {}
-        skip_group0 = slot("raw5", [P, PACK, M], F32)
-        skip[1, 1] = slot("silu1", [P, M], F32)[:]
-        skip[1, 0] = slot("deep2", [P, M], F32)[:]
-
-        def gather_skip(b, t):
-            nc.vector.tensor_copy(out=skip[b, t], in_=h[b, t][:].indirect(pos2_sb[:]))
-
+        wb_q[1, 0] = quantise(round_on_scalar(wb_raw[1, 0], rounded_tile("deep0")), "wb_1_0")
+        acc = banks()
         for t in range(PACK):
-            skip[0, t] = skip_group0[:, t, :]
-            gather_skip(0, t)
-
-        out_rows = out.rearrange("(b p t) m -> b t p m", b=GROUPS, t=PACK)
-
-        def second_products(b):
-            gate = {}
-            val = {}
-            for t in range(PACK):
-                gate[t] = psum.tile([P, BANK], F32, name="acc")
-                val[t] = psum.tile([P, BANK], F32, name="acc")
+            value_pass(acc, 0, 0, t)
+        for t in range(PACK):
             for a in range(GROUPS):
-                x_codes, x_scales = x_q[a]
-                wb_codes, wb_scales = wb_q[a, b]
-                for t in range(PACK):
-                    cols = slice(P * t, P * (t + 1))
-                    nc.tensor.matmul_mx(
-                        out=gate[t][:],
-                        lhsT=wb_codes[:, cols].bitcast(FP8X4),
-                        lhsT_scale=wb_scales[:, cols],
-                        rhs=x_codes[:].bitcast(FP8X4),
-                        rhs_scale=x_scales[:],
-                        start=(a == 0),
-                        stop=(a == GROUPS - 1),
-                    )
-                    wa_cols = slice(H * a + KP * b + P * t, H * a + KP * b + P * (t + 1))
-                    nc.tensor.matmul_mx(
-                        out=val[t][:],
-                        lhsT=wa[:, wa_cols].bitcast(FP4X4),
-                        lhsT_scale=wa_planes[:, wa_cols],
-                        rhs=x_codes[:].bitcast(FP8X4),
-                        rhs_scale=x_scales[:],
-                        start=(a == 0),
-                        stop=(a == GROUPS - 1),
-                    )
-            return gate, val
-
-        def gated_value(b, t, gate, val, tanh):
-            nc.scalar.activation(out=tanh[:], in_=gate[:], func=ACT.Tanh, bias=half_bg[:, b, t : t + 1])
-            gated = ring.tile([P, M], F32, name="gated", bufs=GATED_BUFS)
-            nc.vector.scalar_tensor_tensor(out=gated[:], in0=tanh[:], scalar=1.0, in1=val[:], op0=ALU.add, op1=ALU.mult)
-            return gated
-
-        def tanh_tile():
-            return ring.tile([P, M], F32, name="tanh", bufs=TANH_BUFS)
-
-        def add_and_store(engine, b, t, gated):
-            engine.tensor_tensor(out=skip[b, t], in0=skip[b, t], in1=gated[:], op=ALU.add)
-            nc.sync.dma_start(out=out_rows[b, t], in_=skip[b, t])
-
-        gate, val = second_products(0)
+                gate_pass(acc, a, 0, t)
+            value_pass(acc, 1, 0, t)
+        r_b01 = round_on_scalar(wb_raw[0, 1], rounded_tile("raw3"))
+        r_b11 = round_on_scalar(wb_raw[1, 1], rounded_tile("r1"))
+        skip[0, 2] = slot("x1", [P, M], F32)[:]
+        gather_skip(0, 2)
+        wb_q[0, 1] = quantise(r_b01, "wb_0_1", slot("h_0_2", [P, KP], U32))
+        skip[0, 3] = slot("raw3", [P, M], F32)[:]
+        gather_skip(0, 3)
+        wb_q[1, 1] = quantise(r_b11, "wb_1_1", slot("h_0_3", [P, KP], U32))
+        gated = {}
         for t in range(PACK):
-            tanh = slot("tanh_%d" % t, [P, M], F32) if t < PACK // 2 else tanh_tile()
-            add_and_store(nc.gpsimd, 0, t, gated_value(0, t, gate[t], val[t], tanh))
-
-        wb_q[0, 1] = quantise(round_on_both(wb_raw[0, 1], slot("deep3", [P, KP * PACK], BF16)), "wb_0_1")
-        wb_q[1, 1] = quantise(round_on_scalar(wb_raw[1, 1], rounded_tile()), "wb_1_1")
-        gate, val = second_products(1)
-        left_to_vector = []
+            gated[t] = gated_value(t, acc, tanh_of(0, t, acc, slot("tanh_%d" % t, [P, M], F32)))
+            add_and_store(nc.gpsimd, 0, t, gated[t])
+        acc = banks()
         for t in range(PACK):
-            gated = gated_value(1, t, gate[t], val[t], tanh_tile())
-            if t >= PACK // 2:
-                skip[1, t] = slot("tanh_%d" % (t - PACK // 2), [P, M], F32)[:]
-            gather_skip(1, t)
-            if PACK + t < GPSIMD_SUMS:
-                add_and_store(nc.gpsimd, 1, t, gated)
-            else:
-                left_to_vector.append((t, gated))
-        for t, gated in left_to_vector[:-1]:
-            add_and_store(nc.vector, 1, t, gated)
-        t, gated = left_to_vector[-1]
-        for half in range(2):
-            cols = slice(M // 2 * half, M // 2 * (half + 1))
-            nc.vector.tensor_tensor(out=skip[1, t][:, cols], in0=skip[1, t][:, cols], in1=gated[:, cols], op=ALU.add)
-            nc.sync.dma_start(out=out_rows[1, t][:, cols], in_=skip[1, t][:, cols])
+            for a in range(GROUPS):
+                gate_pass(acc, a, 1, t)
+            for a in range(GROUPS):
+                value_pass(acc, a, 1, t)
+        skip[1, 0] = slot("tanh_3", [P, M], F32)[:]
+        gather_skip(1, 0)
+        for t in range(PACK):
+            gated[t] = gated_value(t, acc, tanh_of(1, t, acc, slot("tanh_%d" % ((4, 0, 1, 2)[t]), [P, M], F32)))
+            if t == 0:
+                add_and_store(nc.gpsimd, 1, t, gated[t])
+            if t >= 2:
+                fused_and_store(1, t - 1, gated[t - 1])
+        fused_and_store(1, 3, gated[3], parts=2)

@@ -52,15 +52,18 @@ def tile_list_reef_mosaic_skip_kernel(
 
         nc.vector.memset(tab_planes[:].bitcast(I32), 0)
         nc.vector.memset(wa_planes_raw[:].bitcast(I32), 0)
-        for q in range(P // QUADRANT):
-            nc.scalar.dma_start(
+        def load_table_scales(queue, q):
+            queue.dma_start(
                 out=tab_planes[QUADRANT * q : QUADRANT * q + 4 * K_PASSES, :].bitcast(I32),
                 in_=tab_scales[:, 4 * q : 4 * q + 4, :].bitcast(I32),
             )
+
+        for q in range(2):
+            load_table_scales(nc.scalar, q)
         for i, vec in enumerate((gain, bg)):
             nc.scalar.dma_start(out=vec_raw[:, i, :, 0:PACK], in_=vec.rearrange("(b p t) -> p b t", b=GROUPS, t=PACK))
         for q in range(P // QUADRANT):
-            nc.scalar.dma_start(
+            nc.gpsimd.dma_start(
                 out=wa_planes_raw[QUADRANT * q : QUADRANT * q + 4, :].bitcast(I32).rearrange("r (a c) -> r a c", a=GROUPS),
                 in_=wa_scales[:, 4 * q : 4 * q + 4, :].bitcast(I32).rearrange("a r c -> r a c"),
             )
@@ -111,14 +114,16 @@ def tile_list_reef_mosaic_skip_kernel(
             nc.scalar.copy(out=dst[:, 1], in_=src[:, 1])
             return rounded
 
-        def round_on_gpsimd(raw, rounded):
+        def round_half_on_gpsimd(raw, rounded, u):
             dst = rounded[:].rearrange("p (u v m j) -> p u m v j", u=2, v=2, j=PACK)
             src = raw[:].rearrange("p j (m u v) -> p u m v j", u=2, v=2)
-            for u in range(2):
-                for c in range(2):
-                    cols = slice(P // 2 * c, P // 2 * (c + 1))
-                    nc.gpsimd.tensor_copy(out=dst[:, u, cols], in_=src[:, u, cols])
-            return rounded
+            for c in range(2):
+                cols = slice(P // 2 * c, P // 2 * (c + 1))
+                nc.gpsimd.tensor_copy(out=dst[:, u, cols], in_=src[:, u, cols])
+
+        def round_half_on_scalar(raw, rounded, u):
+            dst, src = rounding_views(raw, rounded)
+            nc.scalar.copy(out=dst[:, u], in_=src[:, u])
 
         def quantise(rounded, name, codes=None, parts=1):
             if codes is None:
@@ -135,12 +140,12 @@ def tile_list_reef_mosaic_skip_kernel(
             return codes, scales
 
         def gather_words(words, a):
+            picked = slot("v_%d" % a, [P, S], U32)
             halves = []
             for half in range(HALVES):
-                picked = keep.tile([P, BANK], U32, name="v_%d_%d" % (a, half), align_bytes=64)
                 entries = offs_sb[:, BANK // LIST_ROWS * half : BANK // LIST_ROWS * (half + 1)]
-                nc.vector.tensor_copy(out=picked[:], in_=words[:].bitcast(U32).indirect(entries))
-                halves.append(picked)
+                halves.append(picked[:, BANK * half : BANK * (half + 1)])
+                nc.vector.tensor_copy(out=halves[half], in_=words[:].bitcast(U32).indirect(entries))
             return halves
 
 
@@ -168,7 +173,7 @@ def tile_list_reef_mosaic_skip_kernel(
                         out=acc[t, half][:],
                         lhsT=codes[:, cols].bitcast(FP8X4),
                         lhsT_scale=scales[:, cols],
-                        rhs=v[a][half][:].bitcast(FP8X4),
+                        rhs=v[a][half].bitcast(FP8X4),
                         rhs_scale=v_planes[4 * a : P, BANK * half : BANK * (half + 1)],
                         start=(a == 0),
                         stop=(a == K_PASSES - 1),
@@ -184,6 +189,12 @@ def tile_list_reef_mosaic_skip_kernel(
 
         def gather_skip(b, t):
             nc.vector.tensor_copy(out=skip[b, t], in_=h[b, t][:].indirect(pos2_sb[:]))
+
+        def gather_skips(tag, *slices):
+            picked = slot(tag, [P, len(slices), M], F32)
+            for i, (b, t) in enumerate(slices):
+                skip[b, t] = picked[:, i, :]
+                gather_skip(b, t)
 
         def gate_pass(acc, a, b, t):
             x_codes, x_scales = x_q[a]
@@ -231,7 +242,7 @@ def tile_list_reef_mosaic_skip_kernel(
             nc.sync.dma_start(out=out_rows[b, t], in_=skip[b, t])
 
         def fused_and_store(b, t, gated, parts=1):
-            res = slot(("raw1", "raw4", "raw5", "raw2")[t], [P, M], F32)
+            res = slot(("tab_0", "tab_2", "raw5", "raw0")[t], [P, M], F32)
             w = M // parts
             for part in range(parts):
                 cols = slice(w * part, w * (part + 1))
@@ -248,20 +259,25 @@ def tile_list_reef_mosaic_skip_kernel(
         wb_raw = {}
         for a in range(K_PASSES):
             tab[a] = load_table(a)
-            w1_raw[a, 0] = load_weight(w1, a, 0, "raw%d" % a)
+            if a == 0:
+                for q in range(2, 4):
+                    load_table_scales(nc.sync, q)
+            w1_raw[a, 0] = load_weight(w1, a, 0, ("v_1", "raw1", "raw2")[a])
         w1_raw[0, 1] = load_weight(w1, 0, 1, "raw3")
         nc.sync.dma_start(pos1_sb[:], pos1)
         nc.sync.dma_start(pos2_sb[:], pos2)
+        wa_raw = slot("wa_raw", [P, GROUPS, H // 2], I32)
+        nc.sync.dma_start(out=wa_raw[:], in_=wa_words.bitcast(I32).rearrange("a p c -> p a c"))
         w1_raw[1, 1] = load_weight(w1, 1, 1, "raw4")
         w1_raw[2, 1] = load_weight(w1, 2, 1, "raw5")
 
         v[0] = gather_words(tab[0], 0)
         v_planes = keep.tile([P, S], U8, name="v_planes", align_bytes=64)
         nc.vector.tensor_copy(out=v_planes[:], in_=tab_planes[:].indirect(offs_sb[:]))
-        v[1] = gather_words(tab[1], 1)
         acc = banks()
-        w1_q[0, 0] = quantise(round_on_scalar(w1_raw[0, 0], rounded_tile("r0")), "w1_0_0")
+        w1_q[0, 0] = quantise(round_on_both(w1_raw[0, 0], rounded_tile("r0")), "w1_0_0")
         first_pass(acc, 0, 0)
+        v[1] = gather_words(tab[1], 1)
         w1_q[1, 0] = quantise(round_on_both(w1_raw[1, 0], rounded_tile("r1")), "w1_1_0")
         first_pass(acc, 1, 0)
         v[2] = gather_words(tab[2], 2)
@@ -274,8 +290,6 @@ def tile_list_reef_mosaic_skip_kernel(
         for g in range(GROUPS * GROUPS):
             nc.gpsimd.tensor_copy(out=dst_runs[:, g], in_=src_runs[:, g])
         wb_raw[0, 0] = load_weight(wb, 0, 0, "raw0")
-        wa_raw = slot("tab_0", [P, GROUPS, H // 2], I32)
-        nc.sync.dma_start(out=wa_raw[:], in_=wa_words.bitcast(I32).rearrange("a p c -> p a c"))
         wb_raw[1, 0] = load_weight(wb, 1, 0, "raw1")
         wb_raw[0, 1] = load_weight(wb, 0, 1, "raw2")
         wb_raw[1, 1] = load_weight(wb, 1, 1, "tab_1")
@@ -296,24 +310,23 @@ def tile_list_reef_mosaic_skip_kernel(
         gather_deep(0, 3, deep_group0[:, 3, :])
         w1_q[1, 1] = quantise(r11, "w1_1_1")
         w1_q[2, 1] = quantise(r21, "w1_2_1")
-        for t in range(PACK):
-            first_pass(acc, 1, 1, [t])
-            first_pass(acc, 2, 1, [t])
+        first_pass(acc, 1, 1)
+        first_pass(acc, 2, 1)
         wa = slot("wa", [P, GROUPS * H], U16)
-        nc.vector.tensor_copy(
-            out=wa[:].rearrange("p (g t m) -> p g t m", t=PACK, m=P),
-            in_=wa_raw[:].rearrange("p a c -> p (a c)").bitcast(U16).rearrange("p (g m t) -> p g t m", t=PACK, m=P),
-        )
+        dst_runs = wa[:].bitcast(U8).rearrange("p (g t m e) -> p g t m e", t=PACK, m=P, e=2)
+        src_runs = wa_raw[:].rearrange("p a c -> p (a c)").bitcast(U8).rearrange("p (g m t e) -> p g t m e", t=PACK, m=P, e=2)
+        for g in range(GROUPS * GROUPS):
+            nc.gpsimd.tensor_copy(out=dst_runs[:, g], in_=src_runs[:, g])
 
-        silu0 = slot("silu0", [P, M * PACK], F32)
+        silu0 = slot("raw4", [P, M * PACK], F32)
         nc.scalar.activation(
             out=silu0[:].rearrange("p (c i t) -> p c t i", i=2, t=PACK),
             in_=deep_group0[:].rearrange("p t (c i) -> p c t i", i=2),
             func=ACT.Silu,
         )
 
-        rounded_wb00 = round_on_scalar(wb_raw[0, 0], rounded_tile("deep_group0"))
-        x0 = slot("x0", [P, M * PACK], BF16)
+        rounded_wb00 = round_on_scalar(wb_raw[0, 0], rounded_tile("raw3"))
+        x0 = slot("r2", [P, M * PACK], BF16)
         piece_width = M * PACK // GAIN_PIECES
         for piece in range(GAIN_PIECES):
             cols = slice(piece_width * piece, piece_width * (piece + 1))
@@ -324,10 +337,9 @@ def tile_list_reef_mosaic_skip_kernel(
                 op=ALU.mult,
             )
 
-        both = slot("r2", [P, 2, M], F32)
-        for t in range(2):
-            skip[0, t] = both[:, t, :]
-            gather_skip(0, t)
+        gather_skips("r1", (0, 0), (0, 1), (0, 2))
+        r_b01 = rounded_tile("r0")
+        round_half_on_gpsimd(wb_raw[0, 1], r_b01, 0)
 
         silu1 = slot("silu1", [P, PACK, M], F32)
         for t in range(PACK):
@@ -336,9 +348,9 @@ def tile_list_reef_mosaic_skip_kernel(
             deep = slot("deep%d" % t, [P, M], F32)
             gather_deep(1, t, deep[:])
             nc.scalar.activation(out=silu1[:, t, :], in_=deep[:], func=ACT.Silu)
-        x_q[0] = quantise(x0, "x_0", slot("deep1", [P, KP], U32))
-        wb_q[0, 0] = quantise(rounded_wb00, "wb_0_0", slot("deep2", [P, KP], U32))
-        x1 = ring.tile([P, M * PACK], BF16, name="x1", align_bytes=64)
+        x_q[0] = quantise(x0, "x_0")
+        wb_q[0, 0] = quantise(rounded_wb00, "wb_0_0", slot("raw4", [P, KP], U32))
+        x1 = slot("r2", [P, M * PACK], BF16)
         nc.vector.tensor_tensor(
             out=x1[:].rearrange("p (c i t) -> p c t i", i=2, t=PACK),
             in0=silu1[:].rearrange("p t (c i) -> p c t i", i=2),
@@ -346,8 +358,8 @@ def tile_list_reef_mosaic_skip_kernel(
             op=ALU.mult,
         )
 
+        wb_q[1, 0] = quantise(round_on_scalar(wb_raw[1, 0], rounded_tile("deep0")), "wb_1_0", slot("raw3", [P, KP], U32))
         x_q[1] = quantise(x1, "x_1")
-        wb_q[1, 0] = quantise(round_on_scalar(wb_raw[1, 0], rounded_tile("deep0")), "wb_1_0")
         acc = banks()
         for t in range(PACK):
             value_pass(acc, 0, 0, t)
@@ -355,14 +367,12 @@ def tile_list_reef_mosaic_skip_kernel(
             for a in range(GROUPS):
                 gate_pass(acc, a, 0, t)
             value_pass(acc, 1, 0, t)
-        r_b01 = round_on_scalar(wb_raw[0, 1], rounded_tile("raw3"))
-        r_b11 = round_on_scalar(wb_raw[1, 1], rounded_tile("r1"))
-        skip[0, 2] = slot("x1", [P, M], F32)[:]
-        gather_skip(0, 2)
-        wb_q[0, 1] = quantise(r_b01, "wb_0_1", slot("h_0_2", [P, KP], U32))
-        skip[0, 3] = slot("raw3", [P, M], F32)[:]
-        gather_skip(0, 3)
-        wb_q[1, 1] = quantise(r_b11, "wb_1_1", slot("h_0_3", [P, KP], U32))
+        round_half_on_scalar(wb_raw[0, 1], r_b01, 1)
+        r_b11 = round_on_scalar(wb_raw[1, 1], rounded_tile("raw1"))
+        gather_skips("deep0", (0, 3))
+        wb_q[0, 1] = quantise(r_b01, "wb_0_1", slot("r2", [P, KP], U32))
+        gather_skips("h_0_3", (1, 0))
+        wb_q[1, 1] = quantise(r_b11, "wb_1_1", slot("r0", [P, KP], U32))
         gated = {}
         for t in range(PACK):
             gated[t] = gated_value(t, acc, tanh_of(0, t, acc, slot("tanh_%d" % t, [P, M], F32)))
@@ -373,10 +383,8 @@ def tile_list_reef_mosaic_skip_kernel(
                 gate_pass(acc, a, 1, t)
             for a in range(GROUPS):
                 value_pass(acc, a, 1, t)
-        skip[1, 0] = slot("tanh_3", [P, M], F32)[:]
-        gather_skip(1, 0)
         for t in range(PACK):
-            gated[t] = gated_value(t, acc, tanh_of(1, t, acc, slot("tanh_%d" % ((4, 0, 1, 2)[t]), [P, M], F32)))
+            gated[t] = gated_value(t, acc, tanh_of(1, t, acc, slot("tanh_%d" % t, [P, M], F32)))
             if t == 0:
                 add_and_store(nc.gpsimd, 1, t, gated[t])
             if t >= 2:

@@ -25,11 +25,10 @@ QUADRANT = 32
 K_PASSES = K // KP
 GROUPS = H // KP
 HALVES = S // BANK
-ROUNDED_BUFS = 3
-TANH_BUFS = 2
-GATED_BUFS = 6
-GAIN_PIECES = 4
-GPSIMD_SUMS = 5
+KIB = 1024
+ROUND_PIECES = 2
+GAIN_PIECES = 2
+GPSIMD_SUMS = 3
 
 
 def tile_list_reef_mosaic_skip_kernel(
@@ -39,7 +38,8 @@ def tile_list_reef_mosaic_skip_kernel(
     with ExitStack() as ctx:
         keep = ctx.enter_context(tc.tile_pool(name="keep", bufs=1))
         ring = ctx.enter_context(tc.tile_pool(name="ring", bufs=1))
-        psum = ctx.enter_context(tc.psum_pool(name="psum", bufs=8))
+        placed = ctx.enter_context(tc.tile_pool(name="placed", bufs=1))
+        psum = ctx.enter_context(tc.psum_pool(name="psum", bufs=1))
 
         offs_sb = keep.tile([P, S // LIST_ROWS], U16, name="offs_sb")
         pos1_sb = keep.tile([P, M // LIST_ROWS], U16, name="pos1_sb")
@@ -50,104 +50,104 @@ def tile_list_reef_mosaic_skip_kernel(
         vec_half = keep.tile([P, 2, GROUPS, PACK], F32, name="vec_half")
         warm = keep.tile([P, 1], F32, name="warm")
 
-        nc.vector.memset(tab_planes[:].bitcast(I32), 0)
-        nc.vector.memset(wa_planes_raw[:].bitcast(I32), 0)
+        def slot(tag, shape, dtype):
+            return ring.tile(shape, dtype, name=tag, tag=tag, align_bytes=64)
+
+        def place(name, shape, dtype, kib):
+            return placed.tile(shape, dtype, name=name, tag=name, align_bytes=64, offset=kib * KIB)
+
+        def bank(t, half):
+            return psum.tile([P, BANK], F32, name="bank_%d_%d" % (t, half), tag="bank_%d_%d" % (t, half))
+
+        def banks():
+            return {(t, half): bank(t, half) for t in range(PACK) for half in range(HALVES)}
+
         def load_table_scales(queue, q):
             queue.dma_start(
                 out=tab_planes[QUADRANT * q : QUADRANT * q + 4 * K_PASSES, :].bitcast(I32),
                 in_=tab_scales[:, 4 * q : 4 * q + 4, :].bitcast(I32),
             )
 
-        for q in range(2):
-            load_table_scales(nc.scalar, q)
-        for i, vec in enumerate((gain, bg)):
-            nc.scalar.dma_start(out=vec_raw[:, i, :, 0:PACK], in_=vec.rearrange("(b p t) -> p b t", b=GROUPS, t=PACK))
-        for q in range(P // QUADRANT):
-            nc.gpsimd.dma_start(
-                out=wa_planes_raw[QUADRANT * q : QUADRANT * q + 4, :].bitcast(I32).rearrange("r (a c) -> r a c", a=GROUPS),
-                in_=wa_scales[:, 4 * q : 4 * q + 4, :].bitcast(I32).rearrange("a r c -> r a c"),
-            )
-        nc.vector.tensor_scalar(
-            out=vec_half[:], in0=vec_raw[:, :, :, 0:PACK], scalar1=0.5, scalar2=0.0, op0=ALU.mult, op1=ALU.add
-        )
-        nc.scalar.activation(out=warm[:], in_=vec_half[:, 0, 0, 0:1], func=ACT.Silu)
-        half_gain = vec_half[:, 0]
-        half_bg = vec_half[:, 1]
-
-        def slot(tag, shape, dtype):
-            return ring.tile(shape, dtype, name=tag, tag=tag, align_bytes=64)
-
         def load_table(a):
             words = slot("tab_%d" % a, [P, T], I32)
             nc.sync.dma_start(out=words[:], in_=tab_words[a].rearrange("p t i -> p (t i)").bitcast(I32))
             return words
 
-        def load_weight(w, a, b, tag):
-            raw = slot(tag, [P, PACK, KP], F32)
+        def load_weight(w, a, b, raw):
             nc.sync.dma_start(
                 out=raw[:],
                 in_=w[KP * a : KP * (a + 1), KP * b : KP * (b + 1)].rearrange("(p j) c -> p j c", j=PACK),
             )
             return raw
 
-        def rounding_views(raw, rounded):
+        def raw_slot(tag):
+            return slot(tag, [P, PACK, KP], F32)
+
+        def rounded_slot(tag):
+            return slot(tag, [P, KP * PACK], BF16)
+
+        def pair_views(raw, rounded):
             dst = rounded[:].rearrange("p (u v m j) -> p u m j v", u=2, v=2, j=PACK)
             src = raw[:].rearrange("p j (m u v) -> p u m j v", u=2, v=2)
             return dst, src
 
-        def rounded_tile(tag):
-            return slot(tag, [P, KP * PACK], BF16)
-
         def round_on_scalar(raw, rounded):
-            dst, src = rounding_views(raw, rounded)
+            dst, src = pair_views(raw, rounded)
             nc.scalar.copy(out=dst, in_=src)
             return rounded
 
-        def round_on_vector(raw, rounded):
-            dst, src = rounding_views(raw, rounded)
+        def half_views(raw, half, u):
+            dst = half[:].rearrange("p (v m j) -> p m j v", v=2, j=PACK)
+            src = raw[:].rearrange("p j (m u v) -> p u m j v", u=2, v=2)
+            return dst, src[:, u]
+
+        def half_slot(tag):
+            return slot(tag, [P, KP * PACK // 2], BF16)
+
+        def round_half_on_scalar(raw, half, u):
+            dst, src = half_views(raw, half, u)
+            nc.scalar.copy(out=dst, in_=src)
+            return half
+
+        def round_half_on_vector(raw, half, u):
+            dst, src = half_views(raw, half, u)
             nc.vector.tensor_copy(out=dst, in_=src)
+            return half
+
+        def round_on_gpsimd(raw, rounded):
+            dst = rounded[:].rearrange("p (t m j) -> p m t j", t=PACK, j=PACK)
+            src = raw[:].rearrange("p j (m t) -> p m t j", t=PACK)
+            for c in range(ROUND_PIECES):
+                rows = slice(P // ROUND_PIECES * c, P // ROUND_PIECES * (c + 1))
+                nc.gpsimd.tensor_copy(out=dst[:, rows], in_=src[:, rows])
             return rounded
 
-        def round_on_both(raw, rounded):
-            dst, src = rounding_views(raw, rounded)
-            nc.vector.tensor_copy(out=dst[:, 0], in_=src[:, 0])
-            nc.scalar.copy(out=dst[:, 1], in_=src[:, 1])
-            return rounded
-
-        def round_half_on_gpsimd(raw, rounded, u):
-            dst = rounded[:].rearrange("p (u v m j) -> p u m v j", u=2, v=2, j=PACK)
+        def round_half_on_gpsimd(raw, half, u):
+            dst = half[:].rearrange("p (v m j) -> p m v j", v=2, j=PACK)
             src = raw[:].rearrange("p j (m u v) -> p u m v j", u=2, v=2)
-            for c in range(2):
-                cols = slice(P // 2 * c, P // 2 * (c + 1))
-                nc.gpsimd.tensor_copy(out=dst[:, u, cols], in_=src[:, u, cols])
+            nc.gpsimd.tensor_copy(out=dst, in_=src[:, u])
+            return half
 
-        def round_half_on_scalar(raw, rounded, u):
-            dst, src = rounding_views(raw, rounded)
-            nc.scalar.copy(out=dst[:, u], in_=src[:, u])
-
-        def quantise(rounded, name, codes=None, parts=1):
+        def operand(name, codes=None):
             if codes is None:
                 codes = keep.tile([P, KP], U32, name=name + "_codes", align_bytes=64)
             scales = keep.tile([P, KP], U8, name=name + "_scales", align_bytes=64)
-            width = KP // parts
-            for part in range(parts):
-                cols = slice(width * part, width * (part + 1))
-                nc.vector.quantize_mx(
-                    out=codes[:, cols].bitcast(FP8X4),
-                    scales=scales[:, cols],
-                    in_=rounded[:, PACK * width * part : PACK * width * (part + 1)],
-                )
             return codes, scales
+
+        def quantise(rounded, name, codes=None):
+            codes, scales = operand(name, codes)
+            nc.vector.quantize_mx(out=codes[:].bitcast(FP8X4), scales=scales[:], in_=rounded[:])
+            return codes, scales
+
+        def quantise_half(half, target, u):
+            codes, scales = target
+            cols = slice(KP // 2 * u, KP // 2 * (u + 1))
+            nc.vector.quantize_mx(out=codes[:, cols].bitcast(FP8X4), scales=scales[:, cols], in_=half[:])
 
         def gather_words(words, a):
             picked = slot("v_%d" % a, [P, S], U32)
-            halves = []
-            for half in range(HALVES):
-                entries = offs_sb[:, BANK // LIST_ROWS * half : BANK // LIST_ROWS * (half + 1)]
-                halves.append(picked[:, BANK * half : BANK * (half + 1)])
-                nc.vector.tensor_copy(out=halves[half], in_=words[:].bitcast(U32).indirect(entries))
-            return halves
-
+            nc.vector.tensor_copy(out=picked[:], in_=words[:].bitcast(U32).indirect(offs_sb[:]))
+            return picked
 
         h = {}
         skip = {}
@@ -157,44 +157,36 @@ def tile_list_reef_mosaic_skip_kernel(
         x_q = {}
         out_rows = out.rearrange("(b p t) m -> b t p m", b=GROUPS, t=PACK)
 
-        def banks():
-            acc = {}
-            for t in range(PACK):
-                for half in range(HALVES):
-                    acc[t, half] = psum.tile([P, BANK], F32, name="acc")
-            return acc
-
-        def first_pass(acc, a, b, slices=range(PACK)):
+        def first_pass(acc, a, b, t):
             codes, scales = w1_q[a, b]
-            for t in slices:
-                cols = slice(P * t, P * (t + 1))
-                for half in range(HALVES):
-                    nc.tensor.matmul_mx(
-                        out=acc[t, half][:],
-                        lhsT=codes[:, cols].bitcast(FP8X4),
-                        lhsT_scale=scales[:, cols],
-                        rhs=v[a][half].bitcast(FP8X4),
-                        rhs_scale=v_planes[4 * a : P, BANK * half : BANK * (half + 1)],
-                        start=(a == 0),
-                        stop=(a == K_PASSES - 1),
-                    )
+            cols = slice(P * t, P * (t + 1))
+            for half in range(HALVES):
+                entries = slice(BANK * half, BANK * (half + 1))
+                nc.tensor.matmul_mx(
+                    out=acc[t, half][:],
+                    lhsT=codes[:, cols].bitcast(FP8X4),
+                    lhsT_scale=scales[:, cols],
+                    rhs=v[a][:, entries].bitcast(FP8X4),
+                    rhs_scale=v_planes[4 * a : P, entries],
+                    start=(a == 0),
+                    stop=(a == K_PASSES - 1),
+                )
 
-        def leave_psum(b, acc, t, engines=(None, None)):
+        def first_passes(acc, a, b):
+            for t in range(PACK):
+                first_pass(acc, a, b, t)
+
+        def leave_psum(b, acc, t):
             h[b, t] = slot("h_%d_%d" % (b, t), [P, S], F32)
             for half in range(HALVES):
-                if engines[half] is None:
-                    nc.scalar.copy(out=h[b, t][:, BANK * half : BANK * (half + 1)], in_=acc[t, half][:])
-                else:
-                    nc.vector.tensor_copy(out=h[b, t][:, BANK * half : BANK * (half + 1)], in_=acc[t, half][:])
+                nc.scalar.copy(out=h[b, t][:, BANK * half : BANK * (half + 1)], in_=acc[t, half][:])
 
-        def gather_skip(b, t):
-            nc.vector.tensor_copy(out=skip[b, t], in_=h[b, t][:].indirect(pos2_sb[:]))
+        def gather_deep(b, t, deep):
+            nc.vector.tensor_copy(out=deep, in_=h[b, t][:].indirect(pos1_sb[:]))
 
-        def gather_skips(tag, *slices):
-            picked = slot(tag, [P, len(slices), M], F32)
-            for i, (b, t) in enumerate(slices):
-                skip[b, t] = picked[:, i, :]
-                gather_skip(b, t)
+        def gather_skip(b, t, picked):
+            skip[b, t] = picked
+            nc.vector.tensor_copy(out=picked, in_=h[b, t][:].indirect(pos2_sb[:]))
 
         def gate_pass(acc, a, b, t):
             x_codes, x_scales = x_q[a]
@@ -204,7 +196,7 @@ def tile_list_reef_mosaic_skip_kernel(
                 out=acc[t, 0][:],
                 lhsT=wb_codes[:, cols].bitcast(FP8X4),
                 lhsT_scale=wb_scales[:, cols],
-                rhs=x_codes[:, 0:KP].bitcast(FP8X4),
+                rhs=x_codes[:].bitcast(FP8X4),
                 rhs_scale=x_scales[:],
                 start=(a == 0),
                 stop=(a == GROUPS - 1),
@@ -217,32 +209,23 @@ def tile_list_reef_mosaic_skip_kernel(
                 out=acc[t, 1][:],
                 lhsT=wa[:, wa_cols].bitcast(FP4X4),
                 lhsT_scale=wa_planes[:, wa_cols],
-                rhs=x_codes[:, 0:KP].bitcast(FP8X4),
+                rhs=x_codes[:].bitcast(FP8X4),
                 rhs_scale=x_scales[:],
                 start=(a == 0),
                 stop=(a == GROUPS - 1),
             )
 
-        def second_pass(acc, a, b):
-            for t in range(PACK):
-                gate_pass(acc, a, b, t)
-                value_pass(acc, a, b, t)
-
-        def tanh_of(b, t, acc, tanh):
+        def gated_value(b, t, acc, gated):
+            tanh = slot("tanh_%d" % t, [P, M], F32)
             nc.scalar.activation(out=tanh[:], in_=acc[t, 0][:], func=ACT.Tanh, bias=half_bg[:, b, t : t + 1])
-            return tanh
-
-        def gated_value(t, acc, tanh):
-            gated = ring.tile([P, M], F32, name="gated", bufs=GATED_BUFS)
-            nc.vector.scalar_tensor_tensor(out=gated[:], in0=tanh[:], scalar=1.0, in1=acc[t, 1][:], op0=ALU.add, op1=ALU.mult)
+            nc.vector.scalar_tensor_tensor(out=gated, in0=tanh[:], scalar=1.0, in1=acc[t, 1][:], op0=ALU.add, op1=ALU.mult)
             return gated
 
-        def add_and_store(engine, b, t, gated):
-            engine.tensor_tensor(out=skip[b, t], in0=skip[b, t], in1=gated[:], op=ALU.add)
-            nc.sync.dma_start(out=out_rows[b, t], in_=skip[b, t])
+        def add_and_store(engine, b, t, gated, res):
+            engine.tensor_tensor(out=res, in0=skip[b, t], in1=gated, op=ALU.add)
+            nc.sync.dma_start(out=out_rows[b, t], in_=res)
 
-        def fused_and_store(b, t, gated, parts=1):
-            res = slot(("tab_0", "tab_2", "raw5", "raw0")[t], [P, M], F32)
+        def fused_and_store(b, t, gated, res, parts=1):
             w = M // parts
             for part in range(parts):
                 cols = slice(w * part, w * (part + 1))
@@ -250,8 +233,23 @@ def tile_list_reef_mosaic_skip_kernel(
                 nc.vector.tensor_tensor(out=res[:, cols], in0=h[b, t][:].indirect(entries), in1=gated[:, cols], op=ALU.add)
                 nc.scalar.dma_start(out=out_rows[b, t][:, cols], in_=res[:, cols])
 
-        def gather_deep(b, t, deep):
-            nc.vector.tensor_copy(out=deep, in_=h[b, t][:].indirect(pos1_sb[:]))
+        nc.vector.memset(tab_planes[:].bitcast(I32), 0)
+        nc.gpsimd.memset(wa_planes_raw[:].bitcast(I32), 0)
+        for q in range(2):
+            load_table_scales(nc.scalar, q)
+        for i, vec in enumerate((gain, bg)):
+            nc.scalar.dma_start(out=vec_raw[:, i, :, 0:PACK], in_=vec.rearrange("(b p t) -> p b t", b=GROUPS, t=PACK))
+        for q in range(P // QUADRANT):
+            nc.gpsimd.dma_start(
+                out=wa_planes_raw[QUADRANT * q : QUADRANT * q + 4, :].bitcast(I32).rearrange("r (a c) -> r a c", a=GROUPS),
+                in_=wa_scales[:, 4 * q : 4 * q + 4, :].bitcast(I32).rearrange("a r c -> r a c"),
+            )
+        nc.gpsimd.tensor_scalar(
+            out=vec_half[:], in0=vec_raw[:, :, :, 0:PACK], scalar1=0.5, scalar2=0.0, op0=ALU.mult, op1=ALU.add
+        )
+        nc.scalar.activation(out=warm[:], in_=vec_raw[:, 0, 0, 0:1], func=ACT.Silu)
+        half_gain = vec_half[:, 0]
+        half_bg = vec_half[:, 1]
 
         nc.sync.dma_start(offs_sb[:], offs)
         tab = {}
@@ -262,71 +260,82 @@ def tile_list_reef_mosaic_skip_kernel(
             if a == 0:
                 for q in range(2, 4):
                     load_table_scales(nc.sync, q)
-            w1_raw[a, 0] = load_weight(w1, a, 0, ("v_1", "raw1", "raw2")[a])
-        w1_raw[0, 1] = load_weight(w1, 0, 1, "raw3")
+            w1_raw[a, 0] = load_weight(w1, a, 0, raw_slot("raw_%d0" % a))
         nc.sync.dma_start(pos1_sb[:], pos1)
         nc.sync.dma_start(pos2_sb[:], pos2)
         wa_raw = slot("wa_raw", [P, GROUPS, H // 2], I32)
         nc.sync.dma_start(out=wa_raw[:], in_=wa_words.bitcast(I32).rearrange("a p c -> p a c"))
-        w1_raw[1, 1] = load_weight(w1, 1, 1, "raw4")
-        w1_raw[2, 1] = load_weight(w1, 2, 1, "raw5")
-
-        v[0] = gather_words(tab[0], 0)
-        v_planes = keep.tile([P, S], U8, name="v_planes", align_bytes=64)
-        nc.vector.tensor_copy(out=v_planes[:], in_=tab_planes[:].indirect(offs_sb[:]))
-        acc = banks()
-        w1_q[0, 0] = quantise(round_on_both(w1_raw[0, 0], rounded_tile("r0")), "w1_0_0")
-        first_pass(acc, 0, 0)
-        v[1] = gather_words(tab[1], 1)
-        w1_q[1, 0] = quantise(round_on_both(w1_raw[1, 0], rounded_tile("r1")), "w1_1_0")
-        first_pass(acc, 1, 0)
-        v[2] = gather_words(tab[2], 2)
-        w1_q[2, 0] = quantise(round_on_both(w1_raw[2, 0], rounded_tile("r2")), "w1_2_0", parts=2)
-        first_pass(acc, 2, 0)
+        w1_raw[0, 1] = load_weight(w1, 0, 1, raw_slot("raw_01"))
+        w1_raw[1, 1] = load_weight(w1, 1, 1, place("raw_11", [P, PACK, KP], F32, 0))
+        w1_raw[2, 1] = load_weight(w1, 2, 1, place("raw_21", [P, PACK, KP], F32, 8))
 
         wa_planes = keep.tile([P, GROUPS * H], U8, name="wa_planes", align_bytes=64)
         dst_runs = wa_planes[:].rearrange("p (g t m) -> p g t m", t=PACK, m=P)
         src_runs = wa_planes_raw[:].rearrange("p (g m t) -> p g t m", t=PACK, m=P)
         for g in range(GROUPS * GROUPS):
             nc.gpsimd.tensor_copy(out=dst_runs[:, g], in_=src_runs[:, g])
-        wb_raw[0, 0] = load_weight(wb, 0, 0, "raw0")
-        wb_raw[1, 0] = load_weight(wb, 1, 0, "raw1")
-        wb_raw[0, 1] = load_weight(wb, 0, 1, "raw2")
-        wb_raw[1, 1] = load_weight(wb, 1, 1, "tab_1")
 
-        leave_psum(0, acc, 0)
-        r01 = round_on_vector(w1_raw[0, 1], rounded_tile("r0"))
-        for t in range(1, PACK):
-            leave_psum(0, acc, t)
-        deep_group0 = slot("deep_group0", [P, PACK, M], F32)
-        gather_deep(0, 0, deep_group0[:, 0, :])
-        w1_q[0, 1] = quantise(r01, "w1_0_1")
         acc = banks()
-        first_pass(acc, 0, 1)
-        r11 = round_on_scalar(w1_raw[1, 1], rounded_tile("r1"))
-        gather_deep(0, 1, deep_group0[:, 1, :])
-        gather_deep(0, 2, deep_group0[:, 2, :])
-        r21 = round_on_vector(w1_raw[2, 1], rounded_tile("r2"))
-        gather_deep(0, 3, deep_group0[:, 3, :])
-        w1_q[1, 1] = quantise(r11, "w1_1_1")
-        w1_q[2, 1] = quantise(r21, "w1_2_1")
-        first_pass(acc, 1, 1)
-        first_pass(acc, 2, 1)
-        wa = slot("wa", [P, GROUPS * H], U16)
-        dst_runs = wa[:].bitcast(U8).rearrange("p (g t m e) -> p g t m e", t=PACK, m=P, e=2)
-        src_runs = wa_raw[:].rearrange("p a c -> p (a c)").bitcast(U8).rearrange("p (g m t e) -> p g t m e", t=PACK, m=P, e=2)
-        for g in range(GROUPS * GROUPS):
-            nc.gpsimd.tensor_copy(out=dst_runs[:, g], in_=src_runs[:, g])
+        v[0] = gather_words(tab[0], 0)
+        v_planes = keep.tile([P, S], U8, name="v_planes", align_bytes=64)
+        nc.vector.tensor_copy(out=v_planes[:], in_=tab_planes[:].indirect(offs_sb[:]))
+        w1_q[0, 0] = quantise(round_on_scalar(w1_raw[0, 0], rounded_slot("r0")), "w1_0_0")
+        first_passes(acc, 0, 0)
+        for a in range(1, K_PASSES):
+            v[a] = gather_words(tab[a], a)
+            low = round_half_on_vector(w1_raw[a, 0], half_slot("half_a"), 0)
+            high = round_half_on_scalar(w1_raw[a, 0], half_slot("half_b"), 1)
+            w1_q[a, 0] = operand("w1_%d_0" % a)
+            quantise_half(low, w1_q[a, 0], 0)
+            quantise_half(high, w1_q[a, 0], 1)
+            first_passes(acc, a, 0)
+        wb_raw[0, 0] = load_weight(wb, 0, 0, raw_slot("tab_0"))
+        wb_raw[1, 0] = load_weight(wb, 1, 0, raw_slot("tab_1"))
+        wb_raw[0, 1] = load_weight(wb, 0, 1, raw_slot("tab_2"))
+        wb_raw[1, 1] = load_weight(wb, 1, 1, raw_slot("raw_00"))
 
-        silu0 = slot("raw4", [P, M * PACK], F32)
-        nc.scalar.activation(
-            out=silu0[:].rearrange("p (c i t) -> p c t i", i=2, t=PACK),
-            in_=deep_group0[:].rearrange("p t (c i) -> p c t i", i=2),
-            func=ACT.Silu,
+        wa = slot("wa", [P, GROUPS * H], U16)
+        nc.vector.tensor_copy(
+            out=wa[:].rearrange("p (g t l m) -> p g l t m", t=PACK, l=P // 8, m=8),
+            in_=wa_raw[:].rearrange("p a c -> p (a c)").bitcast(U16).rearrange("p (g l m t) -> p g l t m", t=PACK, l=P // 8, m=8),
         )
 
-        rounded_wb00 = round_on_scalar(wb_raw[0, 0], rounded_tile("raw3"))
-        x0 = slot("r2", [P, M * PACK], BF16)
+        for t in range(PACK):
+            leave_psum(0, acc, t)
+        r01 = round_on_gpsimd(w1_raw[0, 1], rounded_slot("r0"))
+        deep0 = slot("wa_raw", [P, PACK, M], F32)
+        for t in range(PACK):
+            gather_deep(0, t, deep0[:, t, :])
+        w1_q[0, 1] = quantise(r01, "w1_0_1")
+
+        acc = banks()
+        first_passes(acc, 0, 1)
+        low = round_half_on_scalar(w1_raw[1, 1], half_slot("half_b"), 0)
+        high = round_half_on_gpsimd(w1_raw[1, 1], half_slot("r0"), 1)
+        r21 = round_on_scalar(w1_raw[2, 1], rounded_slot("r2"))
+        w1_q[1, 1] = operand("w1_1_1")
+        quantise_half(low, w1_q[1, 1], 0)
+        early = slot("raw_01", [P, 2 * M], F32)
+        for t in range(2):
+            gather_skip(0, t, early[:, M * t : M * (t + 1)])
+        quantise_half(high, w1_q[1, 1], 1)
+        w1_q[2, 1] = quantise(r21, "w1_2_1", place("w1_21_codes", [P, KP], U32, 0))
+        for t in range(PACK):
+            first_pass(acc, 1, 1, t)
+            first_pass(acc, 2, 1, t)
+        silu0 = place("silu0", [P, M * PACK], F32, 11)
+        nc.scalar.activation(
+            out=silu0[:].rearrange("p (c i t) -> p c t i", i=2, t=PACK),
+            in_=deep0[:].rearrange("p t (c i) -> p c t i", i=2),
+            func=ACT.Silu,
+        )
+        high = round_half_on_vector(wb_raw[0, 0], place("wb_00_high", [P, KP * PACK // 2], BF16, 9), 1)
+        later = place("later", [P, 2 * M], F32, 5)
+        for t in range(2):
+            gather_skip(0, 2 + t, later[:, M * t : M * (t + 1)])
+
+        low = round_half_on_gpsimd(wb_raw[0, 0], half_slot("r2"), 0)
+        x0 = rounded_slot("x")
         piece_width = M * PACK // GAIN_PIECES
         for piece in range(GAIN_PIECES):
             cols = slice(piece_width * piece, piece_width * (piece + 1))
@@ -337,46 +346,52 @@ def tile_list_reef_mosaic_skip_kernel(
                 op=ALU.mult,
             )
 
-        gather_skips("r1", (0, 0), (0, 1), (0, 2))
-        r_b01 = rounded_tile("r0")
-        round_half_on_gpsimd(wb_raw[0, 1], r_b01, 0)
-
-        silu1 = slot("silu1", [P, PACK, M], F32)
         for t in range(PACK):
             leave_psum(1, acc, t)
+        silu1 = slot("v_2", [P, PACK, M], F32)
         for t in range(PACK):
-            deep = slot("deep%d" % t, [P, M], F32)
+            deep = slot("deep_%d" % t, [P, M], F32)
             gather_deep(1, t, deep[:])
             nc.scalar.activation(out=silu1[:, t, :], in_=deep[:], func=ACT.Silu)
-        x_q[0] = quantise(x0, "x_0")
-        wb_q[0, 0] = quantise(rounded_wb00, "wb_0_0", slot("raw4", [P, KP], U32))
-        x1 = slot("r2", [P, M * PACK], BF16)
+        x_q[0] = quantise(x0, "x_0", slot("deep_1", [P, KP], U32))
+        wb_q[0, 0] = operand("wb_0_0", place("wb_00_codes", [P, KP], U32, 14))
+        quantise_half(low, wb_q[0, 0], 0)
+        quantise_half(high, wb_q[0, 0], 1)
+        x1 = rounded_slot("x")
         nc.vector.tensor_tensor(
             out=x1[:].rearrange("p (c i t) -> p c t i", i=2, t=PACK),
             in0=silu1[:].rearrange("p t (c i) -> p c t i", i=2),
             in1=half_gain[:, 1, :].unsqueeze(1).unsqueeze(3).to_broadcast([P, M // 2, PACK, 2]),
             op=ALU.mult,
         )
-
-        wb_q[1, 0] = quantise(round_on_scalar(wb_raw[1, 0], rounded_tile("deep0")), "wb_1_0", slot("raw3", [P, KP], U32))
+        wb_q[1, 0] = quantise(round_on_scalar(wb_raw[1, 0], rounded_slot("deep_2")), "wb_1_0", place("wb_10_codes", [P, KP], U32, 16))
         x_q[1] = quantise(x1, "x_1")
+        r_b01 = round_on_scalar(wb_raw[0, 1], rounded_slot("deep_3"))
+        low = round_half_on_scalar(wb_raw[1, 1], half_slot("tab_1"), 0)
+        high = round_half_on_gpsimd(wb_raw[1, 1], half_slot("x"), 1)
+
         acc = banks()
         for t in range(PACK):
             value_pass(acc, 0, 0, t)
+            gate_pass(acc, 0, 0, t)
         for t in range(PACK):
-            for a in range(GROUPS):
-                gate_pass(acc, a, 0, t)
+            gate_pass(acc, 1, 0, t)
             value_pass(acc, 1, 0, t)
-        round_half_on_scalar(wb_raw[0, 1], r_b01, 1)
-        r_b11 = round_on_scalar(wb_raw[1, 1], rounded_tile("raw1"))
-        gather_skips("deep0", (0, 3))
-        wb_q[0, 1] = quantise(r_b01, "wb_0_1", slot("r2", [P, KP], U32))
-        gather_skips("h_0_3", (1, 0))
-        wb_q[1, 1] = quantise(r_b11, "wb_1_1", slot("r0", [P, KP], U32))
+        last = slot("v_2", [P, 2 * M], F32)
+        for t in range(2):
+            gather_skip(1, t, last[:, M * t : M * (t + 1)])
+        wb_q[0, 1] = quantise(r_b01, "wb_0_1", slot("raw_00", [P, KP], U32))
+        wb_q[1, 1] = operand("wb_1_1")
+        quantise_half(low, wb_q[1, 1], 0)
+        quantise_half(high, wb_q[1, 1], 1)
         gated = {}
+        first = slot("deep_3", [P, GPSIMD_SUMS * M], F32)
         for t in range(PACK):
-            gated[t] = gated_value(t, acc, tanh_of(0, t, acc, slot("tanh_%d" % t, [P, M], F32)))
-            add_and_store(nc.gpsimd, 0, t, gated[t])
+            if t < GPSIMD_SUMS:
+                gated[0, t] = gated_value(0, t, acc, first[:, M * t : M * (t + 1)])
+                add_and_store(nc.gpsimd, 0, t, gated[0, t], skip[0, t])
+            else:
+                gated[0, t] = gated_value(0, t, acc, slot("x", [P, M], F32)[:])
         acc = banks()
         for t in range(PACK):
             for a in range(GROUPS):
@@ -384,9 +399,9 @@ def tile_list_reef_mosaic_skip_kernel(
             for a in range(GROUPS):
                 value_pass(acc, a, 1, t)
         for t in range(PACK):
-            gated[t] = gated_value(t, acc, tanh_of(1, t, acc, slot("tanh_%d" % t, [P, M], F32)))
-            if t == 0:
-                add_and_store(nc.gpsimd, 1, t, gated[t])
-            if t >= 2:
-                fused_and_store(1, t - 1, gated[t - 1])
-        fused_and_store(1, 3, gated[3], parts=2)
+            gated[1, t] = gated_value(1, t, acc, slot("gated_%d" % t, [P, M], F32)[:])
+        res = slot("deep_3", [P, 5 * M], F32)
+        for i, (b, t) in enumerate(((0, 3), (1, 0), (1, 1))):
+            add_and_store(nc.vector, b, t, gated[b, t], res[:, M * i : M * (i + 1)])
+        fused_and_store(1, 2, gated[1, 2], res[:, 3 * M : 4 * M])
+        fused_and_store(1, 3, gated[1, 3], res[:, 4 * M : 5 * M], parts=2)

@@ -26,9 +26,7 @@ K_PASSES = K // KP
 GROUPS = H // KP
 HALVES = S // BANK
 KIB = 1024
-ROUND_PIECES = 2
 GAIN_PIECES = 2
-GPSIMD_SUMS = 3
 
 
 def tile_list_reef_mosaic_skip_kernel(
@@ -114,19 +112,10 @@ def tile_list_reef_mosaic_skip_kernel(
             nc.vector.tensor_copy(out=dst, in_=src)
             return half
 
-        def round_on_gpsimd(raw, rounded):
-            dst = rounded[:].rearrange("p (t m j) -> p m t j", t=PACK, j=PACK)
-            src = raw[:].rearrange("p j (m t) -> p m t j", t=PACK)
-            for c in range(ROUND_PIECES):
-                rows = slice(P // ROUND_PIECES * c, P // ROUND_PIECES * (c + 1))
-                nc.gpsimd.tensor_copy(out=dst[:, rows], in_=src[:, rows])
+        def round_on_vector(raw, rounded):
+            dst, src = pair_views(raw, rounded)
+            nc.vector.tensor_copy(out=dst, in_=src)
             return rounded
-
-        def round_half_on_gpsimd(raw, half, u):
-            dst = half[:].rearrange("p (v m j) -> p m v j", v=2, j=PACK)
-            src = raw[:].rearrange("p j (m u v) -> p u m v j", u=2, v=2)
-            nc.gpsimd.tensor_copy(out=dst, in_=src[:, u])
-            return half
 
         def operand(name, codes=None):
             if codes is None:
@@ -155,6 +144,7 @@ def tile_list_reef_mosaic_skip_kernel(
         w1_q = {}
         wb_q = {}
         x_q = {}
+        wa = {}
         out_rows = out.rearrange("(b p t) m -> b t p m", b=GROUPS, t=PACK)
 
         def first_pass(acc, a, b, t):
@@ -176,8 +166,8 @@ def tile_list_reef_mosaic_skip_kernel(
             for t in range(PACK):
                 first_pass(acc, a, b, t)
 
-        def leave_psum(b, acc, t):
-            h[b, t] = slot("h_%d_%d" % (b, t), [P, S], F32)
+        def leave_psum(b, acc, t, tile):
+            h[b, t] = tile
             for half in range(HALVES):
                 nc.scalar.copy(out=h[b, t][:, BANK * half : BANK * (half + 1)], in_=acc[t, half][:])
 
@@ -205,9 +195,10 @@ def tile_list_reef_mosaic_skip_kernel(
         def value_pass(acc, a, b, t):
             x_codes, x_scales = x_q[a]
             wa_cols = slice(H * a + KP * b + P * t, H * a + KP * b + P * (t + 1))
+            word_cols = slice(KP * a + P * t, KP * a + P * (t + 1))
             nc.tensor.matmul_mx(
                 out=acc[t, 1][:],
-                lhsT=wa[:, wa_cols].bitcast(FP4X4),
+                lhsT=wa[b][:, word_cols].bitcast(FP4X4),
                 lhsT_scale=wa_planes[:, wa_cols],
                 rhs=x_codes[:].bitcast(FP8X4),
                 rhs_scale=x_scales[:],
@@ -215,8 +206,16 @@ def tile_list_reef_mosaic_skip_kernel(
                 stop=(a == GROUPS - 1),
             )
 
+        def reorder_wa(b, tile):
+            wa[b] = tile
+            dst = tile[:].bitcast(U8).rearrange("p (a t m e) -> p a t m e", a=GROUPS, t=PACK, e=2)
+            src = wa_raw[:].rearrange("p a c -> p (a c)").bitcast(U8)
+            src = src.rearrange("p (a b m t e) -> p b a t m e", a=GROUPS, b=GROUPS, t=PACK, e=2)
+            for a in range(GROUPS):
+                nc.gpsimd.tensor_copy(out=dst[:, a], in_=src[:, b, a])
+
         def gated_value(b, t, acc, gated):
-            tanh = slot("tanh_%d" % t, [P, M], F32)
+            tanh = slot("tanh_%d_%d" % (b, t), [P, M], F32)
             nc.scalar.activation(out=tanh[:], in_=acc[t, 0][:], func=ACT.Tanh, bias=half_bg[:, b, t : t + 1])
             nc.vector.scalar_tensor_tensor(out=gated, in0=tanh[:], scalar=1.0, in1=acc[t, 1][:], op0=ALU.add, op1=ALU.mult)
             return gated
@@ -261,13 +260,15 @@ def tile_list_reef_mosaic_skip_kernel(
                 for q in range(2, 4):
                     load_table_scales(nc.sync, q)
             w1_raw[a, 0] = load_weight(w1, a, 0, raw_slot("raw_%d0" % a))
+        w1_raw[0, 1] = load_weight(w1, 0, 1, raw_slot("raw_01"))
         nc.sync.dma_start(pos1_sb[:], pos1)
         nc.sync.dma_start(pos2_sb[:], pos2)
-        wa_raw = slot("wa_raw", [P, GROUPS, H // 2], I32)
+        wa_raw = place("wa_raw", [P, GROUPS, H // 2], I32, 24)
         nc.sync.dma_start(out=wa_raw[:], in_=wa_words.bitcast(I32).rearrange("a p c -> p a c"))
-        w1_raw[0, 1] = load_weight(w1, 0, 1, raw_slot("raw_01"))
-        w1_raw[1, 1] = load_weight(w1, 1, 1, place("raw_11", [P, PACK, KP], F32, 0))
-        w1_raw[2, 1] = load_weight(w1, 2, 1, place("raw_21", [P, PACK, KP], F32, 8))
+        w1_raw[1, 1] = load_weight(w1, 1, 1, place("raw_11", [P, PACK, KP], F32, 16))
+        w1_raw[2, 1] = load_weight(w1, 2, 1, raw_slot("raw_21"))
+        wide = place("wb_00_raw", [P, 2 * PACK, KP], F32, 0)
+        wb_raw[0, 0] = load_weight(wb, 0, 0, wide[:, 0:PACK, :])
 
         wa_planes = keep.tile([P, GROUPS * H], U8, name="wa_planes", align_bytes=64)
         dst_runs = wa_planes[:].rearrange("p (g t m) -> p g t m", t=PACK, m=P)
@@ -289,53 +290,44 @@ def tile_list_reef_mosaic_skip_kernel(
             quantise_half(low, w1_q[a, 0], 0)
             quantise_half(high, w1_q[a, 0], 1)
             first_passes(acc, a, 0)
-        wb_raw[0, 0] = load_weight(wb, 0, 0, raw_slot("tab_0"))
-        wb_raw[1, 0] = load_weight(wb, 1, 0, raw_slot("tab_1"))
-        wb_raw[0, 1] = load_weight(wb, 0, 1, raw_slot("tab_2"))
-        wb_raw[1, 1] = load_weight(wb, 1, 1, raw_slot("raw_00"))
+        wb_raw[1, 0] = load_weight(wb, 1, 0, raw_slot("tab_0"))
+        wb_raw[0, 1] = load_weight(wb, 0, 1, raw_slot("tab_1"))
+        wb_raw[1, 1] = load_weight(wb, 1, 1, raw_slot("tab_2"))
 
-        wa = slot("wa", [P, GROUPS * H], U16)
-        nc.vector.tensor_copy(
-            out=wa[:].rearrange("p (g t l m) -> p g l t m", t=PACK, l=P // 8, m=8),
-            in_=wa_raw[:].rearrange("p a c -> p (a c)").bitcast(U16).rearrange("p (g l m t) -> p g l t m", t=PACK, l=P // 8, m=8),
-        )
-
+        r01 = round_on_vector(w1_raw[0, 1], rounded_slot("r0"))
         for t in range(PACK):
-            leave_psum(0, acc, t)
-        r01 = round_on_gpsimd(w1_raw[0, 1], rounded_slot("r0"))
-        deep0 = slot("wa_raw", [P, PACK, M], F32)
-        for t in range(PACK):
+            leave_psum(0, acc, t, slot("h_0_%d" % t, [P, S], F32))
+        deep0 = slot("raw_01", [P, PACK, M], F32)
+        gather_deep(0, 0, deep0[:, 0, :])
+        w1_q[0, 1] = quantise(r01, "w1_0_1", slot("codes_01", [P, KP], U32))
+        reorder_wa(0, slot("r0", [P, H], U16))
+        for t in range(1, PACK):
             gather_deep(0, t, deep0[:, t, :])
-        w1_q[0, 1] = quantise(r01, "w1_0_1")
 
         acc = banks()
         first_passes(acc, 0, 1)
-        low = round_half_on_scalar(w1_raw[1, 1], half_slot("half_b"), 0)
-        high = round_half_on_gpsimd(w1_raw[1, 1], half_slot("r0"), 1)
-        r21 = round_on_scalar(w1_raw[2, 1], rounded_slot("r2"))
-        w1_q[1, 1] = operand("w1_1_1")
-        quantise_half(low, w1_q[1, 1], 0)
-        early = slot("raw_01", [P, 2 * M], F32)
-        for t in range(2):
-            gather_skip(0, t, early[:, M * t : M * (t + 1)])
-        quantise_half(high, w1_q[1, 1], 1)
-        w1_q[2, 1] = quantise(r21, "w1_2_1", place("w1_21_codes", [P, KP], U32, 0))
-        for t in range(PACK):
-            first_pass(acc, 1, 1, t)
-            first_pass(acc, 2, 1, t)
-        silu0 = place("silu0", [P, M * PACK], F32, 11)
+        r11 = round_on_scalar(w1_raw[1, 1], rounded_slot("r1"))
+        silu0 = place("silu0", [P, M * PACK], F32, 16)
         nc.scalar.activation(
             out=silu0[:].rearrange("p (c i t) -> p c t i", i=2, t=PACK),
             in_=deep0[:].rearrange("p t (c i) -> p c t i", i=2),
             func=ACT.Silu,
         )
-        high = round_half_on_vector(wb_raw[0, 0], place("wb_00_high", [P, KP * PACK // 2], BF16, 9), 1)
-        later = place("later", [P, 2 * M], F32, 5)
-        for t in range(2):
-            gather_skip(0, 2 + t, later[:, M * t : M * (t + 1)])
+        r_b00 = round_on_scalar(wb_raw[0, 0], rounded_slot("raw_00"))
+        gather_skip(0, 0, slot("codes_01", [P, M], F32)[:])
+        w1_q[1, 1] = quantise(r11, "w1_1_1")
+        first_passes(acc, 1, 1)
+        low = round_half_on_vector(w1_raw[2, 1], half_slot("half_a"), 0)
+        high = round_half_on_vector(w1_raw[2, 1], half_slot("half_b"), 1)
+        w1_q[2, 1] = operand("w1_2_1", slot("codes_21", [P, KP], U32))
+        quantise_half(low, w1_q[2, 1], 0)
+        quantise_half(high, w1_q[2, 1], 1)
+        first_passes(acc, 2, 1)
+        early = slot("raw_21", [P, 3 * M], F32)
+        for t in range(1, PACK):
+            gather_skip(0, t, early[:, M * (t - 1) : M * t])
 
-        low = round_half_on_gpsimd(wb_raw[0, 0], half_slot("r2"), 0)
-        x0 = rounded_slot("x")
+        x0 = rounded_slot("half_a")
         piece_width = M * PACK // GAIN_PIECES
         for piece in range(GAIN_PIECES):
             cols = slice(piece_width * piece, piece_width * (piece + 1))
@@ -345,30 +337,32 @@ def tile_list_reef_mosaic_skip_kernel(
                 in1=half_gain[:, 0, :].unsqueeze(1).to_broadcast([P, piece_width // PACK, PACK]),
                 op=ALU.mult,
             )
+        reorder_wa(1, slot("half_b", [P, H], U16))
 
         for t in range(PACK):
-            leave_psum(1, acc, t)
+            leave_psum(1, acc, t, place("h_1_%d" % t, [P, S], F32, 4 * t))
+        low = round_half_on_scalar(wb_raw[1, 0], half_slot("codes_21"), 0)
         silu1 = slot("v_2", [P, PACK, M], F32)
         for t in range(PACK):
-            deep = slot("deep_%d" % t, [P, M], F32)
+            deep = place("deep_1", [P, M], F32, 28) if t == 1 else slot("deep_%d" % t, [P, M], F32)
             gather_deep(1, t, deep[:])
             nc.scalar.activation(out=silu1[:, t, :], in_=deep[:], func=ACT.Silu)
-        x_q[0] = quantise(x0, "x_0", slot("deep_1", [P, KP], U32))
-        wb_q[0, 0] = operand("wb_0_0", place("wb_00_codes", [P, KP], U32, 14))
-        quantise_half(low, wb_q[0, 0], 0)
-        quantise_half(high, wb_q[0, 0], 1)
-        x1 = rounded_slot("x")
+        high = round_half_on_scalar(wb_raw[1, 0], half_slot("deep_2"), 1)
+        r_b01 = round_on_scalar(wb_raw[0, 1], rounded_slot("deep_3"))
+        codes = place("codes", [P, 3 * KP], U32, 24)
+        x_q[0] = quantise(x0, "x_0", codes[:, 0:KP])
+        wb_q[0, 0] = quantise(r_b00, "wb_0_0", codes[:, KP : 2 * KP])
+        x1 = rounded_slot("half_a")
         nc.vector.tensor_tensor(
             out=x1[:].rearrange("p (c i t) -> p c t i", i=2, t=PACK),
             in0=silu1[:].rearrange("p t (c i) -> p c t i", i=2),
             in1=half_gain[:, 1, :].unsqueeze(1).unsqueeze(3).to_broadcast([P, M // 2, PACK, 2]),
             op=ALU.mult,
         )
-        wb_q[1, 0] = quantise(round_on_scalar(wb_raw[1, 0], rounded_slot("deep_2")), "wb_1_0", place("wb_10_codes", [P, KP], U32, 16))
+        wb_q[1, 0] = operand("wb_1_0", codes[:, 2 * KP : 3 * KP])
+        quantise_half(low, wb_q[1, 0], 0)
+        quantise_half(high, wb_q[1, 0], 1)
         x_q[1] = quantise(x1, "x_1")
-        r_b01 = round_on_scalar(wb_raw[0, 1], rounded_slot("deep_3"))
-        low = round_half_on_scalar(wb_raw[1, 1], half_slot("tab_1"), 0)
-        high = round_half_on_gpsimd(wb_raw[1, 1], half_slot("x"), 1)
 
         acc = banks()
         for t in range(PACK):
@@ -377,21 +371,20 @@ def tile_list_reef_mosaic_skip_kernel(
         for t in range(PACK):
             gate_pass(acc, 1, 0, t)
             value_pass(acc, 1, 0, t)
-        last = slot("v_2", [P, 2 * M], F32)
-        for t in range(2):
-            gather_skip(1, t, last[:, M * t : M * (t + 1)])
-        wb_q[0, 1] = quantise(r_b01, "wb_0_1", slot("raw_00", [P, KP], U32))
+        low = round_half_on_scalar(wb_raw[1, 1], half_slot("tab_0"), 0)
+        high = round_half_on_vector(wb_raw[1, 1], half_slot("v_2"), 1)
+        wb_q[0, 1] = quantise(r_b01, "wb_0_1")
         wb_q[1, 1] = operand("wb_1_1")
         quantise_half(low, wb_q[1, 1], 0)
         quantise_half(high, wb_q[1, 1], 1)
         gated = {}
-        first = slot("deep_3", [P, GPSIMD_SUMS * M], F32)
+        first = slot("tab_0", [P, PACK * M], F32)
         for t in range(PACK):
-            if t < GPSIMD_SUMS:
-                gated[0, t] = gated_value(0, t, acc, first[:, M * t : M * (t + 1)])
-                add_and_store(nc.gpsimd, 0, t, gated[0, t], skip[0, t])
-            else:
-                gated[0, t] = gated_value(0, t, acc, slot("x", [P, M], F32)[:])
+            gated[0, t] = gated_value(0, t, acc, first[:, M * t : M * (t + 1)])
+            add_and_store(nc.gpsimd, 0, t, gated[0, t], skip[0, t])
+        last = slot("tanh_0_2", [P, 2 * M], F32)
+        for t in range(2):
+            gather_skip(1, t, last[:, M * t : M * (t + 1)])
         acc = banks()
         for t in range(PACK):
             for a in range(GROUPS):
@@ -399,9 +392,9 @@ def tile_list_reef_mosaic_skip_kernel(
             for a in range(GROUPS):
                 value_pass(acc, a, 1, t)
         for t in range(PACK):
-            gated[1, t] = gated_value(1, t, acc, slot("gated_%d" % t, [P, M], F32)[:])
-        res = slot("deep_3", [P, 5 * M], F32)
-        for i, (b, t) in enumerate(((0, 3), (1, 0), (1, 1))):
-            add_and_store(nc.vector, b, t, gated[b, t], res[:, M * i : M * (i + 1)])
-        fused_and_store(1, 2, gated[1, 2], res[:, 3 * M : 4 * M])
-        fused_and_store(1, 3, gated[1, 3], res[:, 4 * M : 5 * M], parts=2)
+            gated[1, t] = gated_value(1, t, acc, slot("deep_%d" % (0, 2, 3, 0)[t] if t < 3 else "raw_10", [P, M], F32)[:])
+        res = slot("tab_0", [P, PACK * M], F32)
+        for t in range(2):
+            add_and_store(nc.vector, 1, t, gated[1, t], res[:, M * t : M * (t + 1)])
+        fused_and_store(1, 2, gated[1, 2], res[:, 2 * M : 3 * M])
+        fused_and_store(1, 3, gated[1, 3], res[:, 3 * M : 4 * M], parts=2)

@@ -117,6 +117,13 @@ def tile_list_reef_mosaic_skip_kernel(
             nc.vector.tensor_copy(out=dst, in_=src)
             return rounded
 
+        def round_half_on_gpsimd(raw, half, u):
+            dst = half[:].rearrange("p (v m j) -> p v m j", v=2, j=PACK)
+            src = raw[:].rearrange("p j (m u v) -> p u v m j", u=2, v=2)
+            for v in range(2):
+                nc.gpsimd.tensor_copy(out=dst[:, v], in_=src[:, u, v])
+            return half
+
         def operand(name, codes=None):
             if codes is None:
                 codes = keep.tile([P, KP], U32, name=name + "_codes", align_bytes=64)
@@ -220,15 +227,19 @@ def tile_list_reef_mosaic_skip_kernel(
             nc.vector.scalar_tensor_tensor(out=gated, in0=tanh[:], scalar=1.0, in1=acc[t, 1][:], op0=ALU.add, op1=ALU.mult)
             return gated
 
-        def add_and_store(engine, b, t, gated, res):
-            engine.tensor_tensor(out=res, in0=skip[b, t], in1=gated, op=ALU.add)
-            nc.sync.dma_start(out=out_rows[b, t], in_=res)
-
-        def fused_and_store(b, t, gated, res, parts=1):
-            w = M // parts
+        def add_and_store(engine, b, t, gated, res, parts=1):
+            width = M // parts
             for part in range(parts):
-                cols = slice(w * part, w * (part + 1))
-                entries = pos2_sb[:, w // LIST_ROWS * part : w // LIST_ROWS * (part + 1)]
+                cols = slice(width * part, width * (part + 1))
+                engine.tensor_tensor(out=res[:, cols], in0=skip[b, t][:, cols], in1=gated[:, cols], op=ALU.add)
+                nc.sync.dma_start(out=out_rows[b, t][:, cols], in_=res[:, cols])
+
+        def fused_and_store(b, t, gated, parts=1):
+            res = slot("res_%d" % t, [P, M], F32)
+            width = M // parts
+            for part in range(parts):
+                cols = slice(width * part, width * (part + 1))
+                entries = pos2_sb[:, width // LIST_ROWS * part : width // LIST_ROWS * (part + 1)]
                 nc.vector.tensor_tensor(out=res[:, cols], in0=h[b, t][:].indirect(entries), in1=gated[:, cols], op=ALU.add)
                 nc.scalar.dma_start(out=out_rows[b, t][:, cols], in_=res[:, cols])
 
@@ -263,7 +274,7 @@ def tile_list_reef_mosaic_skip_kernel(
         w1_raw[0, 1] = load_weight(w1, 0, 1, raw_slot("raw_01"))
         nc.sync.dma_start(pos1_sb[:], pos1)
         nc.sync.dma_start(pos2_sb[:], pos2)
-        wa_raw = place("wa_raw", [P, GROUPS, H // 2], I32, 24)
+        wa_raw = slot("wa_raw", [P, GROUPS, H // 2], I32)
         nc.sync.dma_start(out=wa_raw[:], in_=wa_words.bitcast(I32).rearrange("a p c -> p a c"))
         w1_raw[1, 1] = load_weight(w1, 1, 1, place("raw_11", [P, PACK, KP], F32, 16))
         w1_raw[2, 1] = load_weight(w1, 2, 1, raw_slot("raw_21"))
@@ -297,10 +308,11 @@ def tile_list_reef_mosaic_skip_kernel(
         r01 = round_on_vector(w1_raw[0, 1], rounded_slot("r0"))
         for t in range(PACK):
             leave_psum(0, acc, t, slot("h_0_%d" % t, [P, S], F32))
-        deep0 = slot("raw_01", [P, PACK, M], F32)
+        deep0 = slot("raw_10", [P, PACK, M], F32)
         gather_deep(0, 0, deep0[:, 0, :])
-        w1_q[0, 1] = quantise(r01, "w1_0_1", slot("codes_01", [P, KP], U32))
-        reorder_wa(0, slot("r0", [P, H], U16))
+        w1_q[0, 1] = quantise(r01, "w1_0_1")
+        for b in range(GROUPS):
+            reorder_wa(b, slot("wa_%d" % b, [P, H], U16))
         for t in range(1, PACK):
             gather_deep(0, t, deep0[:, t, :])
 
@@ -314,7 +326,6 @@ def tile_list_reef_mosaic_skip_kernel(
             func=ACT.Silu,
         )
         r_b00 = round_on_scalar(wb_raw[0, 0], rounded_slot("raw_00"))
-        gather_skip(0, 0, slot("codes_01", [P, M], F32)[:])
         w1_q[1, 1] = quantise(r11, "w1_1_1")
         first_passes(acc, 1, 1)
         low = round_half_on_vector(w1_raw[2, 1], half_slot("half_a"), 0)
@@ -324,8 +335,8 @@ def tile_list_reef_mosaic_skip_kernel(
         quantise_half(high, w1_q[2, 1], 1)
         first_passes(acc, 2, 1)
         early = slot("raw_21", [P, 3 * M], F32)
-        for t in range(1, PACK):
-            gather_skip(0, t, early[:, M * (t - 1) : M * t])
+        for t in range(3):
+            gather_skip(0, t, early[:, M * t : M * (t + 1)])
 
         x0 = rounded_slot("half_a")
         piece_width = M * PACK // GAIN_PIECES
@@ -337,19 +348,20 @@ def tile_list_reef_mosaic_skip_kernel(
                 in1=half_gain[:, 0, :].unsqueeze(1).to_broadcast([P, piece_width // PACK, PACK]),
                 op=ALU.mult,
             )
-        reorder_wa(1, slot("half_b", [P, H], U16))
+
+        low_01 = round_half_on_gpsimd(wb_raw[0, 1], half_slot("half_b"), 0)
 
         for t in range(PACK):
             leave_psum(1, acc, t, place("h_1_%d" % t, [P, S], F32, 4 * t))
-        low = round_half_on_scalar(wb_raw[1, 0], half_slot("codes_21"), 0)
         silu1 = slot("v_2", [P, PACK, M], F32)
         for t in range(PACK):
-            deep = place("deep_1", [P, M], F32, 28) if t == 1 else slot("deep_%d" % t, [P, M], F32)
+            deep = place("deep_1", [P, M], F32, 24) if t == 1 else slot("deep_%d" % t, [P, M], F32)
             gather_deep(1, t, deep[:])
             nc.scalar.activation(out=silu1[:, t, :], in_=deep[:], func=ACT.Silu)
-        high = round_half_on_scalar(wb_raw[1, 0], half_slot("deep_2"), 1)
-        r_b01 = round_on_scalar(wb_raw[0, 1], rounded_slot("deep_3"))
-        codes = place("codes", [P, 3 * KP], U32, 24)
+        r_b10 = round_on_scalar(wb_raw[1, 0], rounded_slot("deep_2"))
+        high_01 = round_half_on_scalar(wb_raw[0, 1], half_slot("deep_3"), 1)
+        r_b11 = round_on_scalar(wb_raw[1, 1], rounded_slot("tab_0"))
+        codes = place("codes", [P, 2 * KP], U32, 22)
         x_q[0] = quantise(x0, "x_0", codes[:, 0:KP])
         wb_q[0, 0] = quantise(r_b00, "wb_0_0", codes[:, KP : 2 * KP])
         x1 = rounded_slot("half_a")
@@ -359,9 +371,7 @@ def tile_list_reef_mosaic_skip_kernel(
             in1=half_gain[:, 1, :].unsqueeze(1).unsqueeze(3).to_broadcast([P, M // 2, PACK, 2]),
             op=ALU.mult,
         )
-        wb_q[1, 0] = operand("wb_1_0", codes[:, 2 * KP : 3 * KP])
-        quantise_half(low, wb_q[1, 0], 0)
-        quantise_half(high, wb_q[1, 0], 1)
+        wb_q[1, 0] = quantise(r_b10, "wb_1_0", place("wb_10_codes", [P, KP], U32, 20))
         x_q[1] = quantise(x1, "x_1")
 
         acc = banks()
@@ -371,30 +381,26 @@ def tile_list_reef_mosaic_skip_kernel(
         for t in range(PACK):
             gate_pass(acc, 1, 0, t)
             value_pass(acc, 1, 0, t)
-        low = round_half_on_scalar(wb_raw[1, 1], half_slot("tab_0"), 0)
-        high = round_half_on_vector(wb_raw[1, 1], half_slot("v_2"), 1)
-        wb_q[0, 1] = quantise(r_b01, "wb_0_1")
-        wb_q[1, 1] = operand("wb_1_1")
-        quantise_half(low, wb_q[1, 1], 0)
-        quantise_half(high, wb_q[1, 1], 1)
-        gated = {}
-        first = slot("tab_0", [P, PACK * M], F32)
+        gather_skip(0, 3, slot("v_2", [P, M], F32)[:])
+        wb_q[0, 1] = operand("wb_0_1", slot("half_a", [P, KP], U32))
+        quantise_half(low_01, wb_q[0, 1], 0)
+        quantise_half(high_01, wb_q[0, 1], 1)
+        gather_skip(1, 0, slot("tab_1", [P, M], F32)[:])
+        wb_q[1, 1] = quantise(r_b11, "wb_1_1", slot("half_b", [P, KP], U32))
+        first = slot("tab_2", [P, PACK * M], F32)
         for t in range(PACK):
-            gated[0, t] = gated_value(0, t, acc, first[:, M * t : M * (t + 1)])
-            add_and_store(nc.gpsimd, 0, t, gated[0, t], skip[0, t])
-        last = slot("tanh_0_2", [P, 2 * M], F32)
-        for t in range(2):
-            gather_skip(1, t, last[:, M * t : M * (t + 1)])
+            add_and_store(nc.gpsimd, 0, t, gated_value(0, t, acc, first[:, M * t : M * (t + 1)]), skip[0, t])
         acc = banks()
         for t in range(PACK):
             for a in range(GROUPS):
                 gate_pass(acc, a, 1, t)
             for a in range(GROUPS):
                 value_pass(acc, a, 1, t)
+        gated = {}
         for t in range(PACK):
-            gated[1, t] = gated_value(1, t, acc, slot("deep_%d" % (0, 2, 3, 0)[t] if t < 3 else "raw_10", [P, M], F32)[:])
-        res = slot("tab_0", [P, PACK * M], F32)
-        for t in range(2):
-            add_and_store(nc.vector, 1, t, gated[1, t], res[:, M * t : M * (t + 1)])
-        fused_and_store(1, 2, gated[1, 2], res[:, 2 * M : 3 * M])
-        fused_and_store(1, 3, gated[1, 3], res[:, 3 * M : 4 * M], parts=2)
+            gated[t] = gated_value(1, t, acc, slot("gated_%d" % t, [P, M], F32)[:])
+            if t == 0:
+                add_and_store(nc.gpsimd, 1, t, gated[t], skip[1, t])
+            if t >= 2:
+                fused_and_store(1, t - 1, gated[t - 1])
+        fused_and_store(1, 3, gated[3], parts=2)

@@ -44,8 +44,10 @@ def tile_list_reef_mosaic_skip_kernel(
         pos2_sb = keep.tile([P, M // LIST_ROWS], U16, name="pos2_sb")
         tab_planes = keep.tile([P, T], U8, name="tab_planes", align_bytes=64)
         wa_planes_raw = keep.tile([P, GROUPS * H], U8, name="wa_planes_raw", align_bytes=64)
-        vec_raw = keep.tile([P, 2, GROUPS, 2 * PACK], F32, name="vec_raw")
-        vec_half = keep.tile([P, 2, GROUPS, PACK], F32, name="vec_half")
+        gain_raw = keep.tile([P, GROUPS, 2 * PACK], F32, name="gain_raw")
+        bg_raw = keep.tile([P, GROUPS, 2 * PACK], F32, name="bg_raw")
+        half_gain = keep.tile([P, GROUPS, PACK], F32, name="half_gain")
+        half_bg = keep.tile([P, GROUPS, PACK], F32, name="half_bg")
         warm = keep.tile([P, 1], F32, name="warm")
 
         def slot(tag, shape, dtype):
@@ -152,6 +154,7 @@ def tile_list_reef_mosaic_skip_kernel(
         wb_q = {}
         x_q = {}
         wa = {}
+        wa_planes = {}
         out_rows = out.rearrange("(b p t) m -> b t p m", b=GROUPS, t=PACK)
 
         def first_pass(acc, a, b, t):
@@ -201,25 +204,29 @@ def tile_list_reef_mosaic_skip_kernel(
 
         def value_pass(acc, a, b, t):
             x_codes, x_scales = x_q[a]
-            wa_cols = slice(H * a + KP * b + P * t, H * a + KP * b + P * (t + 1))
-            word_cols = slice(KP * a + P * t, KP * a + P * (t + 1))
+            cols = slice(P * t, P * (t + 1))
+            plane_cols = slice(KP * b + P * t, KP * b + P * (t + 1))
             nc.tensor.matmul_mx(
                 out=acc[t, 1][:],
-                lhsT=wa[b][:, word_cols].bitcast(FP4X4),
-                lhsT_scale=wa_planes[:, wa_cols],
+                lhsT=wa[a, b][:, cols].bitcast(FP4X4),
+                lhsT_scale=wa_planes[a][:, plane_cols],
                 rhs=x_codes[:].bitcast(FP8X4),
                 rhs_scale=x_scales[:],
                 start=(a == 0),
                 stop=(a == GROUPS - 1),
             )
 
-        def reorder_wa(b, tile):
-            wa[b] = tile
-            dst = tile[:].bitcast(U8).rearrange("p (a t m e) -> p a t m e", a=GROUPS, t=PACK, e=2)
-            src = wa_raw[:].rearrange("p a c -> p (a c)").bitcast(U8)
-            src = src.rearrange("p (a b m t e) -> p b a t m e", a=GROUPS, b=GROUPS, t=PACK, e=2)
-            for a in range(GROUPS):
-                nc.gpsimd.tensor_copy(out=dst[:, a], in_=src[:, b, a])
+        def reorder_wa(a, b, words):
+            wa[a, b] = words
+            src = wa_raw[:, a, :].bitcast(U8).rearrange("p (b m t e) -> p b t m e", b=GROUPS, t=PACK, e=2)
+            nc.gpsimd.tensor_copy(out=words.bitcast(U8).rearrange("p (t m e) -> p t m e", t=PACK, e=2), in_=src[:, b])
+
+        def reorder_wa_plane(a, plane):
+            wa_planes[a] = plane
+            nc.gpsimd.tensor_copy(
+                out=plane[:].rearrange("p (b t m) -> p b t m", t=PACK, m=P),
+                in_=wa_planes_raw[:, H * a : H * (a + 1)].rearrange("p (b m t) -> p b t m", t=PACK, m=P),
+            )
 
         def gated_value(b, t, acc, gated):
             tanh = slot("tanh_%d_%d" % (b, t), [P, M], F32)
@@ -234,8 +241,7 @@ def tile_list_reef_mosaic_skip_kernel(
                 engine.tensor_tensor(out=res[:, cols], in0=skip[b, t][:, cols], in1=gated[:, cols], op=ALU.add)
                 nc.sync.dma_start(out=out_rows[b, t][:, cols], in_=res[:, cols])
 
-        def fused_and_store(b, t, gated, parts=1):
-            res = slot("res_%d" % t, [P, M], F32)
+        def fused_and_store(b, t, gated, res, parts=1):
             width = M // parts
             for part in range(parts):
                 cols = slice(width * part, width * (part + 1))
@@ -247,19 +253,16 @@ def tile_list_reef_mosaic_skip_kernel(
         nc.gpsimd.memset(wa_planes_raw[:].bitcast(I32), 0)
         for q in range(2):
             load_table_scales(nc.scalar, q)
-        for i, vec in enumerate((gain, bg)):
-            nc.scalar.dma_start(out=vec_raw[:, i, :, 0:PACK], in_=vec.rearrange("(b p t) -> p b t", b=GROUPS, t=PACK))
+        nc.scalar.dma_start(out=gain_raw[:, :, 0:PACK], in_=gain.rearrange("(b p t) -> p b t", b=GROUPS, t=PACK))
         for q in range(P // QUADRANT):
             nc.gpsimd.dma_start(
                 out=wa_planes_raw[QUADRANT * q : QUADRANT * q + 4, :].bitcast(I32).rearrange("r (a c) -> r a c", a=GROUPS),
                 in_=wa_scales[:, 4 * q : 4 * q + 4, :].bitcast(I32).rearrange("a r c -> r a c"),
             )
         nc.gpsimd.tensor_scalar(
-            out=vec_half[:], in0=vec_raw[:, :, :, 0:PACK], scalar1=0.5, scalar2=0.0, op0=ALU.mult, op1=ALU.add
+            out=half_gain[:], in0=gain_raw[:, :, 0:PACK], scalar1=0.5, scalar2=0.0, op0=ALU.mult, op1=ALU.add
         )
-        nc.scalar.activation(out=warm[:], in_=vec_raw[:, 0, 0, 0:1], func=ACT.Silu)
-        half_gain = vec_half[:, 0]
-        half_bg = vec_half[:, 1]
+        nc.scalar.activation(out=warm[:], in_=gain_raw[:, 0, 0:1], func=ACT.Silu)
 
         nc.sync.dma_start(offs_sb[:], offs)
         tab = {}
@@ -281,38 +284,37 @@ def tile_list_reef_mosaic_skip_kernel(
         wide = place("wb_00_raw", [P, 2 * PACK, KP], F32, 0)
         wb_raw[0, 0] = load_weight(wb, 0, 0, wide[:, 0:PACK, :])
 
-        wa_planes = keep.tile([P, GROUPS * H], U8, name="wa_planes", align_bytes=64)
-        dst_runs = wa_planes[:].rearrange("p (g t m) -> p g t m", t=PACK, m=P)
-        src_runs = wa_planes_raw[:].rearrange("p (g m t) -> p g t m", t=PACK, m=P)
-        for g in range(GROUPS * GROUPS):
-            nc.gpsimd.tensor_copy(out=dst_runs[:, g], in_=src_runs[:, g])
-
         acc = banks()
         v[0] = gather_words(tab[0], 0)
         v_planes = keep.tile([P, S], U8, name="v_planes", align_bytes=64)
         nc.vector.tensor_copy(out=v_planes[:], in_=tab_planes[:].indirect(offs_sb[:]))
-        w1_q[0, 0] = quantise(round_on_scalar(w1_raw[0, 0], rounded_slot("r0")), "w1_0_0")
-        first_passes(acc, 0, 0)
-        for a in range(1, K_PASSES):
-            v[a] = gather_words(tab[a], a)
+        for a in range(K_PASSES):
+            if a > 0:
+                v[a] = gather_words(tab[a], a)
             low = round_half_on_vector(w1_raw[a, 0], half_slot("half_a"), 0)
-            high = round_half_on_scalar(w1_raw[a, 0], half_slot("half_b"), 1)
+            high_tag = "half_b" if a == K_PASSES - 1 else "high_%d" % a
+            high = round_half_on_scalar(w1_raw[a, 0], half_slot(high_tag), 1)
             w1_q[a, 0] = operand("w1_%d_0" % a)
-            quantise_half(low, w1_q[a, 0], 0)
-            quantise_half(high, w1_q[a, 0], 1)
+            quantise_half(high, w1_q[a, 0], 1) if a < K_PASSES - 1 else quantise_half(low, w1_q[a, 0], 0)
+            quantise_half(low, w1_q[a, 0], 0) if a < K_PASSES - 1 else quantise_half(high, w1_q[a, 0], 1)
+            if a < GROUPS:
+                reorder_wa_plane(a, slot(high_tag, [P, H], U8))
             first_passes(acc, a, 0)
         wb_raw[1, 0] = load_weight(wb, 1, 0, raw_slot("tab_0"))
         wb_raw[0, 1] = load_weight(wb, 0, 1, raw_slot("tab_1"))
         wb_raw[1, 1] = load_weight(wb, 1, 1, raw_slot("tab_2"))
+        nc.sync.dma_start(out=bg_raw[:, :, 0:PACK], in_=bg.rearrange("(b p t) -> p b t", b=GROUPS, t=PACK))
 
         r01 = round_on_vector(w1_raw[0, 1], rounded_slot("r0"))
         for t in range(PACK):
             leave_psum(0, acc, t, slot("h_0_%d" % t, [P, S], F32))
         deep0 = slot("raw_10", [P, PACK, M], F32)
         gather_deep(0, 0, deep0[:, 0, :])
-        w1_q[0, 1] = quantise(r01, "w1_0_1")
-        for b in range(GROUPS):
-            reorder_wa(b, slot("wa_%d" % b, [P, H], U16))
+        w1_q[0, 1] = quantise(r01, "w1_0_1", slot("codes_01", [P, KP], U32))
+        reorder_wa(0, 0, slot("wa_00", [P, KP], U16)[:])
+        rest = slot("r0", [P, 3 * KP], U16)
+        for i, (a, b) in enumerate(((1, 0), (0, 1), (1, 1))):
+            reorder_wa(a, b, rest[:, KP * i : KP * (i + 1)])
         for t in range(1, PACK):
             gather_deep(0, t, deep0[:, t, :])
 
@@ -326,6 +328,7 @@ def tile_list_reef_mosaic_skip_kernel(
             func=ACT.Silu,
         )
         r_b00 = round_on_scalar(wb_raw[0, 0], rounded_slot("raw_00"))
+        gather_skip(0, 2, slot("codes_01", [P, M], F32)[:])
         w1_q[1, 1] = quantise(r11, "w1_1_1")
         first_passes(acc, 1, 1)
         low = round_half_on_vector(w1_raw[2, 1], half_slot("half_a"), 0)
@@ -335,8 +338,8 @@ def tile_list_reef_mosaic_skip_kernel(
         quantise_half(high, w1_q[2, 1], 1)
         first_passes(acc, 2, 1)
         early = slot("raw_21", [P, 3 * M], F32)
-        for t in range(3):
-            gather_skip(0, t, early[:, M * t : M * (t + 1)])
+        for i, t in enumerate((0, 1, 3)):
+            gather_skip(0, t, early[:, M * i : M * (i + 1)])
 
         x0 = rounded_slot("half_a")
         piece_width = M * PACK // GAIN_PIECES
@@ -359,8 +362,8 @@ def tile_list_reef_mosaic_skip_kernel(
             gather_deep(1, t, deep[:])
             nc.scalar.activation(out=silu1[:, t, :], in_=deep[:], func=ACT.Silu)
         r_b10 = round_on_scalar(wb_raw[1, 0], rounded_slot("deep_2"))
-        high_01 = round_half_on_scalar(wb_raw[0, 1], half_slot("deep_3"), 1)
-        r_b11 = round_on_scalar(wb_raw[1, 1], rounded_slot("tab_0"))
+        nc.scalar.mul(out=half_bg[:], in_=bg_raw[:, :, 0:PACK], mul=0.5)
+        r_b11 = round_on_scalar(wb_raw[1, 1], rounded_slot("deep_3"))
         codes = place("codes", [P, 2 * KP], U32, 22)
         x_q[0] = quantise(x0, "x_0", codes[:, 0:KP])
         wb_q[0, 0] = quantise(r_b00, "wb_0_0", codes[:, KP : 2 * KP])
@@ -381,26 +384,29 @@ def tile_list_reef_mosaic_skip_kernel(
         for t in range(PACK):
             gate_pass(acc, 1, 0, t)
             value_pass(acc, 1, 0, t)
-        gather_skip(0, 3, slot("v_2", [P, M], F32)[:])
+        high_01 = round_half_on_vector(wb_raw[0, 1], half_slot("v_2"), 1)
         wb_q[0, 1] = operand("wb_0_1", slot("half_a", [P, KP], U32))
         quantise_half(low_01, wb_q[0, 1], 0)
         quantise_half(high_01, wb_q[0, 1], 1)
-        gather_skip(1, 0, slot("tab_1", [P, M], F32)[:])
         wb_q[1, 1] = quantise(r_b11, "wb_1_1", slot("half_b", [P, KP], U32))
         first = slot("tab_2", [P, PACK * M], F32)
         for t in range(PACK):
             add_and_store(nc.gpsimd, 0, t, gated_value(0, t, acc, first[:, M * t : M * (t + 1)]), skip[0, t])
+        gather_skip(1, 1, slot("tanh_0_2", [P, M], F32)[:])
         acc = banks()
-        for t in range(PACK):
+        for t in range(PACK + 1):
             for a in range(GROUPS):
-                gate_pass(acc, a, 1, t)
+                if t < PACK:
+                    gate_pass(acc, a, 1, t)
             for a in range(GROUPS):
-                value_pass(acc, a, 1, t)
+                if t > 0:
+                    value_pass(acc, a, 1, t - 1)
         gated = {}
         for t in range(PACK):
             gated[t] = gated_value(1, t, acc, slot("gated_%d" % t, [P, M], F32)[:])
-            if t == 0:
+            if t == 1:
                 add_and_store(nc.gpsimd, 1, t, gated[t], skip[1, t])
-            if t >= 2:
-                fused_and_store(1, t - 1, gated[t - 1])
-        fused_and_store(1, 3, gated[3], parts=2)
+                fused_and_store(1, 0, gated[0], slot("half_a", [P, M], F32)[:])
+        last = slot("r0", [P, 2 * M], F32)
+        fused_and_store(1, 2, gated[2], last[:, 0:M])
+        fused_and_store(1, 3, gated[3], last[:, M : 2 * M], parts=2)

@@ -44,10 +44,8 @@ def tile_list_reef_mosaic_skip_kernel(
         pos2_sb = keep.tile([P, M // LIST_ROWS], U16, name="pos2_sb")
         tab_planes = keep.tile([P, T], U8, name="tab_planes", align_bytes=64)
         wa_planes_raw = keep.tile([P, GROUPS * H], U8, name="wa_planes_raw", align_bytes=64)
-        gain_raw = keep.tile([P, GROUPS, 2 * PACK], F32, name="gain_raw")
-        bg_raw = keep.tile([P, GROUPS, 2 * PACK], F32, name="bg_raw")
-        half_gain = keep.tile([P, GROUPS, PACK], F32, name="half_gain")
-        half_bg = keep.tile([P, GROUPS, PACK], F32, name="half_bg")
+        vec_raw = keep.tile([P, 2, GROUPS, 2 * PACK], F32, name="vec_raw")
+        vec_half = keep.tile([P, 2, GROUPS, PACK], F32, name="vec_half")
         warm = keep.tile([P, 1], F32, name="warm")
 
         def slot(tag, shape, dtype):
@@ -253,16 +251,19 @@ def tile_list_reef_mosaic_skip_kernel(
         nc.gpsimd.memset(wa_planes_raw[:].bitcast(I32), 0)
         for q in range(2):
             load_table_scales(nc.scalar, q)
-        nc.scalar.dma_start(out=gain_raw[:, :, 0:PACK], in_=gain.rearrange("(b p t) -> p b t", b=GROUPS, t=PACK))
+        for i, vec in enumerate((gain, bg)):
+            nc.scalar.dma_start(out=vec_raw[:, i, :, 0:PACK], in_=vec.rearrange("(b p t) -> p b t", b=GROUPS, t=PACK))
         for q in range(P // QUADRANT):
             nc.gpsimd.dma_start(
                 out=wa_planes_raw[QUADRANT * q : QUADRANT * q + 4, :].bitcast(I32).rearrange("r (a c) -> r a c", a=GROUPS),
                 in_=wa_scales[:, 4 * q : 4 * q + 4, :].bitcast(I32).rearrange("a r c -> r a c"),
             )
         nc.gpsimd.tensor_scalar(
-            out=half_gain[:], in0=gain_raw[:, :, 0:PACK], scalar1=0.5, scalar2=0.0, op0=ALU.mult, op1=ALU.add
+            out=vec_half[:], in0=vec_raw[:, :, :, 0:PACK], scalar1=0.5, scalar2=0.0, op0=ALU.mult, op1=ALU.add
         )
-        nc.scalar.activation(out=warm[:], in_=gain_raw[:, 0, 0:1], func=ACT.Silu)
+        nc.scalar.activation(out=warm[:], in_=vec_raw[:, 0, 0, 0:1], func=ACT.Silu)
+        half_gain = vec_half[:, 0]
+        half_bg = vec_half[:, 1]
 
         nc.sync.dma_start(offs_sb[:], offs)
         tab = {}
@@ -303,7 +304,6 @@ def tile_list_reef_mosaic_skip_kernel(
         wb_raw[1, 0] = load_weight(wb, 1, 0, raw_slot("tab_0"))
         wb_raw[0, 1] = load_weight(wb, 0, 1, raw_slot("tab_1"))
         wb_raw[1, 1] = load_weight(wb, 1, 1, raw_slot("tab_2"))
-        nc.sync.dma_start(out=bg_raw[:, :, 0:PACK], in_=bg.rearrange("(b p t) -> p b t", b=GROUPS, t=PACK))
 
         r01 = round_on_vector(w1_raw[0, 1], rounded_slot("r0"))
         for t in range(PACK):
@@ -362,7 +362,6 @@ def tile_list_reef_mosaic_skip_kernel(
             gather_deep(1, t, deep[:])
             nc.scalar.activation(out=silu1[:, t, :], in_=deep[:], func=ACT.Silu)
         r_b10 = round_on_scalar(wb_raw[1, 0], rounded_slot("deep_2"))
-        nc.scalar.mul(out=half_bg[:], in_=bg_raw[:, :, 0:PACK], mul=0.5)
         r_b11 = round_on_scalar(wb_raw[1, 1], rounded_slot("deep_3"))
         codes = place("codes", [P, 2 * KP], U32, 22)
         x_q[0] = quantise(x0, "x_0", codes[:, 0:KP])

@@ -117,12 +117,11 @@ def tile_list_reef_mosaic_skip_kernel(
             nc.vector.tensor_copy(out=dst, in_=src)
             return rounded
 
-        def round_half_on_gpsimd(raw, half, u):
-            dst = half[:].rearrange("p (v m j) -> p v m j", v=2, j=PACK)
-            src = raw[:].rearrange("p j (m u v) -> p u v m j", u=2, v=2)
-            for v in range(2):
-                nc.gpsimd.tensor_copy(out=dst[:, v], in_=src[:, u, v])
-            return half
+        def round_on_gpsimd(raw, rounded):
+            dst = rounded[:].rearrange("p (t m j) -> p m j t", t=PACK, j=PACK)
+            src = raw[:].rearrange("p j (m t) -> p m j t", t=PACK)
+            nc.gpsimd.tensor_copy(out=dst, in_=src)
+            return rounded
 
         def operand(name, codes=None):
             if codes is None:
@@ -352,7 +351,7 @@ def tile_list_reef_mosaic_skip_kernel(
                 op=ALU.mult,
             )
 
-        low_01 = round_half_on_gpsimd(wb_raw[0, 1], half_slot("half_b"), 0)
+        r_b01 = round_on_gpsimd(wb_raw[0, 1], rounded_slot("half_b"))
 
         for t in range(PACK):
             leave_psum(1, acc, t, place("h_1_%d" % t, [P, S], F32, 4 * t))
@@ -383,10 +382,7 @@ def tile_list_reef_mosaic_skip_kernel(
         for t in range(PACK):
             gate_pass(acc, 1, 0, t)
             value_pass(acc, 1, 0, t)
-        high_01 = round_half_on_vector(wb_raw[0, 1], half_slot("v_2"), 1)
-        wb_q[0, 1] = operand("wb_0_1", slot("half_a", [P, KP], U32))
-        quantise_half(low_01, wb_q[0, 1], 0)
-        quantise_half(high_01, wb_q[0, 1], 1)
+        wb_q[0, 1] = quantise(r_b01, "wb_0_1", slot("half_a", [P, KP], U32))
         wb_q[1, 1] = quantise(r_b11, "wb_1_1", slot("half_b", [P, KP], U32))
         first = slot("tab_2", [P, PACK * M], F32)
         for t in range(PACK):

@@ -52,7 +52,7 @@ def tile_list_reef_mosaic_skip_kernel(
             return ring.tile(shape, dtype, name=tag, tag=tag, align_bytes=64)
 
         def place(name, shape, dtype, kib):
-            return placed.tile(shape, dtype, name=name, tag=name, align_bytes=64, offset=kib * KIB)
+            return placed.tile(shape, dtype, name=name, tag=name, align_bytes=64, offset=int(kib * KIB))
 
         def bank(t, half):
             return psum.tile([P, BANK], F32, name="bank_%d_%d" % (t, half), tag="bank_%d_%d" % (t, half))
@@ -213,10 +213,15 @@ def tile_list_reef_mosaic_skip_kernel(
                 stop=(a == GROUPS - 1),
             )
 
+        def reorder_wa_on_scalar(a, b, words):
+            wa[a, b] = words[:]
+            src = wa_raw[:, a, :].bitcast(U16).rearrange("p (b m u v) -> p b u m v", b=GROUPS, u=2, v=2)
+            nc.scalar.copy(out=words[:].rearrange("p (u v m) -> p u m v", u=2, v=2), in_=src[:, b])
+
         def reorder_wa(a, b, words):
-            wa[a, b] = words
+            wa[a, b] = words[:]
             src = wa_raw[:, a, :].bitcast(U8).rearrange("p (b m t e) -> p b t m e", b=GROUPS, t=PACK, e=2)
-            nc.gpsimd.tensor_copy(out=words.bitcast(U8).rearrange("p (t m e) -> p t m e", t=PACK, e=2), in_=src[:, b])
+            nc.gpsimd.tensor_copy(out=words[:].bitcast(U8).rearrange("p (t m e) -> p t m e", t=PACK, e=2), in_=src[:, b])
 
         def reorder_wa_plane(a, plane):
             wa_planes[a] = plane
@@ -277,12 +282,11 @@ def tile_list_reef_mosaic_skip_kernel(
         w1_raw[0, 1] = load_weight(w1, 0, 1, raw_slot("raw_01"))
         nc.sync.dma_start(pos1_sb[:], pos1)
         nc.sync.dma_start(pos2_sb[:], pos2)
+        w1_raw[1, 1] = load_weight(w1, 1, 1, place("raw_11", [P, PACK, KP], F32, 16))
+        w1_raw[2, 1] = load_weight(w1, 2, 1, place("raw_21", [P, PACK, KP], F32, 24))
         wa_raw = slot("wa_raw", [P, GROUPS, H // 2], I32)
         nc.sync.dma_start(out=wa_raw[:], in_=wa_words.bitcast(I32).rearrange("a p c -> p a c"))
-        w1_raw[1, 1] = load_weight(w1, 1, 1, place("raw_11", [P, PACK, KP], F32, 16))
-        w1_raw[2, 1] = load_weight(w1, 2, 1, raw_slot("raw_21"))
-        wide = place("wb_00_raw", [P, 2 * PACK, KP], F32, 0)
-        wb_raw[0, 0] = load_weight(wb, 0, 0, wide[:, 0:PACK, :])
+        wb_raw[0, 0] = load_weight(wb, 0, 0, raw_slot("raw_b00"))
 
         acc = banks()
         v[0] = gather_words(tab[0], 0)
@@ -294,7 +298,7 @@ def tile_list_reef_mosaic_skip_kernel(
             low = round_half_on_vector(w1_raw[a, 0], half_slot("half_a"), 0)
             high_tag = "half_b" if a == K_PASSES - 1 else "high_%d" % a
             high = round_half_on_scalar(w1_raw[a, 0], half_slot(high_tag), 1)
-            w1_q[a, 0] = operand("w1_%d_0" % a)
+            w1_q[a, 0] = operand("w1_%d_0" % a, slot("codes_%d0" % a, [P, KP], U32))
             quantise_half(high, w1_q[a, 0], 1) if a < K_PASSES - 1 else quantise_half(low, w1_q[a, 0], 0)
             quantise_half(low, w1_q[a, 0], 0) if a < K_PASSES - 1 else quantise_half(high, w1_q[a, 0], 1)
             if a < GROUPS:
@@ -304,43 +308,38 @@ def tile_list_reef_mosaic_skip_kernel(
         wb_raw[0, 1] = load_weight(wb, 0, 1, raw_slot("tab_1"))
         wb_raw[1, 1] = load_weight(wb, 1, 1, raw_slot("tab_2"))
 
-        r01 = round_on_vector(w1_raw[0, 1], rounded_slot("r0"))
+        r01 = round_on_vector(w1_raw[0, 1], place("r01", [P, KP * PACK], BF16, 42))
         for t in range(PACK):
             leave_psum(0, acc, t, slot("h_0_%d" % t, [P, S], F32))
-        deep0 = slot("raw_10", [P, PACK, M], F32)
+        deep0 = place("deep0", [P, 2 * PACK, M], F32, 0)[:, 0:PACK, :]
         gather_deep(0, 0, deep0[:, 0, :])
-        w1_q[0, 1] = quantise(r01, "w1_0_1", slot("codes_01", [P, KP], U32))
-        reorder_wa(0, 0, slot("wa_00", [P, KP], U16)[:])
-        rest = slot("r0", [P, 3 * KP], U16)
-        for i, (a, b) in enumerate(((1, 0), (0, 1), (1, 1))):
-            reorder_wa(a, b, rest[:, KP * i : KP * (i + 1)])
+        w1_q[0, 1] = quantise(r01, "w1_0_1", place("codes_01", [P, KP], U32, 59))
         for t in range(1, PACK):
             gather_deep(0, t, deep0[:, t, :])
 
         acc = banks()
         first_passes(acc, 0, 1)
-        r11 = round_on_scalar(w1_raw[1, 1], rounded_slot("r1"))
-        silu0 = place("silu0", [P, M * PACK], F32, 16)
+        r11 = round_on_gpsimd(w1_raw[1, 1], place("r11", [P, KP * PACK], BF16, 42))
+        r21 = round_on_scalar(w1_raw[2, 1], place("r21", [P, KP * PACK], BF16, 46))
+        silu0 = place("silu0", [P, M * PACK], F32, 29.5)
         nc.scalar.activation(
             out=silu0[:].rearrange("p (c i t) -> p c t i", i=2, t=PACK),
-            in_=deep0[:].rearrange("p t (c i) -> p c t i", i=2),
+            in_=deep0.rearrange("p t (c i) -> p c t i", i=2),
             func=ACT.Silu,
         )
-        r_b00 = round_on_scalar(wb_raw[0, 0], rounded_slot("raw_00"))
-        gather_skip(0, 2, slot("codes_01", [P, M], F32)[:])
-        w1_q[1, 1] = quantise(r11, "w1_1_1")
-        first_passes(acc, 1, 1)
-        low = round_half_on_vector(w1_raw[2, 1], half_slot("half_a"), 0)
-        high = round_half_on_vector(w1_raw[2, 1], half_slot("half_b"), 1)
-        w1_q[2, 1] = operand("w1_2_1", slot("codes_21", [P, KP], U32))
-        quantise_half(low, w1_q[2, 1], 0)
-        quantise_half(high, w1_q[2, 1], 1)
-        first_passes(acc, 2, 1)
-        early = slot("raw_21", [P, 3 * M], F32)
-        for i, t in enumerate((0, 1, 3)):
-            gather_skip(0, t, early[:, M * i : M * (i + 1)])
+        r_b00 = round_on_scalar(wb_raw[0, 0], place("r_b00", [P, KP * PACK], BF16, 25.5))
+        w1_q[1, 1] = quantise(r11, "w1_1_1", place("codes_11", [P, KP], U32, 58))
+        gather_skip(0, 0, place("skip_00", [P, M], F32, 60)[:])
+        w1_q[2, 1] = quantise(r21, "w1_2_1", place("codes_21", [P, KP], U32, 42))
+        for pair in range(2):
+            for a in (1, 2):
+                for t in (2 * pair, 2 * pair + 1):
+                    first_pass(acc, a, 1, t)
+        early = place("early", [P, (PACK - 1) * M], F32, 18.5)
+        for t in range(1, PACK):
+            gather_skip(0, t, early[:, M * (t - 1) : M * t])
 
-        x0 = rounded_slot("half_a")
+        x0 = place("x0", [P, KP * PACK], BF16, 44)
         piece_width = M * PACK // GAIN_PIECES
         for piece in range(GAIN_PIECES):
             cols = slice(piece_width * piece, piece_width * (piece + 1))
@@ -350,29 +349,34 @@ def tile_list_reef_mosaic_skip_kernel(
                 in1=half_gain[:, 0, :].unsqueeze(1).to_broadcast([P, piece_width // PACK, PACK]),
                 op=ALU.mult,
             )
-
-        r_b01 = round_on_gpsimd(wb_raw[0, 1], rounded_slot("half_b"))
+        r_b10 = round_on_gpsimd(wb_raw[1, 0], place("r_b10", [P, KP * PACK], BF16, 29.5))
 
         for t in range(PACK):
             leave_psum(1, acc, t, place("h_1_%d" % t, [P, S], F32, 4 * t))
         silu1 = slot("v_2", [P, PACK, M], F32)
         for t in range(PACK):
-            deep = place("deep_1", [P, M], F32, 24) if t == 1 else slot("deep_%d" % t, [P, M], F32)
+            deep = slot("deep_%d" % t, [P, M], F32) if t % 3 == 0 else place("deep_%d" % t, [P, M], F32, 37.5 if t == 1 else 53)
             gather_deep(1, t, deep[:])
+            if t == 2:
+                first_wa = slot("deep_0", [P, GROUPS * KP], U16)
+            if t >= 2:
+                reorder_wa_on_scalar(t - 2, 0, first_wa[:, KP * (t - 2) : KP * (t - 1)])
             nc.scalar.activation(out=silu1[:, t, :], in_=deep[:], func=ACT.Silu)
-        r_b10 = round_on_scalar(wb_raw[1, 0], rounded_slot("deep_2"))
-        r_b11 = round_on_scalar(wb_raw[1, 1], rounded_slot("deep_3"))
-        codes = place("codes", [P, 2 * KP], U32, 22)
+        r_b01 = round_on_scalar(wb_raw[0, 1], place("r_b01", [P, KP * PACK], BF16, 50))
+        r_b11 = round_on_scalar(wb_raw[1, 1], place("r_b11", [P, KP * PACK], BF16, 54))
+        reorder_wa_on_scalar(0, 1, slot("tab_1", [P, KP], U16))
+        codes = place("codes", [P, 3 * KP], U32, 33.5)
         x_q[0] = quantise(x0, "x_0", codes[:, 0:KP])
-        wb_q[0, 0] = quantise(r_b00, "wb_0_0", codes[:, KP : 2 * KP])
-        x1 = rounded_slot("half_a")
+        wb_q[1, 0] = quantise(r_b10, "wb_1_0", codes[:, KP : 2 * KP])
+        wb_q[0, 0] = quantise(r_b00, "wb_0_0", codes[:, 2 * KP : 3 * KP])
+        x1 = place("x1", [P, KP * PACK], BF16, 44)
         nc.vector.tensor_tensor(
             out=x1[:].rearrange("p (c i t) -> p c t i", i=2, t=PACK),
             in0=silu1[:].rearrange("p t (c i) -> p c t i", i=2),
             in1=half_gain[:, 1, :].unsqueeze(1).unsqueeze(3).to_broadcast([P, M // 2, PACK, 2]),
             op=ALU.mult,
         )
-        wb_q[1, 0] = quantise(r_b10, "wb_1_0", place("wb_10_codes", [P, KP], U32, 20))
+        wb_q[0, 1] = quantise(r_b01, "wb_0_1", place("codes_b01", [P, KP], U32, 25.5))
         x_q[1] = quantise(x1, "x_1")
 
         acc = banks()
@@ -382,12 +386,13 @@ def tile_list_reef_mosaic_skip_kernel(
         for t in range(PACK):
             gate_pass(acc, 1, 0, t)
             value_pass(acc, 1, 0, t)
-        wb_q[0, 1] = quantise(r_b01, "wb_0_1", slot("half_a", [P, KP], U32))
-        wb_q[1, 1] = quantise(r_b11, "wb_1_1", slot("half_b", [P, KP], U32))
+        reorder_wa(1, 1, place("wa_11", [P, KP], U16, 50))
+        gather_skip(1, 1, place("skip_11", [P, M], F32, 51)[:])
+        wb_q[1, 1] = quantise(r_b11, "wb_1_1", place("codes_b11", [P, KP], U32, 44))
         first = slot("tab_2", [P, PACK * M], F32)
         for t in range(PACK):
             add_and_store(nc.gpsimd, 0, t, gated_value(0, t, acc, first[:, M * t : M * (t + 1)]), skip[0, t])
-        gather_skip(1, 1, slot("tanh_0_2", [P, M], F32)[:])
+        gather_skip(1, 0, slot("tanh_0_2", [P, M], F32)[:])
         acc = banks()
         for t in range(PACK + 1):
             for a in range(GROUPS):
@@ -399,9 +404,8 @@ def tile_list_reef_mosaic_skip_kernel(
         gated = {}
         for t in range(PACK):
             gated[t] = gated_value(1, t, acc, slot("gated_%d" % t, [P, M], F32)[:])
-            if t == 1:
+            if t < 2:
                 add_and_store(nc.gpsimd, 1, t, gated[t], skip[1, t])
-                fused_and_store(1, 0, gated[0], slot("half_a", [P, M], F32)[:])
-        last = slot("r0", [P, 2 * M], F32)
+        last = place("last", [P, 2 * M], F32, 47)
         fused_and_store(1, 2, gated[2], last[:, 0:M])
         fused_and_store(1, 3, gated[3], last[:, M : 2 * M], parts=2)

@@ -84,6 +84,10 @@ def tile_list_reef_mosaic_skip_kernel(
         def rounded_slot(tag):
             return slot(tag, [P, KP * PACK], BF16)
 
+        def load_columns(raw, part):
+            cols = slice(KP // 2 * part, KP // 2 * (part + 1))
+            nc.sync.dma_start(out=raw[:, :, cols], in_=wb[0:KP, cols].rearrange("(p j) c -> p j c", j=PACK))
+
         def pair_views(raw, rounded):
             dst = rounded[:].rearrange("p (u v m j) -> p u m j v", u=2, v=2, j=PACK)
             src = raw[:].rearrange("p j (m u v) -> p u m j v", u=2, v=2)
@@ -112,16 +116,20 @@ def tile_list_reef_mosaic_skip_kernel(
             nc.vector.tensor_copy(out=dst, in_=src)
             return half
 
+        def line_views(raw, rounded):
+            dst = rounded[:].rearrange("p (t m j) -> p m j t", t=PACK, j=PACK)
+            src = raw[:].rearrange("p j (m t) -> p m j t", t=PACK)
+            return dst, src
+
         def round_on_vector(raw, rounded):
-            dst, src = pair_views(raw, rounded)
+            dst, src = line_views(raw, rounded)
             nc.vector.tensor_copy(out=dst, in_=src)
             return rounded
 
-        def round_on_gpsimd(raw, rounded):
-            dst = rounded[:].rearrange("p (t m j) -> p m j t", t=PACK, j=PACK)
-            src = raw[:].rearrange("p j (m t) -> p m j t", t=PACK)
-            nc.gpsimd.tensor_copy(out=dst, in_=src)
-            return rounded
+        def round_part_on_gpsimd(raw, rounded, part):
+            dst, src = line_views(raw, rounded)
+            words = slice(P // 2 * part, P // 2 * (part + 1))
+            nc.gpsimd.tensor_copy(out=dst[:, words], in_=src[:, words])
 
         def operand(name, codes=None):
             if codes is None:
@@ -213,11 +221,6 @@ def tile_list_reef_mosaic_skip_kernel(
                 stop=(a == GROUPS - 1),
             )
 
-        def reorder_wa_on_scalar(a, b, words):
-            wa[a, b] = words[:]
-            src = wa_raw[:, a, :].bitcast(U16).rearrange("p (b m u v) -> p b u m v", b=GROUPS, u=2, v=2)
-            nc.scalar.copy(out=words[:].rearrange("p (u v m) -> p u m v", u=2, v=2), in_=src[:, b])
-
         def reorder_wa(a, b, words):
             wa[a, b] = words[:]
             src = wa_raw[:, a, :].bitcast(U8).rearrange("p (b m t e) -> p b t m e", b=GROUPS, t=PACK, e=2)
@@ -268,6 +271,10 @@ def tile_list_reef_mosaic_skip_kernel(
         nc.scalar.activation(out=warm[:], in_=vec_raw[:, 0, 0, 0:1], func=ACT.Silu)
         half_gain = vec_half[:, 0]
         half_bg = vec_half[:, 1]
+        gain_row = keep.tile([P, KP], F32, name="gain_row")
+        nc.gpsimd.tensor_copy(
+            out=gain_row[:].rearrange("p (m t) -> p m t", t=PACK), in_=half_gain[:, 0, :].unsqueeze(1).to_broadcast([P, P, PACK])
+        )
 
         nc.sync.dma_start(offs_sb[:], offs)
         tab = {}
@@ -282,11 +289,12 @@ def tile_list_reef_mosaic_skip_kernel(
         w1_raw[0, 1] = load_weight(w1, 0, 1, raw_slot("raw_01"))
         nc.sync.dma_start(pos1_sb[:], pos1)
         nc.sync.dma_start(pos2_sb[:], pos2)
-        w1_raw[1, 1] = load_weight(w1, 1, 1, place("raw_11", [P, PACK, KP], F32, 16))
-        w1_raw[2, 1] = load_weight(w1, 2, 1, place("raw_21", [P, PACK, KP], F32, 24))
         wa_raw = slot("wa_raw", [P, GROUPS, H // 2], I32)
         nc.sync.dma_start(out=wa_raw[:], in_=wa_words.bitcast(I32).rearrange("a p c -> p a c"))
-        wb_raw[0, 0] = load_weight(wb, 0, 0, raw_slot("raw_b00"))
+        w1_raw[1, 1] = load_weight(w1, 1, 1, place("raw_11", [P, PACK, KP], F32, 16))
+        w1_raw[2, 1] = load_weight(w1, 2, 1, place("raw_21", [P, PACK, KP], F32, 24))
+        wb_raw[0, 0] = raw_slot("raw_b00")
+        load_columns(wb_raw[0, 0], 0)
 
         acc = banks()
         v[0] = gather_words(tab[0], 0)
@@ -305,6 +313,7 @@ def tile_list_reef_mosaic_skip_kernel(
                 reorder_wa_plane(a, slot(high_tag, [P, H], U8))
             first_passes(acc, a, 0)
         wb_raw[1, 0] = load_weight(wb, 1, 0, raw_slot("tab_0"))
+        load_columns(wb_raw[0, 0], 1)
         wb_raw[0, 1] = load_weight(wb, 0, 1, raw_slot("tab_1"))
         wb_raw[1, 1] = load_weight(wb, 1, 1, raw_slot("tab_2"))
 
@@ -313,70 +322,73 @@ def tile_list_reef_mosaic_skip_kernel(
             leave_psum(0, acc, t, slot("h_0_%d" % t, [P, S], F32))
         deep0 = place("deep0", [P, 2 * PACK, M], F32, 0)[:, 0:PACK, :]
         gather_deep(0, 0, deep0[:, 0, :])
-        w1_q[0, 1] = quantise(r01, "w1_0_1", place("codes_01", [P, KP], U32, 59))
+        w1_q[0, 1] = quantise(r01, "w1_0_1", None)
+        reorder_wa(0, 0, slot("wa_00", [P, KP], U16))
+        rest = place("rest", [P, 2 * KP], U16, 42)
+        reorder_wa(1, 0, rest[:, 0:KP])
+        reorder_wa(0, 1, rest[:, KP : 2 * KP])
         for t in range(1, PACK):
             gather_deep(0, t, deep0[:, t, :])
 
         acc = banks()
         first_passes(acc, 0, 1)
-        r11 = round_on_gpsimd(w1_raw[1, 1], place("r11", [P, KP * PACK], BF16, 42))
-        r21 = round_on_scalar(w1_raw[2, 1], place("r21", [P, KP * PACK], BF16, 46))
-        silu0 = place("silu0", [P, M * PACK], F32, 29.5)
+        r11 = round_on_scalar(w1_raw[1, 1], place("r11", [P, KP * PACK], BF16, 46))
+        r21 = round_on_scalar(w1_raw[2, 1], place("r21", [P, KP * PACK], BF16, 38))
+        silu0 = place("silu0", [P, M * PACK], F32, 30)
         nc.scalar.activation(
             out=silu0[:].rearrange("p (c i t) -> p c t i", i=2, t=PACK),
             in_=deep0.rearrange("p t (c i) -> p c t i", i=2),
             func=ACT.Silu,
         )
-        r_b00 = round_on_scalar(wb_raw[0, 0], place("r_b00", [P, KP * PACK], BF16, 25.5))
-        w1_q[1, 1] = quantise(r11, "w1_1_1", place("codes_11", [P, KP], U32, 58))
-        gather_skip(0, 0, place("skip_00", [P, M], F32, 60)[:])
-        w1_q[2, 1] = quantise(r21, "w1_2_1", place("codes_21", [P, KP], U32, 42))
-        for pair in range(2):
-            for a in (1, 2):
-                for t in (2 * pair, 2 * pair + 1):
-                    first_pass(acc, a, 1, t)
-        early = place("early", [P, (PACK - 1) * M], F32, 18.5)
-        for t in range(1, PACK):
-            gather_skip(0, t, early[:, M * (t - 1) : M * t])
+        low_10 = round_half_on_scalar(wb_raw[1, 0], place("low_10", [P, KP * PACK // 2], BF16, 28), 0)
+        w1_q[1, 1] = quantise(r11, "w1_1_1")
+        first_passes(acc, 1, 1)
+        r_b00 = place("r_b00", [P, KP * PACK], BF16, 46)
+        round_part_on_gpsimd(wb_raw[0, 0], r_b00, 0)
+        early = place("early", [P, 2 * M], F32, 16)
+        for t in range(2):
+            gather_skip(0, t, early[:, M * t : M * (t + 1)])
+        w1_q[2, 1] = quantise(r21, "w1_2_1", slot("codes_21", [P, KP], U32))
+        first_passes(acc, 2, 1)
+        late = place("late", [P, 2 * M], F32, 24)
+        for t in range(2, PACK):
+            gather_skip(0, t, late[:, M * (t - 2) : M * (t - 1)])
 
-        x0 = place("x0", [P, KP * PACK], BF16, 44)
+        x0 = place("x0", [P, KP * PACK], BF16, 38)
         piece_width = M * PACK // GAIN_PIECES
         for piece in range(GAIN_PIECES):
             cols = slice(piece_width * piece, piece_width * (piece + 1))
             nc.gpsimd.tensor_tensor(
-                out=x0[:, cols].rearrange("p (m t) -> p m t", t=PACK),
-                in0=silu0[:, cols].rearrange("p (m t) -> p m t", t=PACK),
-                in1=half_gain[:, 0, :].unsqueeze(1).to_broadcast([P, piece_width // PACK, PACK]),
+                out=x0[:, cols].rearrange("p (r c) -> p r c", c=KP),
+                in0=silu0[:, cols].rearrange("p (r c) -> p r c", c=KP),
+                in1=gain_row[:].unsqueeze(1).to_broadcast([P, piece_width // KP, KP]),
                 op=ALU.mult,
             )
-        r_b10 = round_on_gpsimd(wb_raw[1, 0], place("r_b10", [P, KP * PACK], BF16, 29.5))
+        round_part_on_gpsimd(wb_raw[0, 0], r_b00, 1)
 
         for t in range(PACK):
             leave_psum(1, acc, t, place("h_1_%d" % t, [P, S], F32, 4 * t))
         silu1 = slot("v_2", [P, PACK, M], F32)
         for t in range(PACK):
-            deep = slot("deep_%d" % t, [P, M], F32) if t % 3 == 0 else place("deep_%d" % t, [P, M], F32, 37.5 if t == 1 else 53)
+            deep = place("deep_2", [P, M], F32, 53) if t == 2 else slot("deep_%d" % t, [P, M], F32)
             gather_deep(1, t, deep[:])
-            if t == 2:
-                first_wa = slot("deep_0", [P, GROUPS * KP], U16)
-            if t >= 2:
-                reorder_wa_on_scalar(t - 2, 0, first_wa[:, KP * (t - 2) : KP * (t - 1)])
             nc.scalar.activation(out=silu1[:, t, :], in_=deep[:], func=ACT.Silu)
-        r_b01 = round_on_scalar(wb_raw[0, 1], place("r_b01", [P, KP * PACK], BF16, 50))
+        high_10 = round_half_on_scalar(wb_raw[1, 0], place("high_10", [P, KP * PACK // 2], BF16, 52), 1)
+        r_b01 = round_on_scalar(wb_raw[0, 1], rounded_slot("deep_3"))
         r_b11 = round_on_scalar(wb_raw[1, 1], place("r_b11", [P, KP * PACK], BF16, 54))
-        reorder_wa_on_scalar(0, 1, slot("tab_1", [P, KP], U16))
-        codes = place("codes", [P, 3 * KP], U32, 33.5)
+        codes = slot("deep_1", [P, 2 * KP], U32)
         x_q[0] = quantise(x0, "x_0", codes[:, 0:KP])
-        wb_q[1, 0] = quantise(r_b10, "wb_1_0", codes[:, KP : 2 * KP])
-        wb_q[0, 0] = quantise(r_b00, "wb_0_0", codes[:, 2 * KP : 3 * KP])
-        x1 = place("x1", [P, KP * PACK], BF16, 44)
+        wb_q[0, 0] = quantise(r_b00, "wb_0_0", codes[:, KP : 2 * KP])
+        x1 = place("x1", [P, KP * PACK], BF16, 38)
         nc.vector.tensor_tensor(
             out=x1[:].rearrange("p (c i t) -> p c t i", i=2, t=PACK),
             in0=silu1[:].rearrange("p t (c i) -> p c t i", i=2),
             in1=half_gain[:, 1, :].unsqueeze(1).unsqueeze(3).to_broadcast([P, M // 2, PACK, 2]),
             op=ALU.mult,
         )
-        wb_q[0, 1] = quantise(r_b01, "wb_0_1", place("codes_b01", [P, KP], U32, 25.5))
+        wb_q[1, 0] = operand("wb_1_0", place("codes_b10", [P, KP], U32, 46))
+        quantise_half(low_10, wb_q[1, 0], 0)
+        quantise_half(high_10, wb_q[1, 0], 1)
         x_q[1] = quantise(x1, "x_1")
 
         acc = banks()
@@ -386,9 +398,10 @@ def tile_list_reef_mosaic_skip_kernel(
         for t in range(PACK):
             gate_pass(acc, 1, 0, t)
             value_pass(acc, 1, 0, t)
-        reorder_wa(1, 1, place("wa_11", [P, KP], U16, 50))
-        gather_skip(1, 1, place("skip_11", [P, M], F32, 51)[:])
-        wb_q[1, 1] = quantise(r_b11, "wb_1_1", place("codes_b11", [P, KP], U32, 44))
+        wb_q[0, 1] = quantise(r_b01, "wb_0_1", place("codes_b01", [P, KP], U32, 52))
+        reorder_wa(1, 1, place("wa_11", [P, KP], U16, 38))
+        gather_skip(1, 1, place("skip_11", [P, M], F32, 40)[:])
+        wb_q[1, 1] = quantise(r_b11, "wb_1_1")
         first = slot("tab_2", [P, PACK * M], F32)
         for t in range(PACK):
             add_and_store(nc.gpsimd, 0, t, gated_value(0, t, acc, first[:, M * t : M * (t + 1)]), skip[0, t])
@@ -406,6 +419,6 @@ def tile_list_reef_mosaic_skip_kernel(
             gated[t] = gated_value(1, t, acc, slot("gated_%d" % t, [P, M], F32)[:])
             if t < 2:
                 add_and_store(nc.gpsimd, 1, t, gated[t], skip[1, t])
-        last = place("last", [P, 2 * M], F32, 47)
+        last = place("last", [P, 2 * M], F32, 35)
         fused_and_store(1, 2, gated[2], last[:, 0:M])
         fused_and_store(1, 3, gated[3], last[:, M : 2 * M], parts=2)

@@ -84,10 +84,6 @@ def tile_list_reef_mosaic_skip_kernel(
         def rounded_slot(tag):
             return slot(tag, [P, KP * PACK], BF16)
 
-        def load_columns(raw, part):
-            cols = slice(KP // 2 * part, KP // 2 * (part + 1))
-            nc.sync.dma_start(out=raw[:, :, cols], in_=wb[0:KP, cols].rearrange("(p j) c -> p j c", j=PACK))
-
         def pair_views(raw, rounded):
             dst = rounded[:].rearrange("p (u v m j) -> p u m j v", u=2, v=2, j=PACK)
             src = raw[:].rearrange("p j (m u v) -> p u m j v", u=2, v=2)
@@ -126,10 +122,10 @@ def tile_list_reef_mosaic_skip_kernel(
             nc.vector.tensor_copy(out=dst, in_=src)
             return rounded
 
-        def round_part_on_gpsimd(raw, rounded, part):
+        def round_on_gpsimd(raw, rounded):
             dst, src = line_views(raw, rounded)
-            words = slice(P // 2 * part, P // 2 * (part + 1))
-            nc.gpsimd.tensor_copy(out=dst[:, words], in_=src[:, words])
+            nc.gpsimd.tensor_copy(out=dst, in_=src)
+            return rounded
 
         def operand(name, codes=None):
             if codes is None:
@@ -221,6 +217,11 @@ def tile_list_reef_mosaic_skip_kernel(
                 stop=(a == GROUPS - 1),
             )
 
+        def reorder_wa_on_scalar(a, b, words):
+            wa[a, b] = words[:]
+            src = wa_raw[:, a, :].bitcast(U16).rearrange("p (b m u v) -> p b u m v", b=GROUPS, u=2, v=2)
+            nc.scalar.copy(out=words[:].rearrange("p (u v m) -> p u m v", u=2, v=2), in_=src[:, b])
+
         def reorder_wa(a, b, words):
             wa[a, b] = words[:]
             src = wa_raw[:, a, :].bitcast(U8).rearrange("p (b m t e) -> p b t m e", b=GROUPS, t=PACK, e=2)
@@ -291,10 +292,9 @@ def tile_list_reef_mosaic_skip_kernel(
         nc.sync.dma_start(pos2_sb[:], pos2)
         wa_raw = slot("wa_raw", [P, GROUPS, H // 2], I32)
         nc.sync.dma_start(out=wa_raw[:], in_=wa_words.bitcast(I32).rearrange("a p c -> p a c"))
-        w1_raw[1, 1] = load_weight(w1, 1, 1, place("raw_11", [P, PACK, KP], F32, 16))
-        w1_raw[2, 1] = load_weight(w1, 2, 1, place("raw_21", [P, PACK, KP], F32, 24))
-        wb_raw[0, 0] = raw_slot("raw_b00")
-        load_columns(wb_raw[0, 0], 0)
+        w1_raw[1, 1] = load_weight(w1, 1, 1, place("raw_11", [P, PACK + 1, KP], F32, 20)[:, 0:PACK, :])
+        w1_raw[2, 1] = load_weight(w1, 2, 1, place("raw_21", [P, PACK, KP], F32, 31))
+        wb_raw[0, 0] = load_weight(wb, 0, 0, raw_slot("raw_b00"))
 
         acc = banks()
         v[0] = gather_words(tab[0], 0)
@@ -313,18 +313,17 @@ def tile_list_reef_mosaic_skip_kernel(
                 reorder_wa_plane(a, slot(high_tag, [P, H], U8))
             first_passes(acc, a, 0)
         wb_raw[1, 0] = load_weight(wb, 1, 0, raw_slot("tab_0"))
-        load_columns(wb_raw[0, 0], 1)
         wb_raw[0, 1] = load_weight(wb, 0, 1, raw_slot("tab_1"))
         wb_raw[1, 1] = load_weight(wb, 1, 1, raw_slot("tab_2"))
 
-        r01 = round_on_vector(w1_raw[0, 1], place("r01", [P, KP * PACK], BF16, 42))
+        r01 = round_on_vector(w1_raw[0, 1], place("r01", [P, KP * PACK], BF16, 46))
         for t in range(PACK):
             leave_psum(0, acc, t, slot("h_0_%d" % t, [P, S], F32))
         deep0 = place("deep0", [P, 2 * PACK, M], F32, 0)[:, 0:PACK, :]
         gather_deep(0, 0, deep0[:, 0, :])
-        w1_q[0, 1] = quantise(r01, "w1_0_1", None)
+        w1_q[0, 1] = quantise(r01, "w1_0_1", place("codes_01", [P, KP], U32, 43))
         reorder_wa(0, 0, slot("wa_00", [P, KP], U16))
-        rest = place("rest", [P, 2 * KP], U16, 42)
+        rest = place("rest", [P, 2 * KP], U16, 46)
         reorder_wa(1, 0, rest[:, 0:KP])
         reorder_wa(0, 1, rest[:, KP : 2 * KP])
         for t in range(1, PACK):
@@ -332,29 +331,27 @@ def tile_list_reef_mosaic_skip_kernel(
 
         acc = banks()
         first_passes(acc, 0, 1)
-        r11 = round_on_scalar(w1_raw[1, 1], place("r11", [P, KP * PACK], BF16, 46))
-        r21 = round_on_scalar(w1_raw[2, 1], place("r21", [P, KP * PACK], BF16, 38))
-        silu0 = place("silu0", [P, M * PACK], F32, 30)
+        r11 = round_on_scalar(w1_raw[1, 1], rounded_slot("r11"))
+        silu0 = place("silu0", [P, M * PACK], F32, 21)
         nc.scalar.activation(
             out=silu0[:].rearrange("p (c i t) -> p c t i", i=2, t=PACK),
             in_=deep0.rearrange("p t (c i) -> p c t i", i=2),
             func=ACT.Silu,
         )
-        low_10 = round_half_on_scalar(wb_raw[1, 0], place("low_10", [P, KP * PACK // 2], BF16, 28), 0)
-        w1_q[1, 1] = quantise(r11, "w1_1_1")
-        first_passes(acc, 1, 1)
-        r_b00 = place("r_b00", [P, KP * PACK], BF16, 46)
-        round_part_on_gpsimd(wb_raw[0, 0], r_b00, 0)
-        early = place("early", [P, 2 * M], F32, 16)
-        for t in range(2):
+        r21 = round_on_vector(w1_raw[2, 1], place("r21", [P, KP * PACK], BF16, 40))
+        w1_q[1, 1] = quantise(r11, "w1_1_1", place("codes_11", [P, KP], U32, 44))
+        w1_q[2, 1] = quantise(r21, "w1_2_1")
+        r_b00 = round_on_scalar(wb_raw[0, 0], place("r_b00", [P, KP * PACK], BF16, 17))
+        low_10 = round_half_on_scalar(wb_raw[1, 0], place("low_10", [P, KP * PACK // 2], BF16, 29), 0)
+        for pair in range(2):
+            for a in (1, 2):
+                for t in (2 * pair, 2 * pair + 1):
+                    first_pass(acc, a, 1, t)
+        early = place("early", [P, PACK * M], F32, 31)
+        for t in range(PACK):
             gather_skip(0, t, early[:, M * t : M * (t + 1)])
-        w1_q[2, 1] = quantise(r21, "w1_2_1", slot("codes_21", [P, KP], U32))
-        first_passes(acc, 2, 1)
-        late = place("late", [P, 2 * M], F32, 24)
-        for t in range(2, PACK):
-            gather_skip(0, t, late[:, M * (t - 2) : M * (t - 1)])
 
-        x0 = place("x0", [P, KP * PACK], BF16, 38)
+        x0 = place("x0", [P, KP * PACK], BF16, 40)
         piece_width = M * PACK // GAIN_PIECES
         for piece in range(GAIN_PIECES):
             cols = slice(piece_width * piece, piece_width * (piece + 1))
@@ -364,7 +361,7 @@ def tile_list_reef_mosaic_skip_kernel(
                 in1=gain_row[:].unsqueeze(1).to_broadcast([P, piece_width // KP, KP]),
                 op=ALU.mult,
             )
-        round_part_on_gpsimd(wb_raw[0, 0], r_b00, 1)
+        r_b01 = round_on_gpsimd(wb_raw[0, 1], place("r_b01", [P, KP * PACK], BF16, 21))
 
         for t in range(PACK):
             leave_psum(1, acc, t, place("h_1_%d" % t, [P, S], F32, 4 * t))
@@ -374,22 +371,22 @@ def tile_list_reef_mosaic_skip_kernel(
             gather_deep(1, t, deep[:])
             nc.scalar.activation(out=silu1[:, t, :], in_=deep[:], func=ACT.Silu)
         high_10 = round_half_on_scalar(wb_raw[1, 0], place("high_10", [P, KP * PACK // 2], BF16, 52), 1)
-        r_b01 = round_on_scalar(wb_raw[0, 1], rounded_slot("deep_3"))
         r_b11 = round_on_scalar(wb_raw[1, 1], place("r_b11", [P, KP * PACK], BF16, 54))
+        reorder_wa_on_scalar(1, 1, slot("deep_3", [P, KP], U16))
         codes = slot("deep_1", [P, 2 * KP], U32)
         x_q[0] = quantise(x0, "x_0", codes[:, 0:KP])
         wb_q[0, 0] = quantise(r_b00, "wb_0_0", codes[:, KP : 2 * KP])
-        x1 = place("x1", [P, KP * PACK], BF16, 38)
+        x1 = place("x1", [P, KP * PACK], BF16, 40)
         nc.vector.tensor_tensor(
             out=x1[:].rearrange("p (c i t) -> p c t i", i=2, t=PACK),
             in0=silu1[:].rearrange("p t (c i) -> p c t i", i=2),
             in1=half_gain[:, 1, :].unsqueeze(1).unsqueeze(3).to_broadcast([P, M // 2, PACK, 2]),
             op=ALU.mult,
         )
-        wb_q[1, 0] = operand("wb_1_0", place("codes_b10", [P, KP], U32, 46))
+        wb_q[1, 0] = operand("wb_1_0", place("codes_b10", [P, KP], U32, 17))
         quantise_half(low_10, wb_q[1, 0], 0)
-        quantise_half(high_10, wb_q[1, 0], 1)
         x_q[1] = quantise(x1, "x_1")
+        quantise_half(high_10, wb_q[1, 0], 1)
 
         acc = banks()
         for t in range(PACK):
@@ -398,14 +395,12 @@ def tile_list_reef_mosaic_skip_kernel(
         for t in range(PACK):
             gate_pass(acc, 1, 0, t)
             value_pass(acc, 1, 0, t)
-        wb_q[0, 1] = quantise(r_b01, "wb_0_1", place("codes_b01", [P, KP], U32, 52))
-        reorder_wa(1, 1, place("wa_11", [P, KP], U16, 38))
-        gather_skip(1, 1, place("skip_11", [P, M], F32, 40)[:])
-        wb_q[1, 1] = quantise(r_b11, "wb_1_1")
+        wb_q[0, 1] = quantise(r_b01, "wb_0_1", place("codes_b01", [P, KP], U32, 40))
+        wb_q[1, 1] = quantise(r_b11, "wb_1_1", place("codes_b11", [P, KP], U32, 42))
         first = slot("tab_2", [P, PACK * M], F32)
         for t in range(PACK):
             add_and_store(nc.gpsimd, 0, t, gated_value(0, t, acc, first[:, M * t : M * (t + 1)]), skip[0, t])
-        gather_skip(1, 0, slot("tanh_0_2", [P, M], F32)[:])
+        gather_skip(1, 1, slot("tanh_0_2", [P, M], F32)[:])
         acc = banks()
         for t in range(PACK + 1):
             for a in range(GROUPS):
@@ -417,8 +412,9 @@ def tile_list_reef_mosaic_skip_kernel(
         gated = {}
         for t in range(PACK):
             gated[t] = gated_value(1, t, acc, slot("gated_%d" % t, [P, M], F32)[:])
-            if t < 2:
+            if t == 1:
                 add_and_store(nc.gpsimd, 1, t, gated[t], skip[1, t])
-        last = place("last", [P, 2 * M], F32, 35)
+                fused_and_store(1, 0, gated[0], place("res_10", [P, M], F32, 40)[:])
+        last = slot("deep_3", [P, 2 * M], F32)
         fused_and_store(1, 2, gated[2], last[:, 0:M])
         fused_and_store(1, 3, gated[3], last[:, M : 2 * M], parts=2)

from contextlib import ExitStack

import concourse.mybir as mybir

K, T, S, M, H = 1536, 2048, 1024, 512, 1024
FLOPS = 2 * K * H * S + 2 * 2 * H * H * M

F32 = mybir.dt.float32
BF16 = mybir.dt.bfloat16
I32 = mybir.dt.int32
U32 = mybir.dt.uint32
U16 = mybir.dt.uint16
U8 = mybir.dt.uint8
FP8X4 = mybir.dt.float8_e4m3fn_x4
FP4X4 = mybir.dt.float4_e2m1fn_x4
ACT = mybir.ActivationFunctionType
ALU = mybir.AluOpType

P = 128
PACK = 4
KP = P * PACK
BANK = 512
LIST_ROWS = 16
QUADRANT = 32
K_PASSES = K // KP
GROUPS = H // KP
HALVES = S // BANK
KIB = 1024
GAIN_PIECES = 2


def tile_list_reef_mosaic_skip_kernel(
    tc, tab_words, tab_scales, offs, pos1, pos2, w1, gain, wa_words, wa_scales, wb, bg, out
):
    nc = tc.nc
    with ExitStack() as ctx:
        keep = ctx.enter_context(tc.tile_pool(name="keep", bufs=1))
        ring = ctx.enter_context(tc.tile_pool(name="ring", bufs=1))
        placed = ctx.enter_context(tc.tile_pool(name="placed", bufs=1))
        psum = ctx.enter_context(tc.psum_pool(name="psum", bufs=1))

        offs_sb = keep.tile([P, S // LIST_ROWS], U16, name="offs_sb")
        pos1_sb = keep.tile([P, M // LIST_ROWS], U16, name="pos1_sb")
        pos2_sb = keep.tile([P, M // LIST_ROWS], U16, name="pos2_sb")
        tab_planes = keep.tile([P, T], U8, name="tab_planes", align_bytes=64)
        wa_planes_raw = keep.tile([P, GROUPS * H], U8, name="wa_planes_raw", align_bytes=64)
        vec_raw = keep.tile([P, 2, GROUPS, 2 * PACK], F32, name="vec_raw")
        vec_half = keep.tile([P, 2, GROUPS, PACK], F32, name="vec_half")
        warm = keep.tile([P, 1], F32, name="warm")

        def slot(tag, shape, dtype):
            return ring.tile(shape, dtype, name=tag, tag=tag, align_bytes=64)

        def place(name, shape, dtype, kib):
            return placed.tile(shape, dtype, name=name, tag=name, align_bytes=64, offset=int(kib * KIB))

        def bank(t, half):
            return psum.tile([P, BANK], F32, name="bank_%d_%d" % (t, half), tag="bank_%d_%d" % (t, half))

        def banks():
            return {(t, half): bank(t, half) for t in range(PACK) for half in range(HALVES)}

        def load_table_scales(queue, q):
            queue.dma_start(
                out=tab_planes[QUADRANT * q : QUADRANT * q + 4 * K_PASSES, :].bitcast(I32),
                in_=tab_scales[:, 4 * q : 4 * q + 4, :].bitcast(I32),
            )

        def load_table(a):
            words = slot("tab_%d" % a, [P, T], I32)
            nc.sync.dma_start(out=words[:], in_=tab_words[a].rearrange("p t i -> p (t i)").bitcast(I32))
            return words

        def load_weight(w, a, b, raw):
            nc.sync.dma_start(
                out=raw[:],
                in_=w[KP * a : KP * (a + 1), KP * b : KP * (b + 1)].rearrange("(p j) c -> p j c", j=PACK),
            )
            return raw

        def raw_slot(tag):
            return slot(tag, [P, PACK, KP], F32)

        def rounded_slot(tag):
            return slot(tag, [P, KP * PACK], BF16)

        def pair_views(raw, rounded):
            dst = rounded[:].rearrange("p (u v m j) -> p u m j v", u=2, v=2, j=PACK)
            src = raw[:].rearrange("p j (m u v) -> p u m j v", u=2, v=2)
            return dst, src

        def round_on_scalar(raw, rounded):
            dst, src = pair_views(raw, rounded)
            nc.scalar.copy(out=dst, in_=src)
            return rounded

        def half_views(raw, half, u):
            dst = half[:].rearrange("p (v m j) -> p m j v", v=2, j=PACK)
            src = raw[:].rearrange("p j (m u v) -> p u m j v", u=2, v=2)
            return dst, src[:, u]

        def half_slot(tag):
            return slot(tag, [P, KP * PACK // 2], BF16)

        def round_half_on_scalar(raw, half, u):
            dst, src = half_views(raw, half, u)
            nc.scalar.copy(out=dst, in_=src)
            return half

        def round_half_on_vector(raw, half, u):
            dst, src = half_views(raw, half, u)
            nc.vector.tensor_copy(out=dst, in_=src)
            return half

        def line_views(raw, rounded):
            dst = rounded[:].rearrange("p (t m j) -> p m j t", t=PACK, j=PACK)
            src = raw[:].rearrange("p j (m t) -> p m j t", t=PACK)
            return dst, src

        def round_on_vector(raw, rounded):
            dst, src = line_views(raw, rounded)
            nc.vector.tensor_copy(out=dst, in_=src)
            return rounded

        def round_on_gpsimd(raw, rounded):
            dst, src = line_views(raw, rounded)
            nc.gpsimd.tensor_copy(out=dst, in_=src)
            return rounded

        def operand(name, codes=None):
            if codes is None:
                codes = keep.tile([P, KP], U32, name=name + "_codes", align_bytes=64)
            scales = keep.tile([P, KP], U8, name=name + "_scales", align_bytes=64)
            return codes, scales

        def quantise(rounded, name, codes=None):
            codes, scales = operand(name, codes)
            nc.vector.quantize_mx(out=codes[:].bitcast(FP8X4), scales=scales[:], in_=rounded[:])
            return codes, scales

        def quantise_half(half, target, u):
            codes, scales = target
            cols = slice(KP // 2 * u, KP // 2 * (u + 1))
            nc.vector.quantize_mx(out=codes[:, cols].bitcast(FP8X4), scales=scales[:, cols], in_=half[:])

        def gather_words(words, a):
            picked = slot("v_%d" % a, [P, S], U32)
            nc.vector.tensor_copy(out=picked[:], in_=words[:].bitcast(U32).indirect(offs_sb[:]))
            return picked

        h = {}
        skip = {}
        v = {}
        w1_q = {}
        wb_q = {}
        x_q = {}
        wa = {}
        wa_planes = {}
        out_rows = out.rearrange("(b p t) m -> b t p m", b=GROUPS, t=PACK)

        def first_pass(acc, a, b, t):
            codes, scales = w1_q[a, b]
            cols = slice(P * t, P * (t + 1))
            for half in range(HALVES):
                entries = slice(BANK * half, BANK * (half + 1))
                nc.tensor.matmul_mx(
                    out=acc[t, half][:],
                    lhsT=codes[:, cols].bitcast(FP8X4),
                    lhsT_scale=scales[:, cols],
                    rhs=v[a][:, entries].bitcast(FP8X4),
                    rhs_scale=v_planes[4 * a : P, entries],
                    start=(a == 0),
                    stop=(a == K_PASSES - 1),
                )

        def first_passes(acc, a, b):
            for t in range(PACK):
                first_pass(acc, a, b, t)

        def leave_psum(b, acc, t, tile):
            h[b, t] = tile
            for half in range(HALVES):
                nc.scalar.copy(out=h[b, t][:, BANK * half : BANK * (half + 1)], in_=acc[t, half][:])

        def gather_deep(b, t, deep):
            nc.vector.tensor_copy(out=deep, in_=h[b, t][:].indirect(pos1_sb[:]))

        def gather_skip(b, t, picked):
            skip[b, t] = picked
            nc.vector.tensor_copy(out=picked, in_=h[b, t][:].indirect(pos2_sb[:]))

        def gate_pass(acc, a, b, t):
            x_codes, x_scales = x_q[a]
            wb_codes, wb_scales = wb_q[a, b]
            cols = slice(P * t, P * (t + 1))
            nc.tensor.matmul_mx(
                out=acc[t, 0][:],
                lhsT=wb_codes[:, cols].bitcast(FP8X4),
                lhsT_scale=wb_scales[:, cols],
                rhs=x_codes[:].bitcast(FP8X4),
                rhs_scale=x_scales[:],
                start=(a == 0),
                stop=(a == GROUPS - 1),
            )

        def value_pass(acc, a, b, t):
            x_codes, x_scales = x_q[a]
            cols = slice(P * t, P * (t + 1))
            plane_cols = slice(KP * b + P * t, KP * b + P * (t + 1))
            nc.tensor.matmul_mx(
                out=acc[t, 1][:],
                lhsT=wa[a, b][:, cols].bitcast(FP4X4),
                lhsT_scale=wa_planes[a][:, plane_cols],
                rhs=x_codes[:].bitcast(FP8X4),
                rhs_scale=x_scales[:],
                start=(a == 0),
                stop=(a == GROUPS - 1),
            )

        def reorder_wa_on_scalar(a, b, words):
            wa[a, b] = words[:]
            src = wa_raw[:, a, :].bitcast(U16).rearrange("p (b m u v) -> p b u m v", b=GROUPS, u=2, v=2)
            nc.scalar.copy(out=words[:].rearrange("p (u v m) -> p u m v", u=2, v=2), in_=src[:, b])

        def reorder_wa(a, b, words):
            wa[a, b] = words[:]
            src = wa_raw[:, a, :].bitcast(U8).rearrange("p (b m t e) -> p b t m e", b=GROUPS, t=PACK, e=2)
            nc.gpsimd.tensor_copy(out=words[:].bitcast(U8).rearrange("p (t m e) -> p t m e", t=PACK, e=2), in_=src[:, b])

        def reorder_wa_plane(a, plane):
            wa_planes[a] = plane
            nc.gpsimd.tensor_copy(
                out=plane[:].rearrange("p (b t m) -> p b t m", t=PACK, m=P),
                in_=wa_planes_raw[:, H * a : H * (a + 1)].rearrange("p (b m t) -> p b t m", t=PACK, m=P),
            )

        def gated_value(b, t, acc, gated):
            tanh = slot("tanh_%d_%d" % (b, t), [P, M], F32)
            nc.scalar.activation(out=tanh[:], in_=acc[t, 0][:], func=ACT.Tanh, bias=half_bg[:, b, t : t + 1])
            nc.vector.scalar_tensor_tensor(out=gated, in0=tanh[:], scalar=1.0, in1=acc[t, 1][:], op0=ALU.add, op1=ALU.mult)
            return gated

        def add_and_store(engine, b, t, gated, res, parts=1):
            width = M // parts
            for part in range(parts):
                cols = slice(width * part, width * (part + 1))
                engine.tensor_tensor(out=res[:, cols], in0=skip[b, t][:, cols], in1=gated[:, cols], op=ALU.add)
                nc.sync.dma_start(out=out_rows[b, t][:, cols], in_=res[:, cols])

        def fused_and_store(b, t, gated, res, parts=1):
            width = M // parts
            for part in range(parts):
                cols = slice(width * part, width * (part + 1))
                entries = pos2_sb[:, width // LIST_ROWS * part : width // LIST_ROWS * (part + 1)]
                nc.vector.tensor_tensor(out=res[:, cols], in0=h[b, t][:].indirect(entries), in1=gated[:, cols], op=ALU.add)
                nc.scalar.dma_start(out=out_rows[b, t][:, cols], in_=res[:, cols])

        nc.vector.memset(tab_planes[:].bitcast(I32), 0)
        nc.gpsimd.memset(wa_planes_raw[:].bitcast(I32), 0)
        for q in range(2):
            load_table_scales(nc.scalar, q)
        for i, vec in enumerate((gain, bg)):
            nc.scalar.dma_start(out=vec_raw[:, i, :, 0:PACK], in_=vec.rearrange("(b p t) -> p b t", b=GROUPS, t=PACK))
        for q in range(P // QUADRANT):
            nc.gpsimd.dma_start(
                out=wa_planes_raw[QUADRANT * q : QUADRANT * q + 4, :].bitcast(I32).rearrange("r (a c) -> r a c", a=GROUPS),
                in_=wa_scales[:, 4 * q : 4 * q + 4, :].bitcast(I32).rearrange("a r c -> r a c"),
            )
        nc.gpsimd.tensor_scalar(
            out=vec_half[:], in0=vec_raw[:, :, :, 0:PACK], scalar1=0.5, scalar2=0.0, op0=ALU.mult, op1=ALU.add
        )
        nc.scalar.activation(out=warm[:], in_=vec_raw[:, 0, 0, 0:1], func=ACT.Silu)
        half_gain = vec_half[:, 0]
        half_bg = vec_half[:, 1]
        gain_row = keep.tile([P, KP], F32, name="gain_row")
        nc.gpsimd.tensor_copy(
            out=gain_row[:].rearrange("p (m t) -> p m t", t=PACK), in_=half_gain[:, 0, :].unsqueeze(1).to_broadcast([P, P, PACK])
        )

        nc.sync.dma_start(offs_sb[:], offs)
        tab = {}
        w1_raw = {}
        wb_raw = {}
        for a in range(K_PASSES):
            tab[a] = load_table(a)
            if a == 0:
                for q in range(2, 4):
                    load_table_scales(nc.sync, q)
            w1_raw[a, 0] = load_weight(w1, a, 0, raw_slot("raw_%d0" % a))
        w1_raw[0, 1] = load_weight(w1, 0, 1, raw_slot("raw_01"))
        nc.sync.dma_start(pos1_sb[:], pos1)
        nc.sync.dma_start(pos2_sb[:], pos2)
        wa_raw = slot("wa_raw", [P, GROUPS, H // 2], I32)
        nc.sync.dma_start(out=wa_raw[:], in_=wa_words.bitcast(I32).rearrange("a p c -> p a c"))
        w1_raw[1, 1] = load_weight(w1, 1, 1, place("raw_11", [P, PACK + 1, KP], F32, 20)[:, 0:PACK, :])
        w1_raw[2, 1] = load_weight(w1, 2, 1, place("raw_21", [P, PACK, KP], F32, 31))
        wb_raw[0, 0] = load_weight(wb, 0, 0, raw_slot("raw_b00"))

        acc = banks()
        v[0] = gather_words(tab[0], 0)
        v_planes = keep.tile([P, S], U8, name="v_planes", align_bytes=64)
        nc.vector.tensor_copy(out=v_planes[:], in_=tab_planes[:].indirect(offs_sb[:]))
        for a in range(K_PASSES):
            if a > 0:
                v[a] = gather_words(tab[a], a)
            low = round_half_on_vector(w1_raw[a, 0], half_slot("half_a"), 0)
            high_tag = "half_b" if a == K_PASSES - 1 else "high_%d" % a
            high = round_half_on_scalar(w1_raw[a, 0], half_slot(high_tag), 1)
            w1_q[a, 0] = operand("w1_%d_0" % a, slot("codes_%d0" % a, [P, KP], U32))
            quantise_half(high, w1_q[a, 0], 1) if a < K_PASSES - 1 else quantise_half(low, w1_q[a, 0], 0)
            quantise_half(low, w1_q[a, 0], 0) if a < K_PASSES - 1 else quantise_half(high, w1_q[a, 0], 1)
            if a < GROUPS:
                reorder_wa_plane(a, slot(high_tag, [P, H], U8))
            first_passes(acc, a, 0)
        wb_raw[1, 0] = load_weight(wb, 1, 0, raw_slot("tab_0"))
        wb_raw[0, 1] = load_weight(wb, 0, 1, raw_slot("tab_1"))
        wb_raw[1, 1] = load_weight(wb, 1, 1, raw_slot("tab_2"))

        r01 = round_on_vector(w1_raw[0, 1], place("r01", [P, KP * PACK], BF16, 46))
        for t in range(PACK):
            leave_psum(0, acc, t, slot("h_0_%d" % t, [P, S], F32))
        deep0 = place("deep0", [P, 2 * PACK, M], F32, 0)[:, 0:PACK, :]
        gather_deep(0, 0, deep0[:, 0, :])
        w1_q[0, 1] = quantise(r01, "w1_0_1", place("codes_01", [P, KP], U32, 43))
        reorder_wa(0, 0, slot("wa_00", [P, KP], U16))
        rest = place("rest", [P, 2 * KP], U16, 46)
        reorder_wa(1, 0, rest[:, 0:KP])
        reorder_wa(0, 1, rest[:, KP : 2 * KP])
        for t in range(1, PACK):
            gather_deep(0, t, deep0[:, t, :])

        acc = banks()
        first_passes(acc, 0, 1)
        r11 = round_on_scalar(w1_raw[1, 1], rounded_slot("r11"))
        silu0 = place("silu0", [P, M * PACK], F32, 21)
        nc.scalar.activation(
            out=silu0[:].rearrange("p (c i t) -> p c t i", i=2, t=PACK),
            in_=deep0.rearrange("p t (c i) -> p c t i", i=2),
            func=ACT.Silu,
        )
        r21 = round_on_vector(w1_raw[2, 1], place("r21", [P, KP * PACK], BF16, 40))
        w1_q[1, 1] = quantise(r11, "w1_1_1", place("codes_11", [P, KP], U32, 44))
        w1_q[2, 1] = quantise(r21, "w1_2_1")
        r_b00 = round_on_scalar(wb_raw[0, 0], place("r_b00", [P, KP * PACK], BF16, 17))
        low_10 = round_half_on_scalar(wb_raw[1, 0], place("low_10", [P, KP * PACK // 2], BF16, 29), 0)
        for pair in range(2):
            for a in (1, 2):
                for t in (2 * pair, 2 * pair + 1):
                    first_pass(acc, a, 1, t)
        early = place("early", [P, PACK * M], F32, 31)
        for t in range(PACK):
            gather_skip(0, t, early[:, M * t : M * (t + 1)])

        x0 = place("x0", [P, KP * PACK], BF16, 40)
        piece_width = M * PACK // GAIN_PIECES
        for piece in range(GAIN_PIECES):
            cols = slice(piece_width * piece, piece_width * (piece + 1))
            nc.gpsimd.tensor_tensor(
                out=x0[:, cols].rearrange("p (r c) -> p r c", c=KP),
                in0=silu0[:, cols].rearrange("p (r c) -> p r c", c=KP),
                in1=gain_row[:].unsqueeze(1).to_broadcast([P, piece_width // KP, KP]),
                op=ALU.mult,
            )
        r_b01 = round_on_gpsimd(wb_raw[0, 1], place("r_b01", [P, KP * PACK], BF16, 21))

        for t in range(PACK):
            leave_psum(1, acc, t, place("h_1_%d" % t, [P, S], F32, 4 * t))
        silu1 = slot("v_2", [P, PACK, M], F32)
        for t in range(PACK):
            deep = place("deep_2", [P, M], F32, 53) if t == 2 else slot("deep_%d" % t, [P, M], F32)
            gather_deep(1, t, deep[:])
            nc.scalar.activation(out=silu1[:, t, :], in_=deep[:], func=ACT.Silu)
        high_10 = round_half_on_scalar(wb_raw[1, 0], place("high_10", [P, KP * PACK // 2], BF16, 52), 1)
        r_b11 = round_on_scalar(wb_raw[1, 1], place("r_b11", [P, KP * PACK], BF16, 54))
        reorder_wa_on_scalar(1, 1, slot("deep_3", [P, KP], U16))
        codes = slot("deep_1", [P, 2 * KP], U32)
        x_q[0] = quantise(x0, "x_0", codes[:, 0:KP])
        wb_q[0, 0] = quantise(r_b00, "wb_0_0", codes[:, KP : 2 * KP])
        x1 = place("x1", [P, KP * PACK], BF16, 40)
        nc.vector.tensor_tensor(
            out=x1[:].rearrange("p (c i t) -> p c t i", i=2, t=PACK),
            in0=silu1[:].rearrange("p t (c i) -> p c t i", i=2),
            in1=half_gain[:, 1, :].unsqueeze(1).unsqueeze(3).to_broadcast([P, M // 2, PACK, 2]),
            op=ALU.mult,
        )
        wb_q[1, 0] = operand("wb_1_0", place("codes_b10", [P, KP], U32, 17))
        quantise_half(low_10, wb_q[1, 0], 0)
        x_q[1] = quantise(x1, "x_1")
        quantise_half(high_10, wb_q[1, 0], 1)

        acc = banks()
        for t in range(PACK):
            value_pass(acc, 0, 0, t)
            gate_pass(acc, 0, 0, t)
        for t in range(PACK):
            gate_pass(acc, 1, 0, t)
            value_pass(acc, 1, 0, t)
        wb_q[0, 1] = quantise(r_b01, "wb_0_1", place("codes_b01", [P, KP], U32, 40))
        wb_q[1, 1] = quantise(r_b11, "wb_1_1", place("codes_b11", [P, KP], U32, 42))
        first = slot("tab_2", [P, PACK * M], F32)
        for t in range(PACK):
            add_and_store(nc.gpsimd, 0, t, gated_value(0, t, acc, first[:, M * t : M * (t + 1)]), skip[0, t])
        gather_skip(1, 1, slot("tanh_0_2", [P, M], F32)[:])
        acc = banks()
        for t in range(PACK + 1):
            for a in range(GROUPS):
                if t < PACK:
                    gate_pass(acc, a, 1, t)
            for a in range(GROUPS):
                if t > 0:
                    value_pass(acc, a, 1, t - 1)
        gated = {}
        for t in range(PACK):
            gated[t] = gated_value(1, t, acc, slot("gated_%d" % t, [P, M], F32)[:])
            if t == 1:
                add_and_store(nc.gpsimd, 1, t, gated[t], skip[1, t])
                fused_and_store(1, 0, gated[0], place("res_10", [P, M], F32, 40)[:])
        last = slot("deep_3", [P, 2 * M], F32)
        fused_and_store(1, 2, gated[2], last[:, 0:M])
        fused_and_store(1, 3, gated[3], last[:, M : 2 * M], parts=2)
